import numpy as np, ml_dtypes
CORES = [16,18,20,22]
N = 4
BF = ml_dtypes.bfloat16
def gentries(a):
    return np.ascontiguousarray(a.reshape(8, 16, -1).transpose(0, 2, 1)).reshape(8, -1)
def gtable(e):
    e = np.asarray(e); return np.ascontiguousarray(e.reshape(8, -1, 16).transpose(0, 2, 1)).reshape(128, -1).astype(np.int32)
C, I, P, R, S, VM, DM = 2048, 256, 16, 4, 1, 64, 15667200
V, W, B = 2 * C, 2 * C + I, I // S
def walk(nx):
    lead = nx.shape[:-1]; full = np.concatenate([nx, np.broadcast_to(V + np.arange(I), lead + (I,))], axis=-1)
    q = [np.broadcast_to(np.arange(I), lead + (I,))]
    for k in range(1, P): q.append(np.take_along_axis(full, q[-1], -1))
    return np.stack(q, axis=-2)
def parts(rng):
    x = np.minimum((256 * rng.random((N, 8, 1, W)) * rng.random((N, 8, 16, W))).astype(np.int64), 255)
    nu = rng.integers(0, 5, (N, 8, 16)); nu[:, :, 5] = np.maximum(nu[:, :, 5], 1)
    nx = I + np.argsort(rng.random((N, 8, V)), axis=-1)
    le = rng.integers(0, 512, (N, 8, 4, C)); vol = rng.integers(1, VM + 1, (N, 8, V))
    lag = np.minimum(np.exp2(13 + 7 * rng.random((N, 8, I))).astype(np.int64), DM)
    return x, nu, nx, le, vol, lag
def pack(x, nu, nx, le, vol, lag):
    return {"x": np.ascontiguousarray(x.reshape(N, 128, W)).astype(np.float32).astype(BF), "nu": np.ascontiguousarray(nu.reshape(N, 128, 1)).astype(np.int32),
            "nx": np.stack([gtable(a) for a in nx]), "le": np.stack([gtable(a.reshape(8, -1)) for a in le]),
            "vol": np.stack([gtable(a) for a in vol]), "lag": np.stack([gtable(a) for a in lag])}
def chains(rng, lens, out, fix, own=()):
    own = np.array(own, np.int64); pool = I + rng.permutation(V - I); pool = pool[~np.isin(pool, own)]; end = np.add.accumulate(lens - 1)
    for i, p in fix:
        e = int(end[i]) - 1; j = int(np.nonzero(pool == p)[0][0]); pool[j] = pool[e]; pool[e] = p
    nx = np.zeros(V, np.int64); nx[own] = own
    for i in range(I):
        s = np.concatenate([[i], pool[end[i] - lens[i] + 1:end[i]], [V + out[i]]]).astype(np.int64); nx[s[:-1]] = s[1:]
    rest = pool[end[-1]:]; nx[rest] = rest[rng.permutation(len(rest))]
    return nx
def setup_inputs(rng):
    return pack(*parts(rng))
def setup_inputs_spread(rng):
    x, nu, nx, le, vol, lag = parts(rng)
    x = np.minimum((np.exp2(8 * rng.random((N, 8, 1, W))) * rng.random((N, 8, 16, W))).astype(np.int64), 255)
    nu = rng.choice(np.array([0, 0, 1, 4]), (N, 8, 16)); nu[:, :, 3] = 4
    le = np.minimum(np.exp2(9 * rng.random((N, 8, 4, C))).astype(np.int64) - 1, 511)
    vol = np.maximum(np.minimum(np.power(float(VM), rng.random((N, 8, V))).astype(np.int64), VM), 1)
    lag = np.maximum(np.minimum(np.power(float(DM), rng.random((N, 8, I))).astype(np.int64), DM), 1)
    return pack(x, nu, nx, le, vol, lag)
def setup_inputs_ends(rng):
    A = np.array([0, 1, I // 2, I - 2, I - 1]); D = np.array([2, 3, I // 2 + 1, I - 4, I - 3])
    o = np.setdiff1d(np.arange(I), np.concatenate([A, D])); row = np.arange(16)[:, None]
    kind = rng.choice(4, (N, 8, 1, W), p=[0.35, 0.15, 0.25, 0.25]); lane = rng.integers(0, 16, (N, 8, 1, W))
    x = np.where(kind == 0, 255, np.where(kind == 1, np.where(row == lane, 254, 255), np.where(kind == 2, 0, 255 * rng.integers(0, 2, (N, 8, 16, W)))))
    nu = 4 * rng.integers(0, 2, (N, 8, 16)); nu[:, :, 0] = 4; nu[:, 0] = 4; nu[:, 7] = 4; nu[:, 1] = 0; nu[:, 2] = 4; nu[:, 2, 15] = 0
    hi = np.array([511, 511, 510, 510])[:, None]; u = rng.random((N, 8, 1, C))
    le = np.where(u < 0.1, hi, np.where(u < 0.2, hi[::-1], np.where(u < 0.3, 511, 511 * rng.integers(0, 2, (N, 8, 4, C)))))
    vol = np.where(rng.random((N, 8, V)) < 0.5, 1, VM); lag = np.where(rng.random((N, 8, I)) < 0.5, 1, DM); nx = np.zeros((N, 8, V), np.int64)
    for r in range(N):
        for g in range(8):
            lens = np.zeros(I, np.int64); lens[A] = P; lens[D] = R + 1; lens[o] = rng.permutation(np.resize(np.array([1, P // 2, P - 1, P, P + 1]), len(o)))
            out = np.zeros(I, np.int64); out[A] = D; out[D] = A; out[o] = rng.permutation(o)
            nx[r, g] = chains(rng, lens, out, [(0, I), (1, I + 1), (I - 2, V - 2), (I - 1, V - 1)])
            q = walk(nx[r, g]); a = q[:, A]; d = q[:R + 1, D]; both = np.concatenate([a.reshape(-1), d.reshape(-1)])
            le[r, g][:, both % C] = 511
            x[r, g][:, both] = 255; x[r, g][:, V + A] = 255; x[r, g][:, V + D] = 255
            mix = 255 * rng.integers(0, 2, (16, 5)); mix[0] = 255; mix[15] = 0; x[r, g][:, d[1]] = mix
            vol[r, g, a] = VM; vol[r, g, a[1, 1]] = VM - 1
            vol[r, g, a[1:, 2:4]] = np.where(rng.random((P - 1, 2)) < 0.5, 1, VM); vol[r, g, a[1, 2:4]] = 1
            tot = 255 * int(np.sum(nu[r, g])) * np.sum(vol[r, g, a[1:]], axis=0)
            lag[r, g, D] = 1; lag[r, g, A] = DM; lag[r, g, A[2]] = max(int(tot[2]), 1); lag[r, g, A[3]] = min(max(int(tot[3]) + 1, 1), DM)
    return pack(x, nu, nx, le, vol, lag)
def setup_inputs_corners(rng):
    x, nu, nx, le, vol, lag = parts(rng); ar = np.arange(I); m = V // I
    vol = rng.choice(np.array([1, 2, VM - 1, VM]), (N, 8, V)); stay = np.array([0, 511, 511, 0])[:, None]
    for r in range(N):
        for g in range(8):
            t = (g + r) % 8; lens = None
            if t == 0: le[r, g] = stay; lens = rng.permutation(np.resize(np.array([1, 2, P - 1, P, P + 1]), I))
            if t == 1: le[r, g] = 511 - stay
            if t == 2: le[r, g] = 0; lens = np.ones(I, np.int64); lens[rng.integers(0, I)] = V - I + 1
            if t == 3: le[r, g] = stay; lens = rng.permutation(np.resize(np.array([1, P - 1]), I))
            if t == 4: le[r, g] = 511; lens = rng.permutation(np.resize(np.array([m - 1, m + 1]), I))
            if t == 5: lag[r, g] = DM; vol[r, g] = 1
            if t == 6: lag[r, g] = 1; vol[r, g] = VM; nu[r, g] = 0; nu[r, g, rng.integers(0, 16)] = 4
            if t == 7:
                e = rng.integers(-100, 101, (7, W)); nu[r, g] = 4; nu[r, g, 0] = 1
                x[r, g, 0] = 128 + rng.integers(0, 2, W); x[r, g, 1:15:2] = 100 + e; x[r, g, 2:15:2] = 100 - e; x[r, g, 15] = 100
                le[r, g] = np.array([511, 511, 510, 510])[:, None]
            if lens is not None:
                nx[r, g] = chains(rng, lens, rng.permutation(I), []); q = walk(nx[r, g])
                if t == 3:
                    off = np.ones(W, bool); off[q.reshape(-1)] = False; p = np.nonzero(off[:V])[0]; nx[r, g, p] = p
                c = np.sum(nu[r, g][:, None] * x[r, g], axis=0); c[:V] = c[:V] * vol[r, g]; c[V:] = 0
                T = np.add.accumulate(c[q], axis=0); k = rng.integers(1, P, I); j = (rng.random(I) * k).astype(np.int64)
                lag[r, g] = np.maximum(np.minimum(T[k, ar] - T[j, ar] + rng.choice(np.array([0, 0, 0, 1]), I), DM), 1)
    return pack(x, nu, nx, le, vol, lag)
def setup_inputs_calm(rng):
    x, nu, nx, le, vol, lag = parts(rng)
    x = (np.argsort(rng.random((N, 8, 16, W)), axis=2) < rng.integers(0, 4, (N, 8, 1, W))).astype(np.int64)
    nu = rng.integers(0, 3, (N, 8, 16)); nu[:, ::2] = 1; nu[:, :, 7] = 1
    le = rng.integers(0, 4, (N, 8, 4, C)); vol = rng.integers(1, 3, (N, 8, V)); vol[:, 0] = 1; vol[:, 5] = 1
    lag = rng.integers(1, 7, (N, 8, I)); t = (np.arange(N)[:, None] + np.arange(8)[None, :]) % 4
    lag = np.where(t[:, :, None] < 3, t[:, :, None] + 1, lag)
    return pack(x, nu, nx, le, vol, lag)
def setup_inputs_fine(rng):
    x, nu, nx, le, vol, lag = parts(rng); ar = np.arange(I); stay = np.array([0, 511, 511, 0])[:, None]; turn = int(rng.integers(0, 4))
    forms = np.array([[255] * 16, [255] * 13 + [182, 0, 0], [255] * 8 + [0] * 8])
    pats = np.array([[511, 511, 510, 511], [511, 510, 511, 511], [511, 511, 505, 504], [504, 505, 511, 511], [510, 509, 511, 511], [511, 511, 509, 510]]).T
    for g in range(8):
        t = (g + turn) % 4; lane = int(rng.integers(0, 16)); others = np.delete(np.arange(16), lane); nu[:, g] = 4
        if t == 0 or t == 2: nu[:, g, lane] = 1
        far = np.append(rng.permutation(I - 1)[:I // 2 - 1], I - 1); near = np.setdiff1d(ar, far); n = len(far)
        for r in range(N):
            if t == 0 or t == 2: x[r, g][others] = 255 - np.argsort(rng.random((15, W)), axis=0)
            if t == 0:
                x[r, g, lane] = 255; le[r, g] = stay; vol[r, g] = rng.integers(VM - 3, VM + 1, V)
                c = np.zeros(W, np.int64); c[:V] = 15135 * vol[r, g]; q = walk(nx[r, g]); T = np.add.accumulate(c[q], axis=0)
                k = np.maximum(np.argmax(rng.random((P, I)) * ((T >= 2 ** 23) & (q < V)), axis=0), 1); j = np.maximum(k - 1 - rng.integers(0, 3, I), 0)
                lag[r, g] = np.maximum(np.minimum(T[k, ar] - T[j, ar] + rng.integers(0, 2, I), DM), 1)
            if t == 1:
                lens = rng.integers(1, 4, I); lens[far] = P; out = np.zeros(I, np.int64); out[far] = rng.permutation(far); out[near] = rng.permutation(near)
                nx[r, g] = chains(rng, lens, out, [], C + far); a = walk(nx[r, g])[:, far]
                le[r, g] = stay; le[r, g][:, far] = np.array([0, 0, 511, 511])[:, None]
                x[r, g][:, a[1:].reshape(-1)] = 255; x[r, g][:, far] = rng.integers(100, 255, (16, n)); x[r, g][:, C + far] = rng.integers(100, 255, (16, n))
                x[r, g][:, V + far] = rng.integers(0, 61, (16, n)); vol[r, g, a[1:]] = VM
                less = rng.random(n) < 0.5; less[0] = True; e = a[rng.integers(1, P, n), np.arange(n)]; x[r, g][rng.integers(0, 16, n)[less], e[less]] = 254
                c = 4 * np.sum(x[r, g], axis=0); tot = VM * np.sum(c[a[1:]], axis=0); u = rng.random(n); u[0] = 0
                lag[r, g, far] = np.where(u < 0.5, DM, np.minimum(tot + (u < 0.75), DM))
            if t == 2:
                x[r, g, lane] = 254 + rng.integers(0, 2, W); a = rng.integers(501, 512, C); b = rng.integers(501, 512, C)
                le[r, g] = np.where(rng.random(C) < 0.5, np.stack([a, b, a - 1, b - 1]), np.stack([a - 1, b - 1, a, b]))
            if t == 3:
                z = rng.choice(3, W, p=[0.45, 0.3, 0.25]); x[r, g] = np.take_along_axis(forms[z].T, np.argsort(rng.random((16, W)), axis=0), 0)
                le[r, g] = pats[:, rng.integers(0, 6, C)]; shut = I + rng.permutation(C - I)[:(C - I) // 4]; le[r, g][:, shut] = np.array([511, 511, 0, 0])[:, None]
                both = np.concatenate([shut, C + shut]); nx[r, g, np.setdiff1d(np.arange(V), both)] = rng.permutation(np.setdiff1d(I + np.arange(V), both))
                sw = rng.random(len(shut)) < 0.5; nx[r, g, shut] = np.where(sw, C + shut, shut); nx[r, g, C + shut] = np.where(sw, shut, C + shut)
    return pack(x, nu, nx, le, vol, lag)
def check_inputs(d):
    bad = []
    for k, lo, hi in (("x", 0, 255), ("nu", 0, 4), ("nx", I, W - 1), ("le", 0, 511), ("vol", 1, VM), ("lag", 1, DM)):
        v = np.asarray(d[k]).astype(np.float64)
        if not bool(np.all((v >= lo) & (v <= hi))): bad.append("range of " + k)
    v = np.asarray(d["x"]).astype(np.float64)
    if not bool(np.all(v == np.floor(v))): bad.append("whole numbers of x")
    if not all(bool(np.all(np.sort(gentries(a), axis=1) == np.arange(I, W))) for a in d["nx"]): bad.append("nx: each number once in each group")
    return bad
def reference(x, nu, nx, le, vol, lag):
    X = x.astype(np.float32).astype(np.int64).reshape(N, 8, 16, W); w = nu.astype(np.int64).reshape(N, 8, 16, 1)
    nxt = np.stack([gentries(a) for a in nx]).astype(np.int64); ln = np.stack([gentries(a) for a in le]).astype(np.int64).reshape(N, 8, 4, C)
    vo = np.stack([gentries(a) for a in vol]).astype(np.int64); vo = np.concatenate([vo, np.zeros((N, 8, I), np.int64)], axis=2)
    de = np.stack([gentries(a) for a in lag]).astype(np.int64)
    for rnd in range(R):
        mu = np.add.reduce(w * X, axis=2)
        ex = mu.copy(); come = np.zeros((N, 8, 16, I), np.int64)
        for r in range(N):
            for s in range(S):
                ex[r, :, V + s * B:V + (s + 1) * B] = mu[(r + 1 + s) % N, :, s * B:(s + 1) * B]
                come[r, :, :, s * B:(s + 1) * B] = X[(r - 1 - s) % N, :, :, V + s * B:V + (s + 1) * B]
        m = np.take_along_axis(ex, nxt, 2); m0, m1 = m[:, :, :C], m[:, :, C:]
        cross = ln[:, :, 1] * m1 + ln[:, :, 2] * m0 < ln[:, :, 0] * m0 + ln[:, :, 3] * m1
        a, b = nxt[:, :, :C], nxt[:, :, C:]
        nxt = np.concatenate([np.where(cross, b, a), np.where(cross, a, b)], axis=2)
        q = walk(nxt)
        T = np.add.accumulate(np.take_along_axis(vo * mu, q.reshape(N, 8, P * I), 2).reshape(N, 8, P, I), axis=2)
        src = np.zeros((N, 8, P, I), np.int64) + (W + np.arange(I))
        for k in range(1, P):
            for j in range(k):
                src[:, :, k] = np.where(T[:, :, k] - T[:, :, j] >= de, q[:, :, j], src[:, :, k])
            src[:, :, k] = np.where(q[:, :, k] >= V, src[:, :, k - 1], src[:, :, k])
        new = np.take_along_axis(np.concatenate([X, come], axis=3), src.reshape(N, 8, 1, P * I), 3)
        np.put_along_axis(X, q.reshape(N, 8, 1, P * I), new, 3)
    return {"y": X.reshape(N, 128, W).astype(np.float32).astype(BF), "yn": np.stack([gtable(a) for a in nxt]).astype(np.float32)}

@@ -1,0 +1,538 @@
+from concourse.mybir import AluOpType as A, ActivationFunctionType as F
+
+R = 4
+V = 4096
+W = 4352
+ST = 272
+TB = 8464
+XW = 12256
+PARTS = [(1, 3), (4, 7), (8, 11), (12, 15)]
+FLAG = [2, 3, 4, 1]
+BUDGET = 500
+SILU = [0, 48, 256]
+FINV = [0, 56, 96, 120]
+MOVES = [(0, 16, 0), (16, 48, 0), (48, 112, 1), (112, 176, 2), (176, 240, 3)]
+NV = 1
+FETCH = [(0, 7)]
+OPT = ("CO0", "CO1", "ZG0v")
+
+SCRATCH = {
+    "X": ("sbuf", [128, XW], "bfloat16"), "XR": ("sbuf", [128, 4368], "bfloat16"),
+    "NL": ("sbuf", [128, 12288], "float32"), "ZG0": ("sbuf", [128, V], "bfloat16"), "ZG1": ("sbuf", [128, V], "bfloat16"),
+    "SC": ("sbuf", [128, 4096], "float32"), "GW": ("sbuf", [128, 256], "float32"),
+    "NEW": ("sbuf", [128, 3840], "bfloat16"), "SUM": ("sbuf", [128, 2048], "float32"),
+    "FM": ("sbuf", [128, 2048], "bfloat16"), "PV": ("sbuf", [128, W], "float32"),
+    "SB": ("sbuf", [128, ST], "bfloat16"), "ZB": ("sbuf", [128, ST], "bfloat16"),
+    "nxi": ("sbuf", [128, 256], "int32"), "lei": ("sbuf", [128, 512], "int32"), "voi": ("sbuf", [128, 256], "int32"),
+    "lai": ("sbuf", [128, 16], "int32"), "nui": ("sbuf", [128, 4], "int32"),
+    "IP": ("sbuf", [128, 4], "int32"), "IQ": ("sbuf", [128, 4], "int32"), "col": ("sbuf", [128, 16], "float32"),
+    "IX": ("sbuf", [128, 144], "float32"), "J": ("sbuf", [128, 256], "float32"), "OKi": ("sbuf", [128, 64], "float32"),
+    "R1": ("sbuf", [128, 512], "bfloat16"), "LB": ("sbuf", [128, 256], "bfloat16"), "ZR": ("sbuf", [128, 128], "bfloat16"),
+    "BO": ("sbuf", [128, 128], "bfloat16"), "RM": ("sbuf", [128, 16], "float32"), "ID": ("sbuf", [128, 128], "bfloat16"),
+    "Bf": ("sbuf", [128, 144], "float32"), "Bw": ("sbuf", [128, 144], "bfloat16"), "Bp": ("sbuf", [128, 144], "bfloat16"),
+    "Bz": ("sbuf", [128, 144], "bfloat16"), "M": ("sbuf", [128, 256], "float32"), "OKK": ("sbuf", [128, 64], "bfloat16"),
+    "OL": ("sbuf", [128, 16], "float32"), "LK": ("sbuf", [128, 64], "float32"),
+    "t0": ("sbuf", [128, 256], "float32"), "t1": ("sbuf", [128, 256], "float32"), "t2": ("sbuf", [128, 256], "float32"),
+    "t3": ("sbuf", [128, 256], "float32"), "i0": ("sbuf", [128, 256], "int32"), "i1": ("sbuf", [128, 256], "int32"),
+    "i2": ("sbuf", [128, 256], "int32"), "nxf": ("sbuf", [128, 256], "float32"),
+    "Lx": ("sbuf", [128, 256], "uint16"), "Lz": ("sbuf", [128, 256], "uint16"), "Lp": ("sbuf", [128, 256], "uint16"),
+    "Ln": ("sbuf", [128, 256], "uint16"), "Ly": ("sbuf", [128, 240], "uint16"), "Lo": ("sbuf", [128, 16], "uint16"),
+    "Q": ("sbuf", [128, 256], "uint16"), "FI": ("sbuf", [128, 240], "uint16"), "DI": ("sbuf", [128, 240], "uint16"),
+    "DL": ("sbuf", [128, 256], "bfloat16"), "AB": ("sbuf", [128, 256], "float32"), "E": ("sbuf", [128, 128], "float32"),
+    "CO": ("sbuf", [128, 256], "float32"), "S": ("sbuf", [128, 128], "bfloat16"), "SE": ("sbuf", [128, 128], "float32"),
+    "TM": ("sbuf", [128, 256], "float32"), "U2": ("sbuf", [128, 128], "float32"), "q0": ("sbuf", [128, 16], "float32"),
+    "QA": ("sbuf", [128, 240], "float32"), "TT": ("sbuf", [128, 240], "float32"),
+    "DE": ("sbuf", [128, 240], "float32"), "VC": ("sbuf", [128, 240], "float32"), "U": ("sbuf", [128, 240], "float32"),
+    "CM": ("sbuf", [128, 1920], "bfloat16"), "DF": ("sbuf", [128, 240], "float32"), "YN": ("sbuf", [128, 256], "float32"),
+    "pp0": ("psum", [128, 512], "float32"), "pp1": ("psum", [128, 512], "float32"), "pp2": ("psum", [128, 512], "float32"),
+    "pp3": ("psum", [128, 512], "float32"), "pm0": ("psum", [128, 512], "float32"), "pm1": ("psum", [128, 512], "float32"),
+    "pc": ("psum", [128, 512], "float32"), "pn": ("psum", [128, 512], "float32"),
+}
+for _t in range(R):
+    SCRATCH["G%d" % _t] = ("sbuf", [128, W], "bfloat16")
+    SCRATCH["OB%d" % _t] = ("sbuf", [128, ST], "bfloat16")
+NDMA = 40
+SEMAPHORES = ["cv", "cs", "ct", "cg", "zarr", "sent"] + ["arr%d" % t for t in range(R)] + ["d%d" % k for k in range(NDMA)]
+
+
+def rank_program(g, core, T, topo):
+    rank = T.rank_of(core)
+    if rank is None:
+        return
+    n = len(T.cores)
+    nxt, prv = T.cores[(rank + 1) % n], T.cores[(rank - 1) % n]
+    Q = {"v": g.vector, "s": g.scalar, "t": g.tensor, "g": g, "y": g.sync}
+    cnt = {"v": 0, "s": 0, "t": 0, "g": 0}
+    waited = {e: {} for e in Q}
+    wr, rd, bank, total = {}, {}, {}, {}
+    nd = [0]
+
+    def wait(e, tok):
+        if waited[e].get(tok[0], 0) < tok[1]:
+            Q[e].wait_ge(T.sem[tok[0]], tok[1])
+            waited[e][tok[0]] = tok[1]
+
+    def deps(e, r, w, b):
+        need = {}
+        own = "c" + e
+
+        def add(tok):
+            need[tok[0]] = max(need.get(tok[0], 0), tok[1])
+        for k in r:
+            assert k in wr or k in OPT, k
+            if k in wr and not (e == "t" and wr[k][0] == own):
+                add(wr[k])
+        for k in w:
+            if k in wr and not (e == "t" and wr[k][0] == own):
+                add(wr[k])
+            for s, v in rd.get(k, {}).items():
+                if not (e == "t" and s == own):
+                    add((s, v))
+        for k in b:
+            for s, v in bank.get(k, {}).items():
+                if s != own:
+                    add((s, v))
+        for s in need:
+            wait(e, (s, need[s]))
+
+    def mark(tok, r, w, b):
+        total[tok[0]] = tok[1]
+        for k in r:
+            rd.setdefault(k, {})[tok[0]] = tok[1]
+        for k in w:
+            wr[k] = tok
+            rd[k] = {}
+        for k in b:
+            bank.setdefault(k, {})[tok[0]] = tok[1]
+
+    def op(e, fns, r=(), w=(), b=()):
+        deps(e, r, w, b)
+        if not isinstance(fns, list):
+            fns = [fns]
+        ins = None
+        for f in fns:
+            ins = f()
+        cnt[e] += 1
+        ins.then_inc(T.sem["c" + e], 1)
+        mark(("c" + e, cnt[e]), r, w, b)
+
+    def dma(e, out, in_, r=(), w=()):
+        deps(e, r, w, ())
+        s = "d%d" % nd[0]
+        nd[0] += 1
+        Q[e].dma_start(out, in_).then_inc(T.sem[s], 16)
+        mark((s, 16), r, w, ())
+
+    def lanes(src, dst):
+        es = topo.engines(src, dst)[::2]
+        m = 0
+        for x in es:
+            m |= 1 << x
+        return m, len(es)
+
+    nsent = [0]
+
+    def send(dst, out, in_, sem, r):
+        deps("g", r, (), ())
+        m, k = lanes(core, dst)
+        rid, pid, _ = topo.addr(dst)
+        g.remote_dma(out, in_, T.sem[sem], T.sem.sent, pid, rid, m)
+        nsent[0] += k
+        total["sent"] = nsent[0]
+
+    v, s, pe = g.vector, g.scalar, g.tensor
+
+    def ts(out, in0, s1, s2, o0, o1=None, **k):
+        if o1 is None:
+            op("v", lambda: v.tensor_scalar(out, in0, s1, None, o0), **k)
+        else:
+            op("v", lambda: v.tensor_scalar(out, in0, s1, s2, o0, o1), **k)
+
+    def tt(out, a, b_, o, **k):
+        op("v", lambda: v.tensor_tensor(out, a, b_, o), **k)
+
+    def cp(out, a, **k):
+        op("v", lambda: v.tensor_copy(out, a), **k)
+
+    def ms(out, c, **k):
+        op("v", lambda: v.memset(out, c), **k)
+
+    def act(out, a, bias=None, **k):
+        if bias is not None:
+            op("s", lambda: s.activation(out, a, F.Identity, bias=bias), **k)
+        else:
+            op("s", lambda: s.activation(out, a, F.Copy), **k)
+
+    def mm(lst, **k):
+        op("t", [(lambda a=a: pe.matmul(*a)) for a in lst], **k)
+
+    def iota(out, pat, base, cm, key, flt=True):
+        wait("g", ("cg", cnt["g"]))
+        if flt:
+            op("g", lambda: g.iota(out, pat, base, cm, allow_small_or_imprecise_dtypes=True), w=[key])
+        else:
+            op("g", lambda: g.iota(out, pat, base, cm), w=[key])
+
+    G = [T["G%d" % t] for t in range(R)]
+    OB = [T["OB%d" % t] for t in range(R)]
+    ZG = [T.ZG0, T.ZG1]
+    pp = [T.pp0, T.pp1, T.pp2, T.pp3]
+    pm = [T.pm0, T.pm1]
+    XK = ["Xh", "Xo", "Xg1", "Xg2"]
+    PK = ["P0%d" % b for b in range(4)] + ["P1%d" % b for b in range(4)]
+    NK = ["NLa", "NLb", "tail"] + PK
+    cb = [8.0 * (b % 2) + 1024.0 * (b // 2) for b in range(4)]
+    pf, pi, pi1, pg, adj, nadj, wf = [T.col[:, k:k + 1] for k in range(7)]
+    TS = T.pm1
+
+    dma("y", T.nxi[:], T.nx[:], w=["nxi"])
+    dma("s", T.XR[:, 0:2176], T.x[:, 0:2176], w=["XRa"])
+    dma("y", T.SB[:, 0:256], T.x[:, 0:256], w=["SBa"])
+    dma("y", T.nui[:, 0:1], T.nu[:], w=["nui"])
+    dma("y", T.XR[:, 2176:W], T.x[:, 2176:W], w=["XRb"])
+    dma("s", T.voi[:], T.vol[:], w=["voi"])
+    dma("y", OB[0][:, 0:256], T.x[:, V:W], w=["OB0"])
+    dma("y", T.lei[:], T.le[:], w=["lei"])
+    dma("y", T.lai[:], T.lag[:], w=["lai"])
+    iota(T.IP[:, 0:1], [[1, 1]], 0, 1, "IP", False)
+    iota(T.IX[:], [[1, 144]], 0, 0, "IX")
+    iota(T.J[:], [[0, 16], [1, 16]], 0, 0, "J")
+    iota(T.OKi[:], [[0, 4], [16, 16]], 0, 0, "OKi")
+    iota(T.NL[:, 8192:8960], [[1, 768]], 8192 + ST, 0, "tail0")
+    ms(T.SB[:, 256:ST], 0.0, w=["SBb"])
+    ms(T.XR[:, W:4368], 0.0, w=["XRz"])
+    ms(T.LB[:, 0:128], 1.0 / 32, w=["LB"])
+    ms(T.LB[:, 128:256], 1.0 / 16, w=["LB2"])
+    ms(T.ZR[:], 0.0, w=["ZR"])
+    ms(OB[0][:, 256:ST], 0.0, w=["OBz"])
+    ms(TS[:, 256:272], 0.0, w=["T0"], b=["pm1"])
+    ms(T.S[:], 0.0, w=["S0", "S1"])
+    ts(T.IQ[:, 0:1], T.IP[:, 0:1], 15, None, A.bitwise_and, r=["IP"], w=["IQ"])
+    cp(pf, T.IP[:, 0:1], r=["IP"], w=["pf"])
+    cp(pi, T.IQ[:, 0:1], r=["IQ"], w=["pi"])
+    tt(pg, pf, pi, A.subtract, r=["pf", "pi"], w=["pg"])
+    ts(pi1, pi, 1.0, None, A.add, r=["pi"], w=["pi1"])
+    ts(adj, pi, 15.0, 16384.0, A.is_lt, A.mult, r=["pi"], w=["adj"])
+    ts(nadj, pi, 15.0, -16384.0, A.is_lt, A.mult, r=["pi"], w=["nadj"])
+    ts(T.RM[:], T.J[:, 0:16], pi, -2048.0, A.is_equal, A.mult, r=["J", "pi"], w=["RM"])
+    tt(T.t0[:, 0:128], T.IX[:, 0:128], T.J[:, 0:128], A.subtract, r=["IX", "J"], w=["t0"])
+    ts(T.Bf[:], T.IX[:], -15.0, pg, A.add, A.is_equal, r=["IX", "pg"], w=["Bf"])
+    ts(T.BO[:], T.t0[:, 0:128], pg, None, A.is_equal, r=["t0", "pg"], w=["BO"])
+    ts(T.ID[:], T.IX[:, 0:128], pf, 256.0, A.is_equal, A.mult, r=["IX", "pf"], w=["ID"])
+    ts(T.t2[:], T.J[:], pi, 32768.0, A.is_equal, A.mult, r=["J", "pi"], w=["t2"])
+    ts(T.t3[:], T.J[:], pi1, -16384.0, A.is_equal, A.mult, r=["J", "pi1"], w=["t3"])
+    tt(T.M[:], T.t2[:], T.t3[:], A.add, r=["t2", "t3"], w=["M"])
+    op("s", [(lambda i=i: s.activation(T.FM[:, 128 * i:128 * i + 128], T.BO[:], F.Identity, scale=T.RM[:, i:i + 1]))
+             for i in range(16)], r=["BO", "RM"], w=["FM"])
+    op("v", [(lambda j=j: v.memset(T.R1[0:32, 64 * j:64 * j + 64], float(j))) for j in range(8)], w=["R1a"])
+    op("v", [(lambda j=j: v.tensor_scalar(T.R1[32:64, 64 * j:64 * j + 64], T.IX[32:64, 0:64], 16.0, None, A.mult)) for j in range(8)],
+       r=["IX"], w=["R1b"])
+    ts(T.OL[:], T.OKi[:, 0:16], pi, None, A.add, r=["OKi", "pi"], w=["OL"])
+    ts(T.OKK[:], T.OKi[:], pi, 1.0 / 256, A.add, A.mult, r=["OKi", "pi"], w=["OKK"])
+    cp(T.Ln[:], T.nxi[:], r=["nxi"], w=["Ln"])
+    ts(T.pc[:, 0:256], T.nxi[:], float(V), None, A.is_ge, r=["nxi"], w=["c0"], b=["pc"])
+    cp(T.nxf[:], T.nxi[:], r=["nxi"], w=["nxf"])
+    cp(T.SB[:, 257:258], T.nui[:, 0:1], r=["nui", "SBb"], w=["SBc"])
+    send(prv, T.ZB[:], T.SB[:], "zarr", ["SBa", "SBb", "SBc"])
+    wr["ZB"] = ("zarr", lanes(nxt, core)[1])
+    total["zarr"] = wr["ZB"][1]
+
+    def silu(j):
+        a, b = SILU[j], SILU[j + 1]
+        op("s", lambda: s.activation(T.PV[:, :].indirect(T.Ln[:, a:b]), T.NL[:, 8192 + 16 * a:8192 + 16 * b], F.Silu),
+           r=["Ln", ("tail0", "tail")[j]], w=["PV"])
+
+    silu(0)
+    tt(T.t0[:, 0:128], T.voi[:, 0:128], T.voi[:, 128:256], A.add, r=["voi"], w=["t0"])
+    ts(T.pc[:, 256:512], T.pc[:, 0:256], float(W), None, A.mult, r=["c0"], w=["c1"], b=["pc"])
+    ts(T.DL[:, 0:128], T.t0[:, 0:128], -2.0 ** -20, None, A.mult, r=["t0"], w=["DLS"])
+    tt(T.t3[:], T.pc[:, 256:512], T.nxf[:], A.max, r=["c1", "nxf"], w=["t3"], b=["pc"])
+    tt(T.t2[:], T.pc[:, 0:256], T.nxf[:], A.mult, r=["c0", "nxf"], w=["t2"], b=["pc"])
+    cp(T.Lx[:], T.t3[:], r=["t3"], w=["Lx"])
+    ts(T.pc[:, 256:512], T.pc[:, 0:256], -float(W), 256.0, A.mult, A.add, r=["c0"], w=["c1"], b=["pc"])
+    ts(T.DL[:, 128:256], T.voi[:, 128:256], -2.0 ** -20, None, A.mult, r=["voi"], w=["DL1"])
+    tt(T.t1[:], T.pc[:, 256:512], T.t2[:], A.add, r=["c1", "t2"], w=["t1"], b=["pc"])
+    cp(wf, T.nui[:, 0:1], r=["nui"], w=["wf"])
+    cp(T.Lz[:], T.t1[:], r=["t1"], w=["Lz"])
+    ts(T.Bw[:], T.Bf[:], wf, None, A.mult, r=["Bf", "wf"], w=["Bw"])
+
+    def spread(src, first, key):
+        for b in range(4):
+            lst = []
+            if first is not None:
+                lst.append((pp[b][:, :], first, T.R1[0:64, :], True, False))
+            for i8 in range(8):
+                i = 8 * (b % 2) + i8
+                lst.append((pp[b][:, 64 * i8:64 * i8 + 64], T.FM[:, 128 * i:128 * i + 128],
+                            src[:, 64 * (b // 2):64 * (b // 2) + 64], False, key != "DL1" and i8 == 7))
+            kk = key if first is not None else key + str(b // 2)
+            mm(lst, r=[kk, "FM", "LB", "LB2", "R1a", "R1b"], w=["pp%d" % b], b=["pp%d" % b])
+
+    spread(T.DL[:, 0:128], T.LB[0:64, 128:256], "DLS")
+    for b in range(4):
+        act(T.SUM[:, 512 * b:512 * b + 512], pp[b][:, :], bias=cb[b], r=["pp%d" % b], w=["SUM"], b=["pp%d" % b])
+    spread(T.DL[:, 128:256], T.LB[0:64, 0:128], "DL1")
+
+    for h in range(2):
+        op("v", [(lambda c=c: v.tensor_copy(T.X[:, 16 * c:16 * c + 1024], T.XR[:, :].indirect(T.Lx[:, c:c + 64])))
+                 for c in (64 * h, 128 + 64 * h)], r=["XRa", "XRb", "XRz", "Lx"], w=[("Xi", "Xh")[h]])
+        op("s", [(lambda c=c: s.activation(ZG[0][:, 16 * c:16 * c + 1024], T.ZB[:, :].indirect(T.Lz[:, c:c + 64]), F.Copy))
+                 for c in (64 * h, 128 + 64 * h)], r=["ZB", "Lz"], w=[("ZGi", "ZG0")[h]])
+        if h == 0:
+            ts(T.Bz[:], T.Bf[:], T.ZB[:, 257:258], None, A.mult, r=["Bf", "ZB"], w=["Bz"])
+    act(ZG[1][:, 0:2048], OB[0][:, :].indirect(T.Lz[:, 0:128]), r=["OB0", "OBz", "Lz"], w=["ZG1"])
+    send(nxt, G[0][:, 0:256], OB[0][:, 0:256], "arr0", ["OB0"])
+    iota(T.NL[:, 8960:12288], [[1, 3328]], 8960 + ST, 0, "tail")
+    dma("y", T.X[:, V:W], T.x[:, V:W], w=["Xo"])
+    dma("y", G[0][:, 256:512], T.x[:, 0:256], w=["G0s1"])
+    dma("y", T.X[:, W:2 * W], T.x[:, :], w=["Xg1"])
+    dma("y", T.X[:, 2 * W:XW], T.x[:, 0:XW - 2 * W], w=["Xg2"])
+
+    def content(src, lhs, h, first, last, keys):
+        lst = []
+        if first:
+            lst.append((pm[h][:, 0:128], T.ZR[:, :], T.ZR[:, :], True, False))
+        for i in range(16):
+            for a in range(2):
+                o = 2048 * a + 1024 * h
+                lst.append((pm[h][:, 64 * a:64 * a + 64], lhs[:, 15 - i:143 - i], src[:, o + i:o + 1024:16], False,
+                            last and i == 15 and a == 1))
+        mm(lst, r=keys + ["ZR"], w=["pm%d" % h], b=["pm%d" % h])
+
+    content(T.X, T.Bw, 0, True, False, ["Xi", "Bw"])
+    content(ZG[0], T.Bz, 0, False, True, ["ZGi", "Bz"])
+    content(T.X, T.Bw, 1, True, False, ["Xh", "Bw"])
+    content(ZG[0], T.Bz, 1, False, True, ["ZG0", "Bz"])
+    for h in range(2):
+        c = 64 * h
+        tt(T.AB[:, 128 * h:128 * h + 64], T.lei[:, 256 + c:320 + c], T.lei[:, c:64 + c], A.subtract, r=["lei"], w=["ABa%d" % h])
+        tt(T.AB[:, 128 * h + 64:128 * h + 128], T.lei[:, 128 + c:192 + c], T.lei[:, 384 + c:448 + c], A.subtract, r=["lei"], w=["ABb%d" % h])
+    def positions():
+        ts(T.i1[:], T.nxi[:], 15, None, A.bitwise_and, r=["nxi"], w=["i1"])
+        ts(T.i0[:], T.nxi[:], 0xC00, None, A.bitwise_and, r=["nxi"], w=["i0"])
+        ts(T.pn[:, 0:256], T.i1[:], 64.0, None, A.mult, r=["i1"], w=["n0"], b=["pn"])
+        ts(T.i2[:], T.nxi[:], 4, 63, A.logical_shift_right, A.bitwise_and, r=["nxi"], w=["i2"])
+        tt(T.pn[:, 256:512], T.pn[:, 0:256], T.i0[:], A.add, r=["n0", "i0"], w=["n1"], b=["pn"])
+        ts(T.Bp[:], T.Bf[:], wf, 512.0, A.mult, A.mult, r=["Bf", "wf"], w=["Bp"])
+        tt(T.pn[:, 0:256], T.pn[:, 256:512], T.i2[:], A.add, r=["n1", "i2"], w=["n0"], b=["pn"])
+        tt(T.t1[:], T.pn[:, 0:256], T.t2[:], A.max, r=["n0", "t2"], w=["t1"], b=["pn"])
+        cp(T.Lp[:], T.t1[:], r=["t1"], w=["Lp"])
+
+    positions()
+
+    def back(a, b, o):
+        lst = [(T.pm0[:, o:o + b - a], T.Bf[:, 15 - i:143 - i], T.PV[:, 16 * a + i:16 * b:16], i == 0, i == 15) for i in range(16)]
+        mm(lst, r=["PV", "Bf"], w=["bk"], b=["pm0"])
+
+    def factors(h):
+        c = 64 * h
+        tt(T.SE[:, c:c + 64], T.S[:, c:c + 64], T.E[:, c:c + 64], A.mult, r=["S%d" % h, "E%d" % h], w=["SE%d" % h])
+        op("v", [(lambda q=q: v.tensor_tensor(T.CO[:, 64 * q:64 * q + 64], T.AB[:, 64 * q:64 * q + 64], T.SE[:, c:c + 64], A.subtract))
+                 for q in (2 * h, 2 * h + 1)], r=["SE%d" % h], w=["CO%d" % h])
+
+    def labels(out, o, k, key):
+        ts(out, T.pm0[:, o:o + k], 1.0 / 16, 0.25 - TB, A.mult, A.add, r=["bk"], w=[key], b=["pm0"])
+
+    for t in range(R):
+        last = t == R - 1
+        wr["G%ds0" % t] = ("arr%d" % t, lanes(prv, core)[1])
+        total["arr%d" % t] = wr["G%ds0" % t][1]
+        co = T.AB if t == 0 else T.CO
+        if t > 0:
+            dma("y", OB[t][:, 0:256], T.X[:, V:W], r=["Xo"], w=["OB%d" % t])
+            send(nxt, G[t][:, 0:256], OB[t][:, 0:256], "arr%d" % t, ["OB%d" % t])
+            content(T.X, T.Bw, 0, False, True, ["Xh", "Bw"])
+            content(T.X, T.Bw, 1, False, True, ["Xh", "Bw"])
+        if last:
+            dma("y", T.y[:, 0:256], G[t][:, 0:256], r=["G%ds0" % t])
+        else:
+            dma("y", G[t + 1][:, 256:512], G[t][:, 0:256], r=["G%ds0" % t], w=["G%ds1" % (t + 1)])
+        for h in range(2):
+            a = 128 * h
+            tt(T.TM[:, a:a + 128], co[:, a:a + 128], pm[h][:, 0:128], A.mult,
+               r=["pm%d" % h, "ABa%d" % h, "ABb%d" % h, "CO%d" % h], w=["TM%d" % h], b=["pm%d" % h])
+            tt(T.U2[:, 64 * h:64 * h + 64], T.TM[:, a:a + 64], T.TM[:, a + 64:a + 128], A.add, r=["TM%d" % h], w=["U2%d" % h])
+            tt(T.S[:, 64 * h:64 * h + 64], T.U2[:, 64 * h:64 * h + 64], T.S[:, 64 * h:64 * h + 64], A.is_lt,
+               r=["U2%d" % h, "S%d" % h], w=["S%d" % h])
+            if h == 0:
+                ts(T.q0[:], T.S[:, 0:16], 2048.0, nadj, A.mult, A.add, r=["S0", "nadj"], w=["q0"])
+                tt(T.SC[:, 15:256:16], T.q0[:], T.OL[:], A.add, r=["q0", "OL"], w=["SC0"])
+                ts(T.Q[:, 0:16], T.SC[:, 15:256:16], adj, None, A.add, r=["SC0", "adj"], w=["Q1"])
+            if 0 < t < R - 1 and h == 0:
+                factors(0)
+            if t == 0 and h == 0:
+                cp(ZG[1][:, 2048:3072], OB[0][:, :].indirect(T.Lz[:, 128:192]), r=["OB0", "OBz", "Lz"], w=["ZG1v"])
+        spread(T.S, None, "S")
+        for b in range(4):
+            o = V + 512 * b
+            act(T.NL[:, o + 2048:o + 2560], pp[b][:, :], bias=cb[b] + 2048.0, r=["pp%d" % b], w=["P1%d" % b], b=["pp%d" % b])
+            b ^= 1
+            o = V + 512 * b
+            tt(T.NL[:, o:o + 512], T.SUM[:, 512 * b:512 * b + 512], pp[b][:, :], A.subtract,
+               r=["pp%d" % b, "SUM"], w=["P0%d" % b], b=["pp%d" % b])
+        cp(T.NL[:, 0:2048], T.NL[:, V:V + W].indirect(T.Lp[:, 0:128]), r=PK + ["tail0", "Lp"], w=["NLa"])
+        act(T.NL[:, 2048:V], T.NL[:, V:V + W].indirect(T.Lp[:, 128:256]), r=PK + ["tail0", "Lp"], w=["NLb"])
+        if t == 1:
+            back(256, 272, 256)
+        if not last:
+            spread(T.DL[:, 128:256], T.LB[0:64, 0:128], "DL1")
+        if t >= 2:
+            back(16 + 120 * (t - 2), 136 + 120 * (t - 2), 256)
+
+        side = []
+
+        part = [-1]
+
+        def job(k, ns, f):
+            side.append((k, ns, f, part[0]))
+
+        if t == 0:
+            job(1, 60, lambda: cp(T.LK[:, 0:16], T.lai[:], r=["lai"], w=["LK0"]))
+            for h in range(2):
+                job(1, 110, lambda h=h: tt(T.E[:, 64 * h:64 * h + 64], T.AB[:, 128 * h:128 * h + 64], T.AB[:, 128 * h + 64:128 * h + 128],
+                                           A.add, r=["ABa%d" % h, "ABb%d" % h], w=["E%d" % h]))
+            job(1, 160, lambda: op("v", [(lambda j=j: v.tensor_copy(T.LK[:, 16 * j:16 * j + 16], T.LK[:, 0:16])) for j in (1, 2, 3)],
+                                   r=["LK0"], w=["LK"]))
+            for a in range(192, 256, 16):
+                job(1, 380, lambda a=a: cp(ZG[1][:, 16 * a:16 * a + 256], OB[0][:, :].indirect(T.Lz[:, a:a + 16]),
+                                           r=["OB0", "OBz", "Lz"], w=["ZG1v"]))
+        if not last:
+            for h in ((0, 1) if t == 0 else (1,)):
+                job(1, 380, lambda h=h: factors(h))
+        else:
+            job(1, 215, lambda: tt(T.t0[:, 0:128], T.nxf[:, 128:256], T.nxf[:, 0:128], A.subtract, r=["nxf"], w=["t0"]))
+            job(1, 215, lambda: tt(T.t0[:, 0:128], T.t0[:, 0:128], T.S[:, :], A.mult, r=["t0", "S0", "S1"], w=["t0"]))
+            job(1, 215, lambda: tt(T.YN[:, 0:128], T.nxf[:, 0:128], T.t0[:, 0:128], A.add, r=["nxf", "t0"], w=["YNa"]))
+            job(1, 215, lambda: tt(T.YN[:, 128:256], T.nxf[:, 128:256], T.t0[:, 0:128], A.subtract, r=["nxf", "t0"], w=["YNb"]))
+            job(1, 0, lambda: dma("y", T.yn[:], T.YN[:], r=["YNa", "YNb"]))
+        if t == 1:
+            job(1, 60, lambda: labels(T.Lo[:, :], 256, 16, "Lo"))
+        if t in (1, 2):
+            zk = "ZG%d" % ((t + 1) % 2)
+            for a in (0, 8):
+                job(2, 400, lambda a=a, zk=zk: cp(ZG[(t + 1) % 2][:, :].indirect(T.Lo[:, a:a + 8]), OB[t][:, 16 * a:16 * a + 128],
+                                                  r=["Lo", "OB%d" % t], w=[zk, zk + "v"]))
+        coff = [0]
+
+        def feet(p):
+            k0, k1 = PARTS[p]
+            a, b = 16 * (k0 - 1), 16 * k1
+            wd = b - a
+            raw = T.SC[:, 256 * k0 + 15:256 * (k1 + 1):16]
+            sk = ["SC%d" % k for k in range(k0, k1 + 1)]
+            k = k1 + 1
+            qa, tq = TS[:, 128:128 + wd], TS[:, 192:192 + wd]
+            job(k1, 60, lambda: ts(qa, T.Q[:, a + 16:b + 16], nadj, None, A.add,
+                                   r=["Q%d" % (j + 1) for j in range(k0, k1 + 1)] + ["nadj"], w=["QA"], b=["pm1"]))
+            job(k1, 60, lambda: ts(tq, raw, float(V - TB), None, A.add, r=sk, w=["TT"], b=["pm1"]))
+            job(k1, 60, lambda: tt(T.DE[:, a:b], raw, qa, A.subtract, r=sk + ["QA"], w=["DE%d" % p], b=["pm1"]))
+            job(k1, 60, lambda: tt(T.DF[:, a:b], T.SC[:, 256 * (k0 - 1) + 15:256 * k1:16], tq, A.max,
+                                   r=sk + ["SC%d" % (k0 - 1), "TT"], w=["DF%d" % p], b=["pm1"]))
+            job(k1, 110, lambda: ts(T.DI[:, a:b], T.DF[:, a:b], adj, None, A.add, r=["DF%d" % p, "adj"], w=["DI%d" % p]))
+            job(k, 60, lambda: tt(T.VC[:, a:b], T.DE[:, a:b], T.pc[:, a:b], A.mult, r=["DE%d" % p, "pc%d" % p], w=["VC%d" % p], b=["pc"]))
+            for j in range(k0, k1 + 1):
+                job(k, 110, lambda j=j: tt(TS[:, 256 + 16 * j:272 + 16 * j], TS[:, 240 + 16 * j:256 + 16 * j], T.VC[:, 16 * j - 16:16 * j],
+                                           A.add, r=["T%d" % (j - 1), "VC%d" % p], w=["T%d" % j], b=["pm1"]))
+            tk = ["T%d" % j for j in range(k1 + 1)]
+            job(k, 110, lambda: tt(T.U[:, a:b], TS[:, 272 + a:272 + b], T.LK[:, 0:wd], A.subtract, r=tk + ["LK", "LK0"],
+                                   w=["U%d" % p], b=["pm1"]))
+            ds = list(range(1, k1 + 1))
+            for x in range(0, k1, 4):
+                grp = []
+                for d in ds[x:x + 4]:
+                    lo = max(k0, d)
+                    grp.append((d, lo, 16 * (k1 + 1 - lo), coff[0]))
+                    coff[0] += 16 * (k1 + 1 - lo)
+
+                def cmpj(grp=grp, x=x):
+                    key = "CM%d_%d" % (p, x)
+                    op("v", [(lambda d=d, lo=lo, w_=w_, o=o: v.tensor_tensor(
+                        T.CM[:, o:o + w_], T.U[:, 16 * (lo - 1):b], TS[:, 256 + 16 * (lo - d):256 + 16 * (lo - d) + w_], A.is_ge))
+                        for d, lo, w_, o in grp], r=tk + ["U%d" % p], w=[key], b=["pm1"])
+                    lst = [(T.pn[:, a:b], T.ID[:, :], T.OKK[:, 0:wd], True, False)] if x == 0 else []
+                    lst += [(T.pn[:, 16 * (lo - 1):b], T.ID[:, :], T.CM[:, o:o + w_], False, d == k1) for d, lo, w_, o in grp]
+                    mm(lst, r=[key, "ID", "OKK"], w=["pn%d" % p], b=["pn"])
+                job(k, 55 * len(grp), cmpj)
+            job(k + FLAG[p], 60, lambda: cp(T.FI[:, a:b], T.pn[:, a:b], r=["pn%d" % p], w=["FI%d" % p], b=["pn"]))
+
+        def fetch(j, e):
+            a, b, p = MOVES[j]
+            k1 = PARTS[p][1]
+            gk = ["G%ds0" % t, "G%ds1" % t] + ["G%dp%d" % (t, k) for k in range(1, k1)]
+            e(T.NEW[:, 16 * a:16 * b], G[t][:, 0:256 * (k1 + 1)].indirect(T.FI[:, a:b]), r=gk + ["FI%d" % p], w=["NEW%d" % j])
+
+        def store(j0, j1):
+            a, b = MOVES[j0][0], MOVES[j1 - 1][1]
+            cp(T.X[:, :].indirect(T.DI[:, a:b]), T.NEW[:, 16 * a:16 * b],
+               r=["NEW%d" % j for j in range(j0, j1)] + ["DI%d" % MOVES[j][2] for j in range(j0, j1)], w=XK)
+
+        for p in range(len(PARTS)):
+            part[0] = p
+            feet(p)
+            if p == 0 and t >= 2:
+                job(PARTS[0][1] + 3, 110, lambda: labels(T.Ly[:, 120 * (t - 2):120 * (t - 1)], 256, 120, "Ly%d" % (t - 2)))
+            for j in range(NV):
+                if FETCH[j][0] == p:
+                    job(FETCH[j][1], 390, lambda j=j: fetch(j, cp))
+
+        def flush(p, k=99):
+            for x in [x for x in side if x[3] <= p and x[0] <= k]:
+                side.remove(x)
+                x[2]()
+
+        def drain(k, ns):
+            j = 0
+            while j < len(side) and ns > 0:
+                if side[j][0] <= k and side[j][1] <= ns + 40:
+                    x = side.pop(j)
+                    ns -= x[1]
+                    x[2]()
+                elif side[j][0] <= k:
+                    return
+                else:
+                    j += 1
+
+        for k in range(1, 16):
+            ql = T.Q[:, 16 * (k - 1):16 * k]
+            act(T.GW[:, :], T.NL[:, 0:XW].indirect(ql), r=NK + ["tail0", "Q%d" % k], w=["GW"])
+            act(G[t][:, 256 * (k + 1):256 * (k + 2)], T.X[:, :].indirect(ql), r=XK + ["Q%d" % k], w=["G%dp%d" % (t, k)])
+            op("v", lambda k=k: v.tensor_tensor_scan(T.SC[:, 256 * k:256 * k + 256], T.M[:, :], T.GW[:, :], 0.0, A.add, A.min),
+               r=["M", "GW"], w=["SC%d" % k])
+            ts(T.Q[:, 16 * k:16 * k + 16], T.SC[:, 256 * k + 15:256 * k + 256:16], adj, None, A.add,
+               r=["SC%d" % k, "adj"], w=["Q%d" % (k + 1)])
+            for p, (k0, k1) in enumerate(PARTS):
+                if k == k1:
+                    mm([(T.pc[:, 16 * (k0 - 1):16 * k1], T.Bp[:, 15 - i:143 - i], G[t][:, 256 * (k0 + 1) + i:256 * (k1 + 2):16],
+                         i == 0, i == 15) for i in range(16)],
+                       r=["Bp"] + ["G%dp%d" % (t, j) for j in range(k0, k1 + 1)], w=["pc%d" % p], b=["pc"])
+            if k < 15:
+                drain(k, BUDGET)
+        np_ = len(PARTS) - 1
+        flush(np_ - 2)
+        for j in range(NV, len(MOVES) - 2):
+            fetch(j, act)
+        flush(np_, 15)
+        store(0, NV)
+        flush(np_ - 1)
+        fetch(len(MOVES) - 2, act)
+        flush(np_, 16)
+        store(NV, NV + 1)
+        flush(np_)
+        fetch(len(MOVES) - 1, act)
+        if not last:
+            z = (t + 1) % 2
+            content(ZG[z], T.Bz, 0, True, False, ["ZG%d" % z, "ZG%dv" % z, "Bz"])
+            content(ZG[z], T.Bz, 1, True, False, ["ZG%d" % z, "ZG%dv" % z, "Bz"])
+        if t == 0:
+            silu(1)
+        for j in range(NV + 1, len(MOVES)):
+            store(j, j + 1)
+
+    dma("y", T.y[:, V:W], T.X[:, V:W], r=["Xo"])
+    for j in range(len(FINV) - 1):
+        for e in range(2):
+            a, b = 120 * e + FINV[j], 120 * e + FINV[j + 1]
+            (cp, act)[e](T.XR[:, 16 * a:16 * b], T.X[:, 0:V].indirect(T.Ly[:, a:b]), r=["Xh", "Ly%d" % e], w=["Y%d%d" % (e, j)])
+            dma("y", T.y[:, 256 + 16 * a:256 + 16 * b], T.XR[:, 16 * a:16 * b], r=["Y%d%d" % (e, j)])
+    for k in total:
+        wait("g", (k, total[k]))

@@ -7,13 +7,15 @@ ST = 272
 TB = 8464
 XW = 12256
 PARTS = [(1, 3), (4, 7), (8, 11), (12, 15)]
-FLAG = [2, 3, 4, 1]
+LAT, MM, SCAT, SLACK, PIECE = 150, 45, 45, 80, 12
+SL2 = (20, 20)
 BUDGET = 500
-SILU = [0, 48, 256]
+SILU = [0, 48, 144, 256]
 FINV = [0, 56, 96, 120]
-MOVES = [(0, 16, 0), (16, 48, 0), (48, 112, 1), (112, 176, 2), (176, 240, 3)]
-NV = 1
-FETCH = [(0, 7)]
+MOVES = [(0, 8, 0), (8, 16, 0), (16, 48, 0), (48, 112, 1), (112, 176, 2), (176, 240, 3)]
+NV = 2
+FETCH = [(0, 1), (0, 1)]
+CG = 3
 OPT = ("CO0", "CO1", "ZG0v")
 
 SCRATCH = {
@@ -72,7 +74,12 @@ def rank_program(g, core, T, topo):
             Q[e].wait_ge(T.sem[tok[0]], tok[1])
             waited[e][tok[0]] = tok[1]
 
-    def deps(e, r, w, b):
+    clk = {e: 0.0 for e in Q}
+    fin = {}
+    probe = [None]
+    cost = [60.0]
+
+    def deps(e, r, w, b, dry=False):
         need = {}
         own = "c" + e
 
@@ -92,8 +99,13 @@ def rank_program(g, core, T, topo):
             for s, v in bank.get(k, {}).items():
                 if s != own:
                     add((s, v))
+        st = clk[e]
         for s in need:
-            wait(e, (s, need[s]))
+            if waited[e].get(s, 0) < need[s]:
+                st = max(st, fin.get((s, need[s]), -LAT) + LAT)
+            if not dry:
+                wait(e, (s, need[s]))
+        return st
 
     def mark(tok, r, w, b):
         total[tok[0]] = tok[1]
@@ -105,8 +117,12 @@ def rank_program(g, core, T, topo):
         for k in b:
             bank.setdefault(k, {})[tok[0]] = tok[1]
 
-    def op(e, fns, r=(), w=(), b=()):
-        deps(e, r, w, b)
+    def op(e, fns, r=(), w=(), b=(), ns=None):
+        if probe[0] is not None:
+            probe[0].append((e, list(r), list(w), list(b)))
+            return
+        clk[e] = deps(e, r, w, b) + (cost[0] if ns is None else ns)
+        fin[("c" + e, cnt[e] + 1)] = clk[e]
         if not isinstance(fns, list):
             fns = [fns]
         ins = None
@@ -117,6 +133,8 @@ def rank_program(g, core, T, topo):
         mark(("c" + e, cnt[e]), r, w, b)
 
     def dma(e, out, in_, r=(), w=()):
+        if probe[0] is not None:
+            return
         deps(e, r, w, ())
         s = "d%d" % nd[0]
         nd[0] += 1
@@ -164,7 +182,7 @@ def rank_program(g, core, T, topo):
             op("s", lambda: s.activation(out, a, F.Copy), **k)
 
     def mm(lst, **k):
-        op("t", [(lambda a=a: pe.matmul(*a)) for a in lst], **k)
+        op("t", [(lambda a=a: pe.matmul(*a)) for a in lst], ns=MM * len(lst), **k)
 
     def iota(out, pat, base, cm, key, flt=True):
         wait("g", ("cg", cnt["g"]))
@@ -240,7 +258,7 @@ def rank_program(g, core, T, topo):
     def silu(j):
         a, b = SILU[j], SILU[j + 1]
         op("s", lambda: s.activation(T.PV[:, :].indirect(T.Ln[:, a:b]), T.NL[:, 8192 + 16 * a:8192 + 16 * b], F.Silu),
-           r=["Ln", ("tail0", "tail")[j]], w=["PV"])
+           r=["Ln", ("tail0", "tail", "tail")[j]], w=["PV"])
 
     silu(0)
     tt(T.t0[:, 0:128], T.voi[:, 0:128], T.voi[:, 128:256], A.add, r=["voi"], w=["t0"])
@@ -324,9 +342,12 @@ def rank_program(g, core, T, topo):
         lst = [(T.pm0[:, o:o + b - a], T.Bf[:, 15 - i:143 - i], T.PV[:, 16 * a + i:16 * b:16], i == 0, i == 15) for i in range(16)]
         mm(lst, r=["PV", "Bf"], w=["bk"], b=["pm0"])
 
-    def factors(h):
+    def factors(h, only=None):
         c = 64 * h
-        tt(T.SE[:, c:c + 64], T.S[:, c:c + 64], T.E[:, c:c + 64], A.mult, r=["S%d" % h, "E%d" % h], w=["SE%d" % h])
+        if only != 1:
+            tt(T.SE[:, c:c + 64], T.S[:, c:c + 64], T.E[:, c:c + 64], A.mult, r=["S%d" % h, "E%d" % h], w=["SE%d" % h])
+        if only == 0:
+            return
         op("v", [(lambda q=q: v.tensor_tensor(T.CO[:, 64 * q:64 * q + 64], T.AB[:, 64 * q:64 * q + 64], T.SE[:, c:c + 64], A.subtract))
                  for q in (2 * h, 2 * h + 1)], r=["SE%d" % h], w=["CO%d" % h])
 
@@ -356,8 +377,8 @@ def rank_program(g, core, T, topo):
                r=["U2%d" % h, "S%d" % h], w=["S%d" % h])
             if h == 0:
                 ts(T.q0[:], T.S[:, 0:16], 2048.0, nadj, A.mult, A.add, r=["S0", "nadj"], w=["q0"])
-                tt(T.SC[:, 15:256:16], T.q0[:], T.OL[:], A.add, r=["q0", "OL"], w=["SC0"])
-                ts(T.Q[:, 0:16], T.SC[:, 15:256:16], adj, None, A.add, r=["SC0", "adj"], w=["Q1"])
+                tt(T.SC[:, 15:256:16], T.q0[:], T.OL[:], A.add, r=["q0", "OL"], w=["SC0", "SD0"])
+                ts(T.Q[:, 0:16], T.SC[:, 15:256:16], adj, None, A.add, r=["SC0", "adj"], w=["Q1", "QB1"])
             if 0 < t < R - 1 and h == 0:
                 factors(0)
             if t == 0 and h == 0:
@@ -379,12 +400,16 @@ def rank_program(g, core, T, topo):
         if t >= 2:
             back(16 + 120 * (t - 2), 136 + 120 * (t - 2), 256)
 
-        side = []
-
-        part = [-1]
+        side, late = [], []
+        todo = set(["pc%d" % p for p in range(len(PARTS))] + ["NEW%d" % j for j in range(len(MOVES))])
+        for k in range(1, 16):
+            todo.update(["SC%d" % k, "SD%d" % k, "Q%d" % (k + 1), "QB%d" % (k + 1), "G%dp%d" % (t, k)])
 
         def job(k, ns, f):
-            side.append((k, ns, f, part[0]))
+            probe[0] = []
+            f()
+            ops, probe[0] = probe[0], None
+            side.append((k, ns, f, ops[0], set(x for o in ops for x in o[1]), set(x for o in ops for x in o[2])))
 
         if t == 0:
             job(1, 60, lambda: cp(T.LK[:, 0:16], T.lai[:], r=["lai"], w=["LK0"]))
@@ -393,24 +418,25 @@ def rank_program(g, core, T, topo):
                                            A.add, r=["ABa%d" % h, "ABb%d" % h], w=["E%d" % h]))
             job(1, 160, lambda: op("v", [(lambda j=j: v.tensor_copy(T.LK[:, 16 * j:16 * j + 16], T.LK[:, 0:16])) for j in (1, 2, 3)],
                                    r=["LK0"], w=["LK"]))
-            for a in range(192, 256, 16):
-                job(1, 380, lambda a=a: cp(ZG[1][:, 16 * a:16 * a + 256], OB[0][:, :].indirect(T.Lz[:, a:a + 16]),
-                                           r=["OB0", "OBz", "Lz"], w=["ZG1v"]))
+            for a in range(192, 256, 8):
+                late.append((1, 220, lambda a=a: cp(ZG[1][:, 16 * a:16 * a + 128], OB[0][:, :].indirect(T.Lz[:, a:a + 8]),
+                                                    r=["OB0", "OBz", "Lz"], w=["ZGv%d" % a])))
         if not last:
             for h in ((0, 1) if t == 0 else (1,)):
-                job(1, 380, lambda h=h: factors(h))
+                job(1, 110, lambda h=h: factors(h, 0))
+                job(1, 215, lambda h=h: factors(h, 1))
         else:
             job(1, 215, lambda: tt(T.t0[:, 0:128], T.nxf[:, 128:256], T.nxf[:, 0:128], A.subtract, r=["nxf"], w=["t0"]))
             job(1, 215, lambda: tt(T.t0[:, 0:128], T.t0[:, 0:128], T.S[:, :], A.mult, r=["t0", "S0", "S1"], w=["t0"]))
             job(1, 215, lambda: tt(T.YN[:, 0:128], T.nxf[:, 0:128], T.t0[:, 0:128], A.add, r=["nxf", "t0"], w=["YNa"]))
-            job(1, 215, lambda: tt(T.YN[:, 128:256], T.nxf[:, 128:256], T.t0[:, 0:128], A.subtract, r=["nxf", "t0"], w=["YNb"]))
-            job(1, 0, lambda: dma("y", T.yn[:], T.YN[:], r=["YNa", "YNb"]))
+            job(1, 215, lambda: (tt(T.YN[:, 128:256], T.nxf[:, 128:256], T.t0[:, 0:128], A.subtract, r=["nxf", "t0", "YNa"], w=["YNb"]),
+                                 dma("y", T.yn[:], T.YN[:], r=["YNa", "YNb"])))
         if t == 1:
             job(1, 60, lambda: labels(T.Lo[:, :], 256, 16, "Lo"))
         if t in (1, 2):
             zk = "ZG%d" % ((t + 1) % 2)
-            for a in (0, 8):
-                job(2, 400, lambda a=a, zk=zk: cp(ZG[(t + 1) % 2][:, :].indirect(T.Lo[:, a:a + 8]), OB[t][:, 16 * a:16 * a + 128],
+            for a in (0, 4, 8, 12):
+                job(1, 230, lambda a=a, zk=zk: cp(ZG[(t + 1) % 2][:, :].indirect(T.Lo[:, a:a + 4]), OB[t][:, 16 * a:16 * a + 64],
                                                   r=["Lo", "OB%d" % t], w=[zk, zk + "v"]))
         coff = [0]
 
@@ -419,27 +445,27 @@ def rank_program(g, core, T, topo):
             a, b = 16 * (k0 - 1), 16 * k1
             wd = b - a
             raw = T.SC[:, 256 * k0 + 15:256 * (k1 + 1):16]
-            sk = ["SC%d" % k for k in range(k0, k1 + 1)]
+            sk = ["SC%d" % k for k in range(k0, k1 + 1)] + ["SD%d" % k for k in range(k0 - 1, k1 + 1)]
             k = k1 + 1
             qa, tq = TS[:, 128:128 + wd], TS[:, 192:192 + wd]
             job(k1, 60, lambda: ts(qa, T.Q[:, a + 16:b + 16], nadj, None, A.add,
-                                   r=["Q%d" % (j + 1) for j in range(k0, k1 + 1)] + ["nadj"], w=["QA"], b=["pm1"]))
+                                   r=[x % (j + 1) for j in range(k0, k1 + 1) for x in ("Q%d", "QB%d")] + ["nadj"], w=["QA"], b=["pm1"]))
             job(k1, 60, lambda: ts(tq, raw, float(V - TB), None, A.add, r=sk, w=["TT"], b=["pm1"]))
             job(k1, 60, lambda: tt(T.DE[:, a:b], raw, qa, A.subtract, r=sk + ["QA"], w=["DE%d" % p], b=["pm1"]))
             job(k1, 60, lambda: tt(T.DF[:, a:b], T.SC[:, 256 * (k0 - 1) + 15:256 * k1:16], tq, A.max,
                                    r=sk + ["SC%d" % (k0 - 1), "TT"], w=["DF%d" % p], b=["pm1"]))
-            job(k1, 110, lambda: ts(T.DI[:, a:b], T.DF[:, a:b], adj, None, A.add, r=["DF%d" % p, "adj"], w=["DI%d" % p]))
+            job(k1, 60, lambda: ts(T.DI[:, a:b], T.DF[:, a:b], adj, None, A.add, r=["DF%d" % p, "adj"], w=["DI%d" % p]))
             job(k, 60, lambda: tt(T.VC[:, a:b], T.DE[:, a:b], T.pc[:, a:b], A.mult, r=["DE%d" % p, "pc%d" % p], w=["VC%d" % p], b=["pc"]))
             for j in range(k0, k1 + 1):
-                job(k, 110, lambda j=j: tt(TS[:, 256 + 16 * j:272 + 16 * j], TS[:, 240 + 16 * j:256 + 16 * j], T.VC[:, 16 * j - 16:16 * j],
+                job(k, 60, lambda j=j: tt(TS[:, 256 + 16 * j:272 + 16 * j], TS[:, 240 + 16 * j:256 + 16 * j], T.VC[:, 16 * j - 16:16 * j],
                                            A.add, r=["T%d" % (j - 1), "VC%d" % p], w=["T%d" % j], b=["pm1"]))
             tk = ["T%d" % j for j in range(k1 + 1)]
-            job(k, 110, lambda: tt(T.U[:, a:b], TS[:, 272 + a:272 + b], T.LK[:, 0:wd], A.subtract, r=tk + ["LK", "LK0"],
+            job(k, 60, lambda: tt(T.U[:, a:b], TS[:, 272 + a:272 + b], T.LK[:, 0:wd], A.subtract, r=tk + ["LK", "LK0"],
                                    w=["U%d" % p], b=["pm1"]))
             ds = list(range(1, k1 + 1))
-            for x in range(0, k1, 4):
+            for x in range(0, k1, CG):
                 grp = []
-                for d in ds[x:x + 4]:
+                for d in ds[x:x + CG]:
                     lo = max(k0, d)
                     grp.append((d, lo, 16 * (k1 + 1 - lo), coff[0]))
                     coff[0] += 16 * (k1 + 1 - lo)
@@ -453,80 +479,122 @@ def rank_program(g, core, T, topo):
                     lst += [(T.pn[:, 16 * (lo - 1):b], T.ID[:, :], T.CM[:, o:o + w_], False, d == k1) for d, lo, w_, o in grp]
                     mm(lst, r=[key, "ID", "OKK"], w=["pn%d" % p], b=["pn"])
                 job(k, 55 * len(grp), cmpj)
-            job(k + FLAG[p], 60, lambda: cp(T.FI[:, a:b], T.pn[:, a:b], r=["pn%d" % p], w=["FI%d" % p], b=["pn"]))
+            job(k, 60, lambda: cp(T.FI[:, a:b], T.pn[:, a:b], r=["pn%d" % p], w=["FI%d" % p], b=["pn"]))
 
         def fetch(j, e):
             a, b, p = MOVES[j]
             k1 = PARTS[p][1]
             gk = ["G%ds0" % t, "G%ds1" % t] + ["G%dp%d" % (t, k) for k in range(1, k1)]
-            e(T.NEW[:, 16 * a:16 * b], G[t][:, 0:256 * (k1 + 1)].indirect(T.FI[:, a:b]), r=gk + ["FI%d" % p], w=["NEW%d" % j])
+            e(T.NEW[:, 16 * a:16 * b], G[t][:, 0:256 * (k1 + 1)].indirect(T.FI[:, a:b]), r=gk + ["FI%d" % p], w=["NEW%d" % j],
+              ns=60 + 21 * (b - a))
+            if probe[0] is None:
+                todo.discard("NEW%d" % j)
 
-        def store(j0, j1):
-            a, b = MOVES[j0][0], MOVES[j1 - 1][1]
-            cp(T.X[:, :].indirect(T.DI[:, a:b]), T.NEW[:, 16 * a:16 * b],
-               r=["NEW%d" % j for j in range(j0, j1)] + ["DI%d" % MOVES[j][2] for j in range(j0, j1)], w=XK)
+        def store(j, a, b):
+            cp(T.X[:, :].indirect(T.DI[:, a:b]), T.NEW[:, 16 * a:16 * b], r=["NEW%d" % j, "DI%d" % MOVES[j][2]], w=XK,
+               ns=50 + SCAT * (b - a))
 
         for p in range(len(PARTS)):
-            part[0] = p
             feet(p)
             if p == 0 and t >= 2:
                 job(PARTS[0][1] + 3, 110, lambda: labels(T.Ly[:, 120 * (t - 2):120 * (t - 1)], 256, 120, "Ly%d" % (t - 2)))
             for j in range(NV):
                 if FETCH[j][0] == p:
-                    job(FETCH[j][1], 390, lambda j=j: fetch(j, cp))
+                    job(FETCH[j][1], 220, lambda j=j: fetch(j, cp))
+        for x in late:
+            job(*x)
 
-        def flush(p, k=99):
-            for x in [x for x in side if x[3] <= p and x[0] <= k]:
-                side.remove(x)
-                x[2]()
+        def ready(k):
+            out, rs, ws = [], set(), set()
+            for x in side:
+                if x[0] <= k and not (x[4] & todo) and not (x[4] & ws) and not (x[5] & (rs | ws)):
+                    out.append((deps(x[3][0], x[3][1], x[3][2], x[3][3], True), x))
+                rs |= x[4]
+                ws |= x[5]
+            return out
 
-        def drain(k, ns):
-            j = 0
-            while j < len(side) and ns > 0:
-                if side[j][0] <= k and side[j][1] <= ns + 40:
-                    x = side.pop(j)
-                    ns -= x[1]
-                    x[2]()
-                elif side[j][0] <= k:
+        def run(x):
+            side.remove(x)
+            cost[0] = x[1]
+            x[2]()
+            cost[0] = 60.0
+
+        def drain(k, until):
+            while True:
+                fit = [c for c in ready(k) if c[0] + c[1][1] <= until + SLACK]
+                if not fit:
                     return
-                else:
-                    j += 1
+                now = [c for c in fit if c[0] <= clk["v"] + 1]
+                run(now[0][1] if now else min(fit, key=lambda c: c[0])[1])
 
+        t00 = max(clk.values())
+        for e in clk:
+            clk[e] = t00
+        clk["t"] = t00 + (0 if t == 0 else 500)
         for k in range(1, 16):
-            ql = T.Q[:, 16 * (k - 1):16 * k]
-            act(T.GW[:, :], T.NL[:, 0:XW].indirect(ql), r=NK + ["tail0", "Q%d" % k], w=["GW"])
-            act(G[t][:, 256 * (k + 1):256 * (k + 2)], T.X[:, :].indirect(ql), r=XK + ["Q%d" % k], w=["G%dp%d" % (t, k)])
-            op("v", lambda k=k: v.tensor_tensor_scan(T.SC[:, 256 * k:256 * k + 256], T.M[:, :], T.GW[:, :], 0.0, A.add, A.min),
-               r=["M", "GW"], w=["SC%d" % k])
-            ts(T.Q[:, 16 * k:16 * k + 16], T.SC[:, 256 * k + 15:256 * k + 256:16], adj, None, A.add,
-               r=["SC%d" % k, "adj"], w=["Q%d" % (k + 1)])
+            for u in range(2):
+                act(T.GW[:, 128 * u:128 * u + 128], T.NL[:, 0:XW].indirect(T.Q[:, 16 * k - 16 + 8 * u:16 * k - 8 + 8 * u]),
+                    r=NK + ["tail0", ("Q%d", "QB%d")[u] % k], w=["GW%d" % u], ns=230)
+            act(G[t][:, 256 * (k + 1):256 * (k + 2)], T.X[:, :].indirect(T.Q[:, 16 * (k - 1):16 * k]),
+                r=XK + ["Q%d" % k, "QB%d" % k], w=["G%dp%d" % (t, k)], ns=400)
+            todo.discard("G%dp%d" % (t, k))
+            for u in range(2):
+                sc, qk, o = ("SC%d", "SD%d")[u] % k, ("Q%d", "QB%d")[u] % (k + 1), 256 * k + 128 * u
+                drain(k - 1, deps("v", ["GW%d" % u], [sc], (), True))
+                op("v", lambda o=o, u=u: v.tensor_tensor_scan(T.SC[:, o:o + 128], T.M[:, 0:128], T.GW[:, 128 * u:128 * u + 128],
+                                                               0.0, A.add, A.min), r=["M", "GW%d" % u], w=[sc], ns=110)
+                drain(k - 1, clk["v"] + LAT - SLACK + SL2[u])
+                ts(T.Q[:, 16 * k + 8 * u:16 * k + 8 * u + 8], T.SC[:, o + 15:o + 128:16], adj, None, A.add, r=[sc, "adj"], w=[qk])
+                todo.discard(sc)
+                todo.discard(qk)
             for p, (k0, k1) in enumerate(PARTS):
                 if k == k1:
                     mm([(T.pc[:, 16 * (k0 - 1):16 * k1], T.Bp[:, 15 - i:143 - i], G[t][:, 256 * (k0 + 1) + i:256 * (k1 + 2):16],
                          i == 0, i == 15) for i in range(16)],
                        r=["Bp"] + ["G%dp%d" % (t, j) for j in range(k0, k1 + 1)], w=["pc%d" % p], b=["pc"])
-            if k < 15:
-                drain(k, BUDGET)
-        np_ = len(PARTS) - 1
-        flush(np_ - 2)
-        for j in range(NV, len(MOVES) - 2):
-            fetch(j, act)
-        flush(np_, 15)
-        store(0, NV)
-        flush(np_ - 1)
-        fetch(len(MOVES) - 2, act)
-        flush(np_, 16)
-        store(NV, NV + 1)
-        flush(np_)
-        fetch(len(MOVES) - 1, act)
+                    todo.discard("pc%d" % p)
+        nf, ns_, at = [NV], [0], [0]
+
+        def fetches():
+            left = set(y for x in side for y in x[5])
+            while nf[0] < len(MOVES) and "FI%d" % MOVES[nf[0]][2] not in left:
+                fetch(nf[0], act)
+                nf[0] += 1
+                if t == 0 and nf[0] == len(MOVES) - 1:
+                    silu(1)
+
+        def piece(wd):
+            j = ns_[0]
+            b = min(MOVES[j][1], at[0] + wd)
+            store(j, at[0], b)
+            at[0] = b
+            if b == MOVES[j][1]:
+                ns_[0] += 1
+
+        while side:
+            fetches()
+            rdy = ready(99)
+            best = min(rdy, key=lambda c: c[0])
+            now = [c for c in rdy if c[0] <= clk["v"] + 1]
+            j = ns_[0]
+            left = set(y for x in side for y in x[5])
+            if now:
+                run(now[0][1])
+            elif (j < nf[0] and "NEW%d" % j not in todo and "DI%d" % MOVES[j][2] not in left
+                  and deps("v", ["NEW%d" % j, "DI%d" % MOVES[j][2]], XK, (), True) <= best[0]):
+                piece(PIECE)
+            else:
+                run(best[1])
+        fetches()
         if not last:
             z = (t + 1) % 2
-            content(ZG[z], T.Bz, 0, True, False, ["ZG%d" % z, "ZG%dv" % z, "Bz"])
-            content(ZG[z], T.Bz, 1, True, False, ["ZG%d" % z, "ZG%dv" % z, "Bz"])
+            zs = ["ZG%d" % z, "ZG%dv" % z, "Bz"] + ["ZGv%d" % a for a in range(192, 256, 8)]
+            content(ZG[z], T.Bz, 0, True, False, zs)
+            content(ZG[z], T.Bz, 1, True, False, zs)
         if t == 0:
-            silu(1)
-        for j in range(NV + 1, len(MOVES)):
-            store(j, j + 1)
+            silu(2)
+        while ns_[0] < len(MOVES):
+            piece(256)
 
     dma("y", T.y[:, V:W], T.X[:, V:W], r=["Xo"])
     for j in range(len(FINV) - 1):

@@ -3,58 +3,175 @@ from concourse.mybir import AluOpType as A, ActivationFunctionType as F
 R = 4
 V = 4096
 W = 4352
-ST = 272
-TB = 8464
-XW = 12256
-PARTS = [(1, 3), (4, 7), (8, 11), (12, 15)]
-LAT, MM, SCAT, SLACK, PIECE = 150, 45, 45, 80, 12
-SL2 = (20, 20)
-BUDGET = 500
-SILU = [0, 48, 144, 256]
-FINV = [0, 56, 96, 120]
-MOVES = [(0, 8, 0), (8, 16, 0), (16, 48, 0), (48, 112, 1), (112, 176, 2), (176, 240, 3)]
-NV = 2
-FETCH = [(0, 1), (0, 1)]
-CG = 3
-OPT = ("CO0", "CO1", "ZG0v")
+ST = 256
+XW = V + 15 * ST
+ZW = 280
+PARTS = [(1, 2), (3, 5), (6, 8), (9, 12), (13, 15)]
+TPE = (1, 1, 1, 1, 1, 1)
+HALVES = 9
+VCOL = 1
+CG = 4
+PRE0 = 2
+SQA, SY, MAGIC = True, True, 1.5 * 2.0 ** 23
+NX0 = (64, 64, 64, 32)
+NXV = (32, 32, 32, 32)
+YQ = ("y", "s", "y", "s")
+LAT, CY, PE, GA, SCA, MINP = 140, 0.92, 0.66, 1.37, 2.9, 170
+DFIX, DBW, RFIX, RFIRST = 1000.0, 230.0, 1300.0, 2500.0
+TOL = {"v": 60, "s": 60, "t": 60, "g": 600, "y": 60, "a": 0}
+TWALK = {"v": 150, "s": 250}
+TFEET = {"v": 250, "s": 300, "t": 100}
+TLAST = {"v": 250, "s": 100, "t": 60}
+CAP = {"fetc": 900}
+UPF, NUP, NUPF, LEUP = 3e4, 3, 0, 4e5
+BOOST, AHEAD, DEPTH, MANY, EXTRA = 3000.0, 0, 6, 12, 300.0
 
 SCRATCH = {
-    "X": ("sbuf", [128, XW], "bfloat16"), "XR": ("sbuf", [128, 4368], "bfloat16"),
-    "NL": ("sbuf", [128, 12288], "float32"), "ZG0": ("sbuf", [128, V], "bfloat16"), "ZG1": ("sbuf", [128, V], "bfloat16"),
+    "X": ("sbuf", [128, XW], "bfloat16"), "XO": ("sbuf", [128, W + V], "bfloat16"), "G": ("sbuf", [128, W], "bfloat16"),
+    "NL": ("sbuf", [128, XW], "float32"), "ZG": ("sbuf", [128, V], "bfloat16"),
     "SC": ("sbuf", [128, 4096], "float32"), "GW": ("sbuf", [128, 256], "float32"),
     "NEW": ("sbuf", [128, 3840], "bfloat16"), "SUM": ("sbuf", [128, 2048], "float32"),
-    "FM": ("sbuf", [128, 2048], "bfloat16"), "PV": ("sbuf", [128, W], "float32"),
-    "SB": ("sbuf", [128, ST], "bfloat16"), "ZB": ("sbuf", [128, ST], "bfloat16"),
+    "SB": ("sbuf", [128, ZW], "bfloat16"), "ZB": ("sbuf", [128, ZW], "bfloat16"),
+    "KN": ("sbuf", [128, 512], "bfloat16"), "KO": ("sbuf", [128, 512], "bfloat16"), "ZK": ("sbuf", [128, 512], "float32"),
     "nxi": ("sbuf", [128, 256], "int32"), "lei": ("sbuf", [128, 512], "int32"), "voi": ("sbuf", [128, 256], "int32"),
-    "lai": ("sbuf", [128, 16], "int32"), "nui": ("sbuf", [128, 4], "int32"),
+    "lai": ("sbuf", [128, 96], "int32"), "nui": ("sbuf", [128, 4], "int32"),
     "IP": ("sbuf", [128, 4], "int32"), "IQ": ("sbuf", [128, 4], "int32"), "col": ("sbuf", [128, 16], "float32"),
-    "IX": ("sbuf", [128, 144], "float32"), "J": ("sbuf", [128, 256], "float32"), "OKi": ("sbuf", [128, 64], "float32"),
-    "R1": ("sbuf", [128, 512], "bfloat16"), "LB": ("sbuf", [128, 256], "bfloat16"), "ZR": ("sbuf", [128, 128], "bfloat16"),
-    "BO": ("sbuf", [128, 128], "bfloat16"), "RM": ("sbuf", [128, 16], "float32"), "ID": ("sbuf", [128, 128], "bfloat16"),
-    "Bf": ("sbuf", [128, 144], "float32"), "Bw": ("sbuf", [128, 144], "bfloat16"), "Bp": ("sbuf", [128, 144], "bfloat16"),
-    "Bz": ("sbuf", [128, 144], "bfloat16"), "M": ("sbuf", [128, 256], "float32"), "OKK": ("sbuf", [128, 64], "bfloat16"),
-    "OL": ("sbuf", [128, 16], "float32"), "LK": ("sbuf", [128, 64], "float32"),
-    "t0": ("sbuf", [128, 256], "float32"), "t1": ("sbuf", [128, 256], "float32"), "t2": ("sbuf", [128, 256], "float32"),
-    "t3": ("sbuf", [128, 256], "float32"), "i0": ("sbuf", [128, 256], "int32"), "i1": ("sbuf", [128, 256], "int32"),
-    "i2": ("sbuf", [128, 256], "int32"), "nxf": ("sbuf", [128, 256], "float32"),
-    "Lx": ("sbuf", [128, 256], "uint16"), "Lz": ("sbuf", [128, 256], "uint16"), "Lp": ("sbuf", [128, 256], "uint16"),
-    "Ln": ("sbuf", [128, 256], "uint16"), "Ly": ("sbuf", [128, 240], "uint16"), "Lo": ("sbuf", [128, 16], "uint16"),
-    "Q": ("sbuf", [128, 256], "uint16"), "FI": ("sbuf", [128, 240], "uint16"), "DI": ("sbuf", [128, 240], "uint16"),
-    "DL": ("sbuf", [128, 256], "bfloat16"), "AB": ("sbuf", [128, 256], "float32"), "E": ("sbuf", [128, 128], "float32"),
-    "CO": ("sbuf", [128, 256], "float32"), "S": ("sbuf", [128, 128], "bfloat16"), "SE": ("sbuf", [128, 128], "float32"),
-    "TM": ("sbuf", [128, 256], "float32"), "U2": ("sbuf", [128, 128], "float32"), "q0": ("sbuf", [128, 16], "float32"),
-    "QA": ("sbuf", [128, 240], "float32"), "TT": ("sbuf", [128, 240], "float32"),
+    "IX": ("sbuf", [128, 144], "float32"), "J": ("sbuf", [128, 128], "float32"), "K8": ("sbuf", [128, 128], "float32"),
+    "RM": ("sbuf", [128, 16], "float32"), "IDf": ("sbuf", [128, 128], "float32"), "ID": ("sbuf", [128, 128], "bfloat16"),
+    "ZR": ("sbuf", [128, 128], "bfloat16"), "BO": ("sbuf", [128, 128], "bfloat16"), "FM": ("sbuf", [128, 1024], "bfloat16"),
+    "OKK": ("sbuf", [128, 512], "bfloat16"), "WL": ("sbuf", [128, 144], "bfloat16"), "WH": ("sbuf", [128, 144], "bfloat16"),
+    "DU": ("sbuf", [128, 256], "float32"), "UN": ("sbuf", [128, 256], "bfloat16"),
+    "Bf": ("sbuf", [128, 152], "float32"), "B2": ("sbuf", [128, 144], "float32"), "Bw": ("sbuf", [128, 144], "bfloat16"),
+    "Bz": ("sbuf", [128, 144], "bfloat16"), "Bp": ("sbuf", [128, 144], "bfloat16"), "M": ("sbuf", [128, 256], "float32"),
+    "LK": ("sbuf", [128, 96], "float32"), "t0": ("sbuf", [128, 256], "float32"), "t1": ("sbuf", [128, 256], "float32"),
+    "t4": ("sbuf", [128, 64], "float32"), "i0": ("sbuf", [128, 256], "int32"), "i1": ("sbuf", [128, 256], "int32"),
+    "LP": ("sbuf", [128, 1280], "bfloat16"), "PC": ("sbuf", [128, 1024], "bfloat16"),
+    "Lx": ("sbuf", [128, 256], "uint16"), "Lz": ("sbuf", [128, 256], "uint16"),
+    "Q": ("sbuf", [128, 256], "uint16"), "FI": ("sbuf", [128, 240], "uint16"),
+    "H": ("sbuf", [128, 256], "float32"), "E": ("sbuf", [128, 256], "float32"), "F0": ("sbuf", [128, 256], "float32"),
+    "F1": ("sbuf", [128, 256], "float32"), "D": ("sbuf", [128, 256], "bfloat16"), "XD": ("sbuf", [128, 1024], "bfloat16"),
+    "TM": ("sbuf", [128, 256], "float32"), "RI": ("sbuf", [128, 240], "float32"),
     "DE": ("sbuf", [128, 240], "float32"), "VC": ("sbuf", [128, 240], "float32"), "U": ("sbuf", [128, 240], "float32"),
-    "CM": ("sbuf", [128, 1920], "bfloat16"), "DF": ("sbuf", [128, 240], "float32"), "YN": ("sbuf", [128, 256], "float32"),
+    "CM": ("sbuf", [128, 1920], "bfloat16"), "YN": ("sbuf", [128, 256], "float32"),
     "pp0": ("psum", [128, 512], "float32"), "pp1": ("psum", [128, 512], "float32"), "pp2": ("psum", [128, 512], "float32"),
     "pp3": ("psum", [128, 512], "float32"), "pm0": ("psum", [128, 512], "float32"), "pm1": ("psum", [128, 512], "float32"),
-    "pc": ("psum", [128, 512], "float32"), "pn": ("psum", [128, 512], "float32"),
+    "pc": ("psum", [128, 512], "float32"), "ps": ("psum", [128, 512], "float32"),
 }
 for _t in range(R):
-    SCRATCH["G%d" % _t] = ("sbuf", [128, W], "bfloat16")
-    SCRATCH["OB%d" % _t] = ("sbuf", [128, ST], "bfloat16")
-NDMA = 40
-SEMAPHORES = ["cv", "cs", "ct", "cg", "zarr", "sent"] + ["arr%d" % t for t in range(R)] + ["d%d" % k for k in range(NDMA)]
+    SCRATCH["AR%d" % _t] = ("sbuf", [128, 256], "bfloat16")
+NDMA = 56
+SEMAPHORES = (["cv", "cs", "ct", "cg", "zarr"] + ["arr%d" % t for t in range(R)] + ["sent%d" % t for t in range(R + 1)]
+              + ["d%d" % k for k in range(NDMA)])
+ORDER = []
+
+
+def order(ops):
+    n = len(ops)
+    succ = [[] for _ in ops]
+    for i, o in enumerate(ops):
+        for p in o["pre"]:
+            succ[p].append(i)
+    pri = [0.0] * n
+    for i in range(n - 1, -1, -1):
+        o = ops[i]
+        pri[i] = ((1.0 if o["range"] else o["lat"]) + o["up"]
+                  + max([pri[j] + (LAT if ops[j]["pre"][i] and ops[j]["stream"] != o["stream"] else 0) for j in succ[i]] + [0.0]))
+    pri = [x + o["rank"] for x, o in zip(pri, ops)]
+    pri0, ahead = list(pri), [0]
+    kind = [str(o["stream"])[:4] for o in ops]
+    left = [len(o["pre"]) for o in ops]
+    fin = [None] * n
+    free = {e: 0.0 for e in "vstgya"}
+    bank = {}
+    ready = set(i for i in range(n) if left[i] == 0)
+    out = []
+    dfree = 0.0
+
+    def start(i, est=None):
+        o = ops[i]
+        t = free[o["e"]]
+        for p, hard in o["pre"].items():
+            f = fin[p] if fin[p] is not None else est[p]
+            if hard is not None:
+                t = max(t, f + (LAT if hard else 0))
+        for k in o["b"]:
+            for e2, j in bank.get(k, {}).items():
+                if e2 != o["e"]:
+                    t = max(t, fin[j] + LAT)
+        return t
+
+    def done(i, t):
+        fin[i] = t
+        ready.discard(i)
+        for j in succ[i]:
+            left[j] -= 1
+            if left[j] == 0:
+                ready.add(j)
+
+    while ready:
+        st = {i: start(i) for i in ready}
+        i0 = min(st, key=lambda i: (st[i], -pri[i]))
+        e, now = ops[i0]["e"], st[i0]
+        est = {i: st[i] + ops[i]["lat"] + ops[i]["fix"] for i in ready}
+        front = list(ready)
+        for i in ready:
+            if kind[i] == "fetc":
+                pri[i] = pri0[i] + (BOOST if ahead[0] < AHEAD else 0.0)
+        for _ in range(DEPTH):
+            nxt = []
+            for i in front:
+                for j in succ[i]:
+                    if j not in est and all(fin[p] is not None or p in est for p in ops[j]["pre"]):
+                        st[j] = start(j, est)
+                        est[j] = st[j] + ops[j]["lat"] + ops[j]["fix"]
+                        nxt.append(j)
+            front = nxt
+        mine = [i for i in st if ops[i]["e"] == e]
+        can = sorted([i for i in mine if i in ready and st[i] <= now + 1], key=lambda i: (-pri[i], i))
+        pick = None
+        for i in can:
+            lim = min([st[j] + ops[j]["tol"] for j in mine
+                       if pri[j] > pri[i] and st[j] > now + 1 and ops[j]["stream"] != ops[i]["stream"]] + [1e18])
+            o = ops[i]
+            if kind[i] == "stor" and ahead[0] >= MANY:
+                lim += EXTRA
+            need = o["fix"] + max(o["ns"], MINP if o["range"] else 0)
+            if now + need <= lim:
+                pick = (i, lim)
+                break
+        if pick is None:
+            free[e] = min(st[j] for j in mine if st[j] > now + 1)
+            continue
+        i, lim = pick
+        o = ops[i]
+        grp, t = [i], now + o["fix"] + o["ns"]
+        pre = dict(o["pre"])
+        while o["range"]:
+            j = grp[-1] + 1
+            if j >= n or ops[j]["stream"] != o["stream"] or fin[j] is not None or t + ops[j]["ns"] > min(lim, now + o["cap"]):
+                break
+            if any(p not in grp and (fin[p] is None or fin[p] + (LAT if h else 0) > now + 1) for p, h in ops[j]["pre"].items()):
+                break
+            grp.append(j)
+            t += ops[j]["ns"]
+            for p, h in ops[j]["pre"].items():
+                if p not in grp:
+                    pre[p] = pre.get(p, False) or h
+        for k in o["b"]:
+            for e2, j in bank.get(k, {}).items():
+                if e2 != e:
+                    pre[j] = True
+            bank.setdefault(k, {})[e] = grp[-1]
+        free[e] = t
+        ahead[0] += len(grp) * {"fetc": 1, "stor": -1}.get(kind[i], 0)
+        end = t + o["lat"] - o["ns"]
+        if o["kind"] == "d":
+            dfree = max(dfree, now + 0.6 * DFIX) + o["lat"] - DFIX
+            end = dfree + 0.4 * DFIX
+        for j in grp:
+            done(j, end)
+        out.append((grp, pre))
+    return out
 
 
 def rank_program(g, core, T, topo):
@@ -63,83 +180,47 @@ def rank_program(g, core, T, topo):
         return
     n = len(T.cores)
     nxt, prv = T.cores[(rank + 1) % n], T.cores[(rank - 1) % n]
-    Q = {"v": g.vector, "s": g.scalar, "t": g.tensor, "g": g, "y": g.sync}
-    cnt = {"v": 0, "s": 0, "t": 0, "g": 0}
-    waited = {e: {} for e in Q}
-    wr, rd, bank, total = {}, {}, {}, {}
-    nd = [0]
+    v, s, pe = g.vector, g.scalar, g.tensor
+    Q = {"v": v, "s": s, "t": pe, "g": g, "y": g.sync}
+    ops, wr, rd = [], {}, {}
+    tol, lastg, rank_ = [TOL], [None], [0.0]
 
-    def wait(e, tok):
-        if waited[e].get(tok[0], 0) < tok[1]:
-            Q[e].wait_ge(T.sem[tok[0]], tok[1])
-            waited[e][tok[0]] = tok[1]
+    def put(e, kind, fn, r, w, b, ns, lat=None, fix=0.0, stream=None, rng=None, sem=None, up=0.0):
+        i = len(ops)
+        pre = {}
 
-    clk = {e: 0.0 for e in Q}
-    fin = {}
-    probe = [None]
-    cost = [60.0]
-
-    def deps(e, r, w, b, dry=False):
-        need = {}
-        own = "c" + e
-
-        def add(tok):
-            need[tok[0]] = max(need.get(tok[0], 0), tok[1])
+        def add(p):
+            pre[p] = not (e == "t" and ops[p]["e"] == "t")
         for k in r:
-            assert k in wr or k in OPT, k
-            if k in wr and not (e == "t" and wr[k][0] == own):
-                add(wr[k])
+            assert k in wr, k
+            add(wr[k])
         for k in w:
-            if k in wr and not (e == "t" and wr[k][0] == own):
+            if k in wr:
                 add(wr[k])
-            for s, v in rd.get(k, {}).items():
-                if not (e == "t" and s == own):
-                    add((s, v))
-        for k in b:
-            for s, v in bank.get(k, {}).items():
-                if s != own:
-                    add((s, v))
-        st = clk[e]
-        for s in need:
-            if waited[e].get(s, 0) < need[s]:
-                st = max(st, fin.get((s, need[s]), -LAT) + LAT)
-            if not dry:
-                wait(e, (s, need[s]))
-        return st
-
-    def mark(tok, r, w, b):
-        total[tok[0]] = tok[1]
+            for p in rd.get(k, []):
+                add(p)
         for k in r:
-            rd.setdefault(k, {})[tok[0]] = tok[1]
+            rd.setdefault(k, []).append(i)
         for k in w:
-            wr[k] = tok
-            rd[k] = {}
-        for k in b:
-            bank.setdefault(k, {})[tok[0]] = tok[1]
+            wr[k] = i
+            rd[k] = []
+        ops.append({"e": e, "kind": kind, "fn": fn, "pre": pre, "b": list(b), "ns": ns, "lat": ns if lat is None else lat,
+                    "fix": fix, "stream": stream or i, "range": rng, "sem": sem, "up": up, "rank": rank_[0],
+                    "tol": tol[0][e], "cap": CAP.get((stream or "")[:4], 1e9)})
+        if e == "g":
+            if lastg[0] is not None:
+                pre.setdefault(lastg[0], None)
+            lastg[0] = i
 
-    def op(e, fns, r=(), w=(), b=(), ns=None):
-        if probe[0] is not None:
-            probe[0].append((e, list(r), list(w), list(b)))
-            return
-        clk[e] = deps(e, r, w, b) + (cost[0] if ns is None else ns)
-        fin[("c" + e, cnt[e] + 1)] = clk[e]
-        if not isinstance(fns, list):
-            fns = [fns]
-        ins = None
-        for f in fns:
-            ins = f()
-        cnt[e] += 1
-        ins.then_inc(T.sem["c" + e], 1)
-        mark(("c" + e, cnt[e]), r, w, b)
+    def op(e, fns, r=(), w=(), b=(), ns=60.0, up=0.0):
+        put(e, "c", fns if isinstance(fns, list) else [fns], r, w, b, ns, up=up)
 
-    def dma(e, out, in_, r=(), w=()):
-        if probe[0] is not None:
-            return
-        deps(e, r, w, ())
-        s = "d%d" % nd[0]
-        nd[0] += 1
-        Q[e].dma_start(out, in_).then_inc(T.sem[s], 16)
-        mark((s, 16), r, w, ())
+    def stream(e, name, fn, a, b, unit, el, r, w):
+        for c in range(a, b, unit):
+            put(e, "c", fn, r(c), w(c), (), 16 * unit * el, None, 60.0, name, (c, c + unit))
+
+    def dma(out, in_, r=(), w=(), up=0.0, size=2, e="y"):
+        put(e, "d", lambda: Q[e].dma_start(out, in_), r, w, (), 60.0, DFIX + 128 * out.shape[1] * size / DBW, up=up)
 
     def lanes(src, dst):
         es = topo.engines(src, dst)[::2]
@@ -148,459 +229,437 @@ def rank_program(g, core, T, topo):
             m |= 1 << x
         return m, len(es)
 
-    nsent = [0]
-
-    def send(dst, out, in_, sem, r):
-        deps("g", r, (), ())
+    def send(dst, out, in_, sem, sent, r, first=0.0):
         m, k = lanes(core, dst)
         rid, pid, _ = topo.addr(dst)
-        g.remote_dma(out, in_, T.sem[sem], T.sem.sent, pid, rid, m)
-        nsent[0] += k
-        total["sent"] = nsent[0]
+        put("g", "r", lambda: g.remote_dma(out, in_, T.sem[sem], T.sem[sent], pid, rid, m), r, [sent], (), 300.0 + first,
+            RFIX + first, sem=(sent, k))
 
-    v, s, pe = g.vector, g.scalar, g.tensor
+    def arrive(src, sem, sent, key):
+        put("a", "a", None, [sent], [key], (), 0.0, sem=(sem, lanes(src, core)[1]))
 
-    def ts(out, in0, s1, s2, o0, o1=None, **k):
+    def cyc(a, two=1):
+        return max(64, a.shape[1] * two) * CY
+
+    def ts(out, in0, s1, s2, o0, o1=None, two=1, **k):
         if o1 is None:
-            op("v", lambda: v.tensor_scalar(out, in0, s1, None, o0), **k)
+            op("v", lambda: v.tensor_scalar(out, in0, s1, None, o0), ns=cyc(out, two), **k)
         else:
-            op("v", lambda: v.tensor_scalar(out, in0, s1, s2, o0, o1), **k)
+            op("v", lambda: v.tensor_scalar(out, in0, s1, s2, o0, o1), ns=cyc(out, two), **k)
 
-    def tt(out, a, b_, o, **k):
-        op("v", lambda: v.tensor_tensor(out, a, b_, o), **k)
+    def tt(out, a, b_, o, two=1, **k):
+        op("v", lambda: v.tensor_tensor(out, a, b_, o), ns=cyc(out, two), **k)
 
     def cp(out, a, **k):
-        op("v", lambda: v.tensor_copy(out, a), **k)
+        op("v", lambda: v.tensor_copy(out, a), ns=cyc(out), **k)
 
     def ms(out, c, **k):
-        op("v", lambda: v.memset(out, c), **k)
+        op("v", lambda: v.memset(out, c), ns=cyc(out, 0.5), **k)
 
-    def act(out, a, bias=None, **k):
-        if bias is not None:
-            op("s", lambda: s.activation(out, a, F.Identity, bias=bias), **k)
-        else:
-            op("s", lambda: s.activation(out, a, F.Copy), **k)
+    def act(out, a, **k):
+        op("s", lambda: s.activation(out, a, F.Copy), ns=cyc(out), **k)
 
-    def mm(lst, **k):
-        op("t", [(lambda a=a: pe.matmul(*a)) for a in lst], ns=MM * len(lst), **k)
+    def move(e, out, a):
+        return v.tensor_copy(out, a) if e == "v" else s.activation(out, a, F.Copy)
+
+    def gather(e, out, a, **k):
+        op(e, lambda: move(e, out, a), ns=60 + GA * out.shape[1], **k)
+
+    def mm(lst, f32=1, **k):
+        k["w"] = list(k["w"]) + ["group " + k["b"][0]]
+        op("t", [(lambda a=a: pe.matmul(*a)) for a in lst], ns=sum(PE * f32 * max(64, a[0].shape[1]) for a in lst), **k)
 
     def iota(out, pat, base, cm, key, flt=True):
-        wait("g", ("cg", cnt["g"]))
+        ns = 130 + 2 * CY * out.shape[1]
         if flt:
-            op("g", lambda: g.iota(out, pat, base, cm, allow_small_or_imprecise_dtypes=True), w=[key])
+            op("g", lambda: g.iota(out, pat, base, cm, allow_small_or_imprecise_dtypes=True), w=[key], ns=ns)
         else:
-            op("g", lambda: g.iota(out, pat, base, cm), w=[key])
+            op("g", lambda: g.iota(out, pat, base, cm), w=[key], ns=ns)
 
-    G = [T["G%d" % t] for t in range(R)]
-    OB = [T["OB%d" % t] for t in range(R)]
-    ZG = [T.ZG0, T.ZG1]
+    X, G, XO, NL, ZG = T.X, T.G, T.XO, T.NL, T.ZG
+    AR = [T["AR%d" % t] for t in range(R)]
     pp = [T.pp0, T.pp1, T.pp2, T.pp3]
-    pm = [T.pm0, T.pm1]
-    XK = ["Xh", "Xo", "Xg1", "Xg2"]
-    PK = ["P0%d" % b for b in range(4)] + ["P1%d" % b for b in range(4)]
-    NK = ["NLa", "NLb", "tail"] + PK
-    cb = [8.0 * (b % 2) + 1024.0 * (b // 2) for b in range(4)]
-    pf, pi, pi1, pg, adj, nadj, wf = [T.col[:, k:k + 1] for k in range(7)]
-    TS = T.pm1
+    pa, pn, ps, pc = T.pm0, T.pm1, T.ps, T.pc
+    BK, BN = [pa[:, 0:128], pn[:, 0:128], pa[:, 128:256], pn[:, 128:256]], ["pm0", "pm1", "pm0", "pm1"]
+    XK = ["Xa", "Xb", "Xi"]
+    XN = ["XN%d" % c for c in range(0, 256, 8)]
+    PK = ["P0%d" % b for b in range(4)] + ["P1%d" % b for b in range(4)] + ["tail"]
+    pf, pi, pi1, pg, adj, wf, lo, hi, p8, k8, k88, r8, pm8 = [T.col[:, k:k + 1] for k in range(13)]
+    nadj = T.col[:, 13:14]
+    NP = len(PARTS)
+    NMAX = max(k1 - k0 + 1 for k0, k1 in PARTS)
+    AK, NK = ["pc%d" % p for p in range(NP)], ["pn%d" % p for p in range(NP)]
+    MK = [["m0"] + AK, ["m1"] + NK, ["m2"] + AK, ["m3"] + NK]
+    TK = ["T%d" % j for j in range(16)]
 
-    dma("y", T.nxi[:], T.nx[:], w=["nxi"])
-    dma("s", T.XR[:, 0:2176], T.x[:, 0:2176], w=["XRa"])
-    dma("y", T.SB[:, 0:256], T.x[:, 0:256], w=["SBa"])
-    dma("y", T.nui[:, 0:1], T.nu[:], w=["nui"])
-    dma("y", T.XR[:, 2176:W], T.x[:, 2176:W], w=["XRb"])
-    dma("s", T.voi[:], T.vol[:], w=["voi"])
-    dma("y", OB[0][:, 0:256], T.x[:, V:W], w=["OB0"])
-    dma("y", T.lei[:], T.le[:], w=["lei"])
-    dma("y", T.lai[:], T.lag[:], w=["lai"])
+    def repeat(buf, width, key, size):
+        a = 16
+        while a < width:
+            b = min(2 * a, width)
+            dma(buf[:, a:b], buf[:, 0:b - a], r=[key], w=[key], size=size)
+            a = b
+
+    dma(T.nui[:, 0:1], T.nu[:, :], w=["nui"], up=9e5)
+    dma(T.SB[:, 16:272], T.x[:, 0:256], w=["SBa"], up=8e5)
+    dma(T.nxi[:, :], T.nx[:, :], w=["nxi"], up=7e5, size=4)
+    dma(T.voi[:, :], T.vol[:, :], w=["voi"], size=4, up=6e5)
+    dma(X[:, 256:2304], T.x[:, 256:2304], w=["Xa"], up=5e5)
+    dma(X[:, 2304:W], T.x[:, 2304:W], w=["Xb"], up=5e5)
+    dma(T.lei[:, :], T.le[:, :], w=["lei"], size=4, up=LEUP)
+    dma(X[:, 0:256], T.x[:, 0:256], w=["Xi"], up=5e5)
+    for j in range(NMAX):
+        dma(T.lai[:, 16 * j:16 * j + 16], T.lag[:, :], w=["lai%d" % j], size=4)
+    dma(G[:, 256:512], T.x[:, 0:256], w=["G1"])
+    dma(XO[:, 0:W], T.x[:, :], w=["XO"])
     iota(T.IP[:, 0:1], [[1, 1]], 0, 1, "IP", False)
-    iota(T.IX[:], [[1, 144]], 0, 0, "IX")
-    iota(T.J[:], [[0, 16], [1, 16]], 0, 0, "J")
-    iota(T.OKi[:], [[0, 4], [16, 16]], 0, 0, "OKi")
-    iota(T.NL[:, 8192:8960], [[1, 768]], 8192 + ST, 0, "tail0")
-    ms(T.SB[:, 256:ST], 0.0, w=["SBb"])
-    ms(T.XR[:, W:4368], 0.0, w=["XRz"])
-    ms(T.LB[:, 0:128], 1.0 / 32, w=["LB"])
-    ms(T.LB[:, 128:256], 1.0 / 16, w=["LB2"])
-    ms(T.ZR[:], 0.0, w=["ZR"])
-    ms(OB[0][:, 256:ST], 0.0, w=["OBz"])
-    ms(TS[:, 256:272], 0.0, w=["T0"], b=["pm1"])
-    ms(T.S[:], 0.0, w=["S0", "S1"])
+    iota(T.IX[:, :], [[1, 144]], 0, 0, "IX")
+    iota(T.J[:, :], [[16, 8], [0, 16]], 0, 0, "J")
+    ms(T.SB[:, 0:16], 0.0, w=["SBb"])
+    ms(T.SB[:, 272:ZW], 0.0, w=["SBd"])
+    ms(T.ZR[:, :], 0.0, w=["ZR"])
+    ms(T.Bf[:, 0:8], 0.0, w=["Bf0"])
     ts(T.IQ[:, 0:1], T.IP[:, 0:1], 15, None, A.bitwise_and, r=["IP"], w=["IQ"])
+    ts(T.IQ[:, 1:2], T.IP[:, 0:1], 7, None, A.bitwise_and, r=["IP"], w=["IQ8"])
     cp(pf, T.IP[:, 0:1], r=["IP"], w=["pf"])
     cp(pi, T.IQ[:, 0:1], r=["IQ"], w=["pi"])
+    cp(r8, T.IQ[:, 1:2], r=["IQ8"], w=["r8"])
     tt(pg, pf, pi, A.subtract, r=["pf", "pi"], w=["pg"])
     ts(pi1, pi, 1.0, None, A.add, r=["pi"], w=["pi1"])
     ts(adj, pi, 15.0, 16384.0, A.is_lt, A.mult, r=["pi"], w=["adj"])
     ts(nadj, pi, 15.0, -16384.0, A.is_lt, A.mult, r=["pi"], w=["nadj"])
-    ts(T.RM[:], T.J[:, 0:16], pi, -2048.0, A.is_equal, A.mult, r=["J", "pi"], w=["RM"])
-    tt(T.t0[:, 0:128], T.IX[:, 0:128], T.J[:, 0:128], A.subtract, r=["IX", "J"], w=["t0"])
-    ts(T.Bf[:], T.IX[:], -15.0, pg, A.add, A.is_equal, r=["IX", "pg"], w=["Bf"])
-    ts(T.BO[:], T.t0[:, 0:128], pg, None, A.is_equal, r=["t0", "pg"], w=["BO"])
-    ts(T.ID[:], T.IX[:, 0:128], pf, 256.0, A.is_equal, A.mult, r=["IX", "pf"], w=["ID"])
-    ts(T.t2[:], T.J[:], pi, 32768.0, A.is_equal, A.mult, r=["J", "pi"], w=["t2"])
-    ts(T.t3[:], T.J[:], pi1, -16384.0, A.is_equal, A.mult, r=["J", "pi1"], w=["t3"])
-    tt(T.M[:], T.t2[:], T.t3[:], A.add, r=["t2", "t3"], w=["M"])
-    op("s", [(lambda i=i: s.activation(T.FM[:, 128 * i:128 * i + 128], T.BO[:], F.Identity, scale=T.RM[:, i:i + 1]))
-             for i in range(16)], r=["BO", "RM"], w=["FM"])
-    op("v", [(lambda j=j: v.memset(T.R1[0:32, 64 * j:64 * j + 64], float(j))) for j in range(8)], w=["R1a"])
-    op("v", [(lambda j=j: v.tensor_scalar(T.R1[32:64, 64 * j:64 * j + 64], T.IX[32:64, 0:64], 16.0, None, A.mult)) for j in range(8)],
-       r=["IX"], w=["R1b"])
-    ts(T.OL[:], T.OKi[:, 0:16], pi, None, A.add, r=["OKi", "pi"], w=["OL"])
-    ts(T.OKK[:], T.OKi[:], pi, 1.0 / 256, A.add, A.mult, r=["OKi", "pi"], w=["OKK"])
-    cp(T.Ln[:], T.nxi[:], r=["nxi"], w=["Ln"])
-    ts(T.pc[:, 0:256], T.nxi[:], float(V), None, A.is_ge, r=["nxi"], w=["c0"], b=["pc"])
-    cp(T.nxf[:], T.nxi[:], r=["nxi"], w=["nxf"])
-    cp(T.SB[:, 257:258], T.nui[:, 0:1], r=["nui", "SBb"], w=["SBc"])
-    send(prv, T.ZB[:], T.SB[:], "zarr", ["SBa", "SBb", "SBc"])
-    wr["ZB"] = ("zarr", lanes(nxt, core)[1])
-    total["zarr"] = wr["ZB"][1]
-
-    def silu(j):
-        a, b = SILU[j], SILU[j + 1]
-        op("s", lambda: s.activation(T.PV[:, :].indirect(T.Ln[:, a:b]), T.NL[:, 8192 + 16 * a:8192 + 16 * b], F.Silu),
-           r=["Ln", ("tail0", "tail", "tail")[j]], w=["PV"])
-
-    silu(0)
-    tt(T.t0[:, 0:128], T.voi[:, 0:128], T.voi[:, 128:256], A.add, r=["voi"], w=["t0"])
-    ts(T.pc[:, 256:512], T.pc[:, 0:256], float(W), None, A.mult, r=["c0"], w=["c1"], b=["pc"])
-    ts(T.DL[:, 0:128], T.t0[:, 0:128], -2.0 ** -20, None, A.mult, r=["t0"], w=["DLS"])
-    tt(T.t3[:], T.pc[:, 256:512], T.nxf[:], A.max, r=["c1", "nxf"], w=["t3"], b=["pc"])
-    tt(T.t2[:], T.pc[:, 0:256], T.nxf[:], A.mult, r=["c0", "nxf"], w=["t2"], b=["pc"])
-    cp(T.Lx[:], T.t3[:], r=["t3"], w=["Lx"])
-    ts(T.pc[:, 256:512], T.pc[:, 0:256], -float(W), 256.0, A.mult, A.add, r=["c0"], w=["c1"], b=["pc"])
-    ts(T.DL[:, 128:256], T.voi[:, 128:256], -2.0 ** -20, None, A.mult, r=["voi"], w=["DL1"])
-    tt(T.t1[:], T.pc[:, 256:512], T.t2[:], A.add, r=["c1", "t2"], w=["t1"], b=["pc"])
+    ts(lo, pi, 8.0, None, A.is_lt, r=["pi"], w=["lo"])
+    ts(hi, pi, 8.0, None, A.is_ge, r=["pi"], w=["hi"])
+    ts(p8, pf, 8.0, None, A.add, r=["pf"], w=["p8"])
+    ts(pm8, pf, -8.0, None, A.add, r=["pf"], w=["pm8"])
+    tt(k8, pg, r8, A.add, r=["pg", "r8"], w=["k8"])
+    ts(k88, k8, 8.0, None, A.add, r=["k8"], w=["k88"])
+    ts(T.RM[:, 0:8], T.IX[:, 0:8], r8, -1.0, A.is_equal, A.mult, r=["IX", "r8"], w=["RM"])
+    ts(T.BO[:, :], T.J[:, :], pg, None, A.is_equal, r=["J", "pg"], w=["BO"])
+    for q in range(2):
+        op("s", [(lambda i=i: s.activation(T.FM[:, 128 * i:128 * i + 128], T.BO[:, :], F.Identity, scale=T.RM[:, i:i + 1]))
+                 for i in range(4 * q, 4 * q + 4)], r=["BO", "RM"], w=["FM%d" % q], ns=4 * 128 * CY)
+    FK = ["FM0", "FM1"]
+    ts(T.WL[:, :], T.IX[:, :], p8, lo, A.is_equal, A.mult, r=["IX", "p8", "lo"], w=["WL"])
+    ts(T.WH[:, :], T.IX[:, :], p8, hi, A.is_equal, A.mult, r=["IX", "p8", "hi"], w=["WH"])
+    ts(T.Bf[:, 8:152], T.IX[:, :], -15.0, pg, A.add, A.is_equal, r=["IX", "pg"], w=["Bf"])
+    tt(T.B2[:, :], T.Bf[:, 8:152], T.Bf[:, 0:144], A.add, 2, r=["Bf", "Bf0"], w=["B2"])
+    ts(T.ID[:, :], T.IX[:, 0:128], pf, 256.0, A.is_equal, A.mult, r=["IX", "pf"], w=["ID"])
+    ts(T.IDf[:, :], T.IX[:, 0:128], pf, None, A.is_equal, r=["IX", "pf"], w=["IDf"])
+    ts(T.UN[:, 0:128], T.IX[:, 0:128], k8, 0.5, A.is_equal, A.mult, r=["IX", "k8"], w=["UN0"])
+    ts(T.UN[:, 128:256], T.IX[:, 0:128], k88, 0.5, A.is_equal, A.mult, r=["IX", "k88"], w=["UN1"])
+    ts(T.t4[:, 0:16], T.IX[:, 0:16], pi, 32768.0, A.is_equal, A.mult, r=["IX", "pi"], w=["t4"])
+    ts(T.t4[:, 16:32], T.IX[:, 0:16], pi1, -16384.0, A.is_equal, A.mult, r=["IX", "pi1"], w=["t5"])
+    tt(T.M[:, 0:16], T.t4[:, 0:16], T.t4[:, 16:32], A.add, r=["t4", "t5"], w=["M"])
+    repeat(T.M, 256, "M", 4)
+    ts(T.t4[:, 32:48], T.IX[:, 0:16], 16.0, pi, A.mult, A.add, r=["IX", "pi"], w=["OL"])
+    ts(T.OKK[:, 0:16], T.t4[:, 32:48], 1.0 / 256, None, A.mult, r=["OL"], w=["OKK"])
+    repeat(T.OKK, 16 * NMAX, "OKK", 2)
+    cp(T.SB[:, 272:273], T.nui[:, 0:1], r=["nui", "SBd"], w=["SBc"])
+    send(prv, T.ZB[:, :], T.SB[:, :], "zarr", "sent%d" % R, ["SBa", "SBb", "SBc"], RFIRST)
+    arrive(nxt, "zarr", "sent%d" % R, "ZB")
+    iota(T.K8[:, :], [[16, 8], [0, 2], [1, 8]], 0, 0, "K8")
+    send(nxt, AR[0][:, :], X[:, V:W], "arr0", "sent0", ["Xb"])
+    arrive(prv, "arr0", "sent0", "AR0")
+    iota(NL[:, V:XW], [[1, XW - V]], V + ST, 0, "tail")
+    ts(T.DU[:, 0:128], T.K8[:, :], pf, 0.5, A.is_equal, A.mult, r=["K8", "pf"], w=["DU0"])
+    ts(T.DU[:, 128:256], T.K8[:, :], pm8, 0.5, A.is_equal, A.mult, r=["K8", "pm8"], w=["DU1"])
     cp(wf, T.nui[:, 0:1], r=["nui"], w=["wf"])
-    cp(T.Lz[:], T.t1[:], r=["t1"], w=["Lz"])
-    ts(T.Bw[:], T.Bf[:], wf, None, A.mult, r=["Bf", "wf"], w=["Bw"])
+    ts(T.Bw[:, :], T.B2[:, :], wf, None, A.mult, r=["B2", "wf"], w=["Bw"])
+    ts(T.Bz[:, :], T.B2[:, :], T.ZB[:, 272:273], None, A.mult, r=["B2", "ZB"], w=["Bz"])
+    ts(T.Bp[:, :], T.Bf[:, 8:152], wf, 512.0, A.mult, A.mult, r=["Bf", "wf"], w=["Bp"])
+    cp(T.LK[:, 0:16 * NMAX], T.lai[:, 0:16 * NMAX], r=["lai%d" % j for j in range(NMAX)], w=["LK"])
+    cp(T.Lx[:, :], T.nxi[:, :], r=["nxi"], w=["Lx"])
+    ts(T.Lz[:, :], T.nxi[:, :], 16.0 - V, 0.0, A.add, A.max, r=["nxi"], w=["Lz"])
+    LP, PC = T.LP, T.PC
+    rank_[0] = 2e4
+    ts(T.i0[:, :], T.nxi[:, :], 0x1FC0, None, A.bitwise_and, r=["nxi"], w=["i0"])
+    ts(T.i1[:, :], T.nxi[:, :], 63, None, A.bitwise_and, r=["nxi"], w=["i1"])
+    cp(LP[:, 0:256], T.i0[:, :], r=["i0"], w=["Lhi"])
+    cp(LP[:, 256:512], T.i1[:, :], r=["i1"], w=["Llo"])
+    ts(LP[:, 768:1024], T.voi[:, :], 1.0 / 512, None, A.mult, r=["voi"], w=["Lv"])
+    rank_[0] = 0.0
+    ts(LP[:, 512:640], LP[:, 0:128], -1.0, None, A.mult, two=0.5, r=["Lhi"], w=["Lnh"])
+    ts(LP[:, 640:768], LP[:, 256:384], -1.0, None, A.mult, two=0.5, r=["Llo"], w=["Lnl"])
+    ts(LP[:, 1024:1280], LP[:, 0:256], float(V), None, A.is_ge, two=0.5, r=["Lhi"], w=["Lk"])
+    up_ = [T.WL[:, 8:136], T.WH[:, 16:144]]
+    dn_ = [T.WL[:, 0:128], T.WH[:, 8:136]]
 
-    def spread(src, first, key):
-        for b in range(4):
-            lst = []
-            if first is not None:
-                lst.append((pp[b][:, :], first, T.R1[0:64, :], True, False))
-            for i8 in range(8):
-                i = 8 * (b % 2) + i8
-                lst.append((pp[b][:, 64 * i8:64 * i8 + 64], T.FM[:, 128 * i:128 * i + 128],
-                            src[:, 64 * (b // 2):64 * (b // 2) + 64], False, key != "DL1" and i8 == 7))
-            kk = key if first is not None else key + str(b // 2)
-            mm(lst, r=[kk, "FM", "LB", "LB2", "R1a", "R1b"], w=["pp%d" % b], b=["pp%d" % b])
+    def double(bank, o, terms, keys, key, name):
+        mm([(bank[:, o + u:o + 256:2], m[u], LP[:, c:c + 128], j == 0, j == len(terms) - 1)
+            for u in range(2) for j, (m, c) in enumerate(terms)], r=keys + ["WL", "WH"], w=key, b=[name])
 
-    spread(T.DL[:, 0:128], T.LB[0:64, 128:256], "DLS")
-    for b in range(4):
-        act(T.SUM[:, 512 * b:512 * b + 512], pp[b][:, :], bias=cb[b], r=["pp%d" % b], w=["SUM"], b=["pp%d" % b])
-    spread(T.DL[:, 128:256], T.LB[0:64, 0:128], "DL1")
+    hl = ["Lhi", "Llo"]
+    c0, c1, a0, n0 = ["s0", "s1"], ["x%d" % b for b in range(4)], ["m0", "m2"] + AK, ["m1", "m3"] + NK
+    EK = ["EP%d" % b for b in range(4)]
+    rank_[0] = 2e4
+    double(pc, 0, [(up_, 0), (up_, 128), (dn_, 256), (dn_, 384)], hl, c0, "pc")
+    double(pc, 256, [(up_, 768), (up_, 896)], ["Lv"], c1, "pc")
+    double(pa, 0, [(up_, 128), (dn_, 384)], hl, a0, "pm0")
+    double(pa, 256, [(up_, 896)], ["Lv"], ["a1"], "pm0")
+    op("s", lambda: s.activation(PC[:, 0:512], pc[:, :], F.Identity, scale=-1.0), r=c0 + c1, w=["PC0"], b=["pc"], ns=512 * CY)
+    op("s", lambda: s.activation(PC[:, 512:1024], pa[:, :], F.Identity, scale=-1.0), r=a0 + ["a1"], w=["PC1"], b=["pm0"], ns=512 * CY)
+    rank_[0] = 0.0
+    double(pn, 0, [(up_, 128), (dn_, 384), (up_, 512), (dn_, 640)], hl + ["Lnh", "Lnl"], n0, "pm1")
+    double(ps, 0, [(up_, 1024), (dn_, 1024)], ["Lk"], TK, "ps")
+    double(ps, 256, [(up_, 1152), (dn_, 1152)], ["Lk"], EK, "ps")
+    act(T.D[:, :], pn[:, 0:256], r=n0, w=["D%d" % b for b in range(4)], b=["pm1"])
+    op("s", lambda: s.activation(T.KN[:, :], ps[:, :], F.Identity, scale=-1.0, bias=1.0), r=TK + EK, w=["KN"], b=["ps"], ns=512 * CY)
+    op("s", lambda: s.activation(T.KO[:, :], T.KN[:, :], F.Identity, scale=-1.0, bias=1.0), r=["KN"], w=["KO"], ns=512 * CY)
 
-    for h in range(2):
-        op("v", [(lambda c=c: v.tensor_copy(T.X[:, 16 * c:16 * c + 1024], T.XR[:, :].indirect(T.Lx[:, c:c + 64])))
-                 for c in (64 * h, 128 + 64 * h)], r=["XRa", "XRb", "XRz", "Lx"], w=[("Xi", "Xh")[h]])
-        op("s", [(lambda c=c: s.activation(ZG[0][:, 16 * c:16 * c + 1024], T.ZB[:, :].indirect(T.Lz[:, c:c + 64]), F.Copy))
-                 for c in (64 * h, 128 + 64 * h)], r=["ZB", "Lz"], w=[("ZGi", "ZG0")[h]])
-        if h == 0:
-            ts(T.Bz[:], T.Bf[:], T.ZB[:, 257:258], None, A.mult, r=["Bf", "ZB"], w=["Bz"])
-    act(ZG[1][:, 0:2048], OB[0][:, :].indirect(T.Lz[:, 0:128]), r=["OB0", "OBz", "Lz"], w=["ZG1"])
-    send(nxt, G[0][:, 0:256], OB[0][:, 0:256], "arr0", ["OB0"])
-    iota(T.NL[:, 8960:12288], [[1, 3328]], 8960 + ST, 0, "tail")
-    dma("y", T.X[:, V:W], T.x[:, V:W], w=["Xo"])
-    dma("y", G[0][:, 256:512], T.x[:, 0:256], w=["G0s1"])
-    dma("y", T.X[:, W:2 * W], T.x[:, :], w=["Xg1"])
-    dma("y", T.X[:, 2 * W:XW], T.x[:, 0:XW - 2 * W], w=["Xg2"])
-
-    def content(src, lhs, h, first, last, keys):
+    def spread(b, srcs, keys, how):
         lst = []
-        if first:
-            lst.append((pm[h][:, 0:128], T.ZR[:, :], T.ZR[:, :], True, False))
-        for i in range(16):
-            for a in range(2):
-                o = 2048 * a + 1024 * h
-                lst.append((pm[h][:, 64 * a:64 * a + 64], lhs[:, 15 - i:143 - i], src[:, o + i:o + 1024:16], False,
-                            last and i == 15 and a == 1))
-        mm(lst, r=keys + ["ZR"], w=["pm%d" % h], b=["pm%d" % h])
-
-    content(T.X, T.Bw, 0, True, False, ["Xi", "Bw"])
-    content(ZG[0], T.Bz, 0, False, True, ["ZGi", "Bz"])
-    content(T.X, T.Bw, 1, True, False, ["Xh", "Bw"])
-    content(ZG[0], T.Bz, 1, False, True, ["ZG0", "Bz"])
-    for h in range(2):
-        c = 64 * h
-        tt(T.AB[:, 128 * h:128 * h + 64], T.lei[:, 256 + c:320 + c], T.lei[:, c:64 + c], A.subtract, r=["lei"], w=["ABa%d" % h])
-        tt(T.AB[:, 128 * h + 64:128 * h + 128], T.lei[:, 128 + c:192 + c], T.lei[:, 384 + c:448 + c], A.subtract, r=["lei"], w=["ABb%d" % h])
-    def positions():
-        ts(T.i1[:], T.nxi[:], 15, None, A.bitwise_and, r=["nxi"], w=["i1"])
-        ts(T.i0[:], T.nxi[:], 0xC00, None, A.bitwise_and, r=["nxi"], w=["i0"])
-        ts(T.pn[:, 0:256], T.i1[:], 64.0, None, A.mult, r=["i1"], w=["n0"], b=["pn"])
-        ts(T.i2[:], T.nxi[:], 4, 63, A.logical_shift_right, A.bitwise_and, r=["nxi"], w=["i2"])
-        tt(T.pn[:, 256:512], T.pn[:, 0:256], T.i0[:], A.add, r=["n0", "i0"], w=["n1"], b=["pn"])
-        ts(T.Bp[:], T.Bf[:], wf, 512.0, A.mult, A.mult, r=["Bf", "wf"], w=["Bp"])
-        tt(T.pn[:, 0:256], T.pn[:, 256:512], T.i2[:], A.add, r=["n1", "i2"], w=["n0"], b=["pn"])
-        tt(T.t1[:], T.pn[:, 0:256], T.t2[:], A.max, r=["n0", "t2"], w=["t1"], b=["pn"])
-        cp(T.Lp[:], T.t1[:], r=["t1"], w=["Lp"])
-
-    positions()
-
-    def back(a, b, o):
-        lst = [(T.pm0[:, o:o + b - a], T.Bf[:, 15 - i:143 - i], T.PV[:, 16 * a + i:16 * b:16], i == 0, i == 15) for i in range(16)]
-        mm(lst, r=["PV", "Bf"], w=["bk"], b=["pm0"])
-
-    def factors(h, only=None):
-        c = 64 * h
-        if only != 1:
-            tt(T.SE[:, c:c + 64], T.S[:, c:c + 64], T.E[:, c:c + 64], A.mult, r=["S%d" % h, "E%d" % h], w=["SE%d" % h])
-        if only == 0:
+        if how == "open":
+            mm([(pp[b][:, :], T.ZR[:, :], T.FM[:, 0:512], True, False)], r=FK + ["ZR"], w=["pp%d" % b], b=["pp%d" % b])
+            for src in srcs:
+                spread(b, [src], keys, "more")
             return
-        op("v", [(lambda q=q: v.tensor_tensor(T.CO[:, 64 * q:64 * q + 64], T.AB[:, 64 * q:64 * q + 64], T.SE[:, c:c + 64], A.subtract))
-                 for q in (2 * h, 2 * h + 1)], r=["SE%d" % h], w=["CO%d" % h])
+        for r in range(8):
+            for j, src in enumerate(srcs):
+                lst.append((pp[b][:, r:512:8], T.FM[:, 128 * r:128 * r + 128], src[:, 64 * b:64 * b + 64], how == "whole" and j == 0,
+                            j == len(srcs) - 1 and (how == "whole" or how == "close" and r == 7)))
+        mm(lst, r=keys + FK + ["ZR"], w=["pp%d" % b], b=["pp%d" % b])
 
-    def labels(out, o, k, key):
-        ts(out, T.pm0[:, o:o + k], 1.0 / 16, 0.25 - TB, A.mult, A.add, r=["bk"], w=[key], b=["pm0"])
+    def before(b, t):
+        spread(b, [PC[:, 512:768], PC[:, 768:1024]] + [T.XD[:, 256 * j:256 * j + 256] for j in range(t)],
+               ["PC1"] + ["XD%d_%d" % (j, b) for j in range(t)], "open")
+
+    rank_[0] = 1e4
+    for b in range(4):
+        spread(b, [PC[:, 0:256], PC[:, 256:512]], ["PC0"], "whole")
+        act(T.SUM[:, 512 * b:512 * b + 512], pp[b][:, :], r=["pp%d" % b], w=["SUM%d" % b], b=["pp%d" % b], up=2e4)
+        if b < PRE0:
+            before(b, 0)
+    rank_[0] = 0.0
+    tt(T.t0[:, 0:128], T.lei[:, 256:384], T.lei[:, 0:128], A.subtract, 2, r=["lei"], w=["al"])
+    tt(T.t0[:, 128:256], T.lei[:, 128:256], T.lei[:, 384:512], A.subtract, 2, r=["lei"], w=["be"])
+    tt(T.t1[:, 0:128], T.t0[:, 0:128], T.t0[:, 128:256], A.add, 2, r=["al", "be"], w=["t1a"])
+    tt(T.t1[:, 128:256], T.t0[:, 0:128], T.t0[:, 128:256], A.subtract, 2, r=["al", "be"], w=["t1b"])
+    mm([(ps[:, 256 * a + u:256 * a + 256:2], T.DU[:, 128 * u:128 * u + 128], T.t1[:, 128 * a:128 * a + 128], True, True)
+        for a in range(2) for u in range(2)], 4, r=["t1a", "t1b", "DU0", "DU1"], w=TK + EK, b=["ps"])
+    act(T.H[:, :], ps[:, 0:256], r=["T0"], w=["H"], b=["ps"])
+
+    def factors(b):
+        c = 64 * b
+        ep = ps[:, 256 + c:320 + c]
+        op("v", [lambda: v.tensor_tensor(T.F0[:, c:c + 64], T.H[:, c:c + 64], ep, A.add),
+                 lambda: v.tensor_tensor(T.F1[:, c:c + 64], ep, T.H[:, c:c + 64], A.subtract)],
+           r=["H", "EP%d" % b], w=["F%d" % b], b=["ps"], ns=120)
+
+    for b in range(4):
+        factors(b)
+
+    def content(src, o, lhs, b, key, keys, out, w, bank):
+        mm([(out[:, 64 * a:64 * a + 64], lhs[:, 15 - r:143 - r], src[:, o + 2048 * a + 512 * b + r:o + 2048 * a + 512 * b + 512:8],
+             r == 0, r == 7) for a in range(2) for r in range(8)],
+           r=keys + [key % (c + x) for c in (32 * b, 128 + 32 * b) for x in range(0, 32, 8)], w=w, b=[bank])
+
+    def sides(out, in0, in1, o, q, **k):
+        op("v", [(lambda a=a: v.tensor_tensor(out[:, 64 * a:64 * a + 64], in0[:, 256 * a + 64 * q:256 * a + 64 * q + 64],
+                                              in1[:, 64 * a:64 * a + 64], o)) for a in range(2)], ns=120, **k)
+
+    for b in range(4):
+        for c in (32 * b, 128 + 32 * b):
+            gather("s", ZG[:, 16 * c:16 * c + 512], T.ZB[:, 0:272].indirect(T.Lz[:, c:c + 32]), r=["ZB", "Lz"],
+                   w=["Z%d" % x for x in range(c, c + 32, 8)])
+        content(ZG, 0, T.Bz, b, "Z%d", ["Bz"], pa[:, 256 + 128 * (b % 2):384 + 128 * (b % 2)], ["a1", "z%d" % (b % 2)], "pm0")
+        act(T.ZK[:, 128 * b:128 * b + 128], pa[:, 256 + 128 * (b % 2):384 + 128 * (b % 2)], r=["z%d" % (b % 2)], w=["ZK%d" % b], b=["pm0"])
 
     for t in range(R):
         last = t == R - 1
-        wr["G%ds0" % t] = ("arr%d" % t, lanes(prv, core)[1])
-        total["arr%d" % t] = wr["G%ds0" % t][1]
-        co = T.AB if t == 0 else T.CO
         if t > 0:
-            dma("y", OB[t][:, 0:256], T.X[:, V:W], r=["Xo"], w=["OB%d" % t])
-            send(nxt, G[t][:, 0:256], OB[t][:, 0:256], "arr%d" % t, ["OB%d" % t])
-            content(T.X, T.Bw, 0, False, True, ["Xh", "Bw"])
-            content(T.X, T.Bw, 1, False, True, ["Xh", "Bw"])
+            send(nxt, AR[t][:, :], X[:, V:W], "arr%d" % t, "sent%d" % t, ["Xb"])
+            arrive(prv, "arr%d" % t, "sent%d" % t, "AR%d" % t)
+            dma(XO[:, 256:V], X[:, 256:V], r=XK, w=["XO"])
+            dma(G[:, 256:512], AR[t - 1][:, :], r=["AR%d" % (t - 1)], w=["G1"])
+        dma(G[:, 0:256], AR[t][:, :], r=["AR%d" % t], w=["G0"])
         if last:
-            dma("y", T.y[:, 0:256], G[t][:, 0:256], r=["G%ds0" % t])
-        else:
-            dma("y", G[t + 1][:, 256:512], G[t][:, 0:256], r=["G%ds0" % t], w=["G%ds1" % (t + 1)])
-        for h in range(2):
-            a = 128 * h
-            tt(T.TM[:, a:a + 128], co[:, a:a + 128], pm[h][:, 0:128], A.mult,
-               r=["pm%d" % h, "ABa%d" % h, "ABb%d" % h, "CO%d" % h], w=["TM%d" % h], b=["pm%d" % h])
-            tt(T.U2[:, 64 * h:64 * h + 64], T.TM[:, a:a + 64], T.TM[:, a + 64:a + 128], A.add, r=["TM%d" % h], w=["U2%d" % h])
-            tt(T.S[:, 64 * h:64 * h + 64], T.U2[:, 64 * h:64 * h + 64], T.S[:, 64 * h:64 * h + 64], A.is_lt,
-               r=["U2%d" % h, "S%d" % h], w=["S%d" % h])
-            if h == 0:
-                ts(T.q0[:], T.S[:, 0:16], 2048.0, nadj, A.mult, A.add, r=["S0", "nadj"], w=["q0"])
-                tt(T.SC[:, 15:256:16], T.q0[:], T.OL[:], A.add, r=["q0", "OL"], w=["SC0", "SD0"])
-                ts(T.Q[:, 0:16], T.SC[:, 15:256:16], adj, None, A.add, r=["SC0", "adj"], w=["Q1", "QB1"])
-            if 0 < t < R - 1 and h == 0:
-                factors(0)
-            if t == 0 and h == 0:
-                cp(ZG[1][:, 2048:3072], OB[0][:, :].indirect(T.Lz[:, 128:192]), r=["OB0", "OBz", "Lz"], w=["ZG1v"])
-        spread(T.S, None, "S")
+            dma(T.y[:, 0:256], AR[t][:, :], r=["AR%d" % t])
         for b in range(4):
-            o = V + 512 * b
-            act(T.NL[:, o + 2048:o + 2560], pp[b][:, :], bias=cb[b] + 2048.0, r=["pp%d" % b], w=["P1%d" % b], b=["pp%d" % b])
-            b ^= 1
-            o = V + 512 * b
-            tt(T.NL[:, o:o + 512], T.SUM[:, 512 * b:512 * b + 512], pp[b][:, :], A.subtract,
-               r=["pp%d" % b, "SUM"], w=["P0%d" % b], b=["pp%d" % b])
-        cp(T.NL[:, 0:2048], T.NL[:, V:V + W].indirect(T.Lp[:, 0:128]), r=PK + ["tail0", "Lp"], w=["NLa"])
-        act(T.NL[:, 2048:V], T.NL[:, V:V + W].indirect(T.Lp[:, 128:256]), r=PK + ["tail0", "Lp"], w=["NLb"])
-        if t == 1:
-            back(256, 272, 256)
-        if not last:
-            spread(T.DL[:, 128:256], T.LB[0:64, 0:128], "DL1")
-        if t >= 2:
-            back(16 + 120 * (t - 2), 136 + 120 * (t - 2), 256)
-
-        side, late = [], []
-        todo = set(["pc%d" % p for p in range(len(PARTS))] + ["NEW%d" % j for j in range(len(MOVES))])
-        for k in range(1, 16):
-            todo.update(["SC%d" % k, "SD%d" % k, "Q%d" % (k + 1), "QB%d" % (k + 1), "G%dp%d" % (t, k)])
-
-        def job(k, ns, f):
-            probe[0] = []
-            f()
-            ops, probe[0] = probe[0], None
-            side.append((k, ns, f, ops[0], set(x for o in ops for x in o[1]), set(x for o in ops for x in o[2])))
-
+            h, u, c = b // 2, b % 2, 64 * b
+            cols = list(range(32 * b, 32 * b + 32, 8)) + list(range(128 + 32 * b, 160 + 32 * b, 8))
+            nv = (NX0[b] if t == 0 else NXV[b]) // 8
+            for e, cs in (("v", cols[:nv]), ("s", cols[nv:])):
+                for run in ([x for x in cs if x < 128], [x for x in cs if x >= 128]):
+                    if run:
+                        gather(e, XO[:, W + 16 * run[0]:W + 16 * run[-1] + 128], X[:, 0:W].indirect(T.Lx[:, run[0]:run[-1] + 8]),
+                               r=XK + ["Lx"], w=["XN%d" % x for x in run])
+            content(XO, W, T.Bw, b, "XN%d", ["Bw"], BK[b], MK[b], BN[b])
+            m, sk, x1 = pc[:, 128 * u:128 * u + 128], "s%d" % u, pc[:, 256 + c:320 + c]
+            sides(m, T.KN, BK[b], A.mult, b, r=["m%d" % b, "KN"], w=[sk], b=[BN[b], "pc"])
+            tt(m, T.ZK[:, 128 * b:128 * b + 128], m, A.add, r=[sk, "ZK%d" % b], w=[sk], b=["pc"])
+            op("v", [lambda c=c, m=m: v.tensor_tensor(T.TM[:, c:c + 64], T.F0[:, c:c + 64], m[:, 0:64], A.mult),
+                     lambda c=c, m=m: v.tensor_tensor(m[:, 64:128], T.F1[:, c:c + 64], m[:, 64:128], A.mult)],
+               r=[sk, "F%d" % b], w=["TM%d" % b, sk], b=["pc"], ns=120)
+            tt(x1, T.TM[:, c:c + 64], m[:, 64:128], A.is_lt, r=["TM%d" % b, sk], w=["x%d" % b], b=["pc"])
+            tt(T.XD[:, 256 * t + c:256 * t + c + 64], T.D[:, c:c + 64], x1, A.mult, r=["x%d" % b, "D%d" % b], w=["XD%d_%d" % (t, b)], b=["pc"])
+            if t == 0 and b >= PRE0:
+                spread(b, [PC[:, 512:768], PC[:, 768:1024], T.XD[:, 0:256]], ["PC1", "XD0_%d" % b], "whole")
+            else:
+                spread(b, [T.XD[:, 256 * t:256 * t + 256]], ["XD%d_%d" % (t, b)], "close")
+            o = 512 * b
+            act(NL[:, o + 2048:o + 2560], pp[b][:, :], r=["pp%d" % b], w=["P1%d" % b], b=["pp%d" % b])
+            tt(NL[:, o:o + 512], T.SUM[:, o:o + 512], pp[b][:, :], A.subtract, r=["pp%d" % b, "SUM%d" % b], w=["P0%d" % b], b=["pp%d" % b])
+        for b in range(4):
+            c = 64 * b
+            x1, ep, bn = pc[:, 256 + c:320 + c], ps[:, 256 + c:320 + c], "pc"
+            if t == 0:
+                act(T.E[:, c:c + 64], ep, r=["EP%d" % b], w=["E%d" % b], b=["ps"], up=5e4)
+            if SY:
+                op("s", lambda x1=x1: s.activation(x1, x1, F.Identity, bias=1.0, scale=-2.0), r=["x%d" % b], w=["x%d" % b], b=[bn])
+            else:
+                ts(x1, x1, -2.0, 1.0, A.mult, A.add, r=["x%d" % b], w=["x%d" % b], b=[bn])
+            tt(T.D[:, c:c + 64], T.D[:, c:c + 64], x1, A.mult, r=["x%d" % b, "D%d" % b], w=["D%d" % b], b=[bn])
+            if not last:
+                tt(ep, T.E[:, c:c + 64], x1, A.mult, r=["x%d" % b, "E%d" % b], w=["EP%d" % b], b=[bn, "ps"])
+                factors(b)
+                if t < R - 2:
+                    act(T.E[:, c:c + 64], ep, r=["EP%d" % b], w=["E%d" % b], b=["ps"], up=5e4)
+                before(b, t + 1)
+                z = pn[:, 256 + 128 * (b % 2):384 + 128 * (b % 2)]
+                content(XO, W, T.Bz, b, "XN%d", ["Bz"], z, ["z%d" % (b % 2)], "pm1")
+                sides(T.ZK[:, 128 * b:128 * b + 128], T.KO, z, A.mult, b, r=["z%d" % (b % 2), "KO"], w=["ZK%d" % b], b=["pm1"])
+        if last:
+            mm([(pn[:, 256:384], T.UN[:, 128 * u:128 * u + 128], T.D[:, u:256:2], u == 0, u == 1) for u in range(2)],
+               r=["UN0", "UN1"] + ["D%d" % b for b in range(4)], w=["z0"], b=["pm1"])
+            tt(T.t0[:, 0:128], T.nxi[:, 128:256], T.nxi[:, 0:128], A.add, 2, r=["nxi"], w=["al"])
+            ts(T.t0[:, 128:256], T.t0[:, 0:128], 0.5, None, A.mult, r=["al"], w=["be"])
+            tt(T.YN[:, 0:128], T.t0[:, 128:256], pn[:, 256:384], A.subtract, r=["be", "z0"], w=["YNa"], b=["pm1"])
+            tt(T.YN[:, 128:256], T.t0[:, 128:256], pn[:, 256:384], A.add, r=["be", "z0"], w=["YNb"], b=["pm1"])
+            dma(T.yn[:, :], T.YN[:, :], r=["YNa", "YNb"], size=4)
         if t == 0:
-            job(1, 60, lambda: cp(T.LK[:, 0:16], T.lai[:], r=["lai"], w=["LK0"]))
-            for h in range(2):
-                job(1, 110, lambda h=h: tt(T.E[:, 64 * h:64 * h + 64], T.AB[:, 128 * h:128 * h + 64], T.AB[:, 128 * h + 64:128 * h + 128],
-                                           A.add, r=["ABa%d" % h, "ABb%d" % h], w=["E%d" % h]))
-            job(1, 160, lambda: op("v", [(lambda j=j: v.tensor_copy(T.LK[:, 16 * j:16 * j + 16], T.LK[:, 0:16])) for j in (1, 2, 3)],
-                                   r=["LK0"], w=["LK"]))
-            for a in range(192, 256, 8):
-                late.append((1, 220, lambda a=a: cp(ZG[1][:, 16 * a:16 * a + 128], OB[0][:, :].indirect(T.Lz[:, a:a + 8]),
-                                                    r=["OB0", "OBz", "Lz"], w=["ZGv%d" % a])))
-        if not last:
-            for h in ((0, 1) if t == 0 else (1,)):
-                job(1, 110, lambda h=h: factors(h, 0))
-                job(1, 215, lambda h=h: factors(h, 1))
-        else:
-            job(1, 215, lambda: tt(T.t0[:, 0:128], T.nxf[:, 128:256], T.nxf[:, 0:128], A.subtract, r=["nxf"], w=["t0"]))
-            job(1, 215, lambda: tt(T.t0[:, 0:128], T.t0[:, 0:128], T.S[:, :], A.mult, r=["t0", "S0", "S1"], w=["t0"]))
-            job(1, 215, lambda: tt(T.YN[:, 0:128], T.nxf[:, 0:128], T.t0[:, 0:128], A.add, r=["nxf", "t0"], w=["YNa"]))
-            job(1, 215, lambda: (tt(T.YN[:, 128:256], T.nxf[:, 128:256], T.t0[:, 0:128], A.subtract, r=["nxf", "t0", "YNa"], w=["YNb"]),
-                                 dma("y", T.yn[:], T.YN[:], r=["YNa", "YNb"])))
-        if t == 1:
-            job(1, 60, lambda: labels(T.Lo[:, :], 256, 16, "Lo"))
-        if t in (1, 2):
-            zk = "ZG%d" % ((t + 1) % 2)
-            for a in (0, 4, 8, 12):
-                job(1, 230, lambda a=a, zk=zk: cp(ZG[(t + 1) % 2][:, :].indirect(T.Lo[:, a:a + 4]), OB[t][:, 16 * a:16 * a + 64],
-                                                  r=["Lo", "OB%d" % t], w=[zk, zk + "v"]))
-        coff = [0]
+            mm([(ps[:, 0:16], T.ZR[:, :], T.FM[:, 0:16], True, True)], r=["ZR"] + FK, w=["T0"], b=["ps"])
 
-        def feet(p):
-            k0, k1 = PARTS[p]
+        tol[0] = TWALK
+        for k in range(16):
+            for u, (a, b) in enumerate(((0, 8), (8, 16)) if 0 < k <= HALVES else ((0, 16),)):
+                nm = [("SC%d", "Q%d"), ("SD%d", "QB%d")]
+                nm = nm[u:u + 1] if 0 < k <= HALVES else nm
+                gk = ["GW%d" % x for x in range(a // 8, b // 8)]
+                src = T.GW[:, 16 * a:16 * b]
+                if k == 0:
+                    src, gk = NL[:, 0:256], ["P00"]
+                else:
+                    gather("s", src, NL[:, :].indirect(T.Q[:, 16 * k - 16 + a:16 * k - 16 + b]), r=PK + [x[1] % k for x in nm], w=gk)
+                o = 256 * k
+                op("v", lambda o=o, a=a, b=b, src=src: v.tensor_tensor_scan(T.SC[:, o + 16 * a:o + 16 * b], T.M[:, 16 * a:16 * b],
+                                                                             src, 0.0, A.add, A.min),
+                   r=["M"] + gk, w=[x[0] % k for x in nm], ns=16 * (b - a) * CY)
+                ts(T.Q[:, 16 * k + a:16 * k + b], T.SC[:, o + 16 * a + 15:o + 16 * b:16], adj, None, A.add,
+                   r=[x[0] % k for x in nm] + ["adj"], w=[x[1] % (k + 1) for x in nm])
+        tol[0] = TFEET
+        gather("s", G[:, 512:768], X[:, 0:W].indirect(T.Q[:, 0:16]), r=XK + ["Q1"], w=["Gp1"])
+        for e, a, b in (("v", 1, VCOL), ("s", VCOL, 15)):
+            stream(e, "col%s%d" % (e, t), lambda a, b, e=e: move(e, G[:, 512 + 16 * a:512 + 16 * b], XO[:, 0:XW].indirect(T.Q[:, a:b])),
+                   16 * a, 16 * b, 16, GA, lambda c: ["XO"] + XN + ["Q%d" % (c // 16 + 1), "QB%d" % (c // 16 + 1)],
+                   lambda c: ["Gp%d" % (c // 16 + 1)])
+        coff = 0
+        for p, (k0, k1) in enumerate(PARTS):
             a, b = 16 * (k0 - 1), 16 * k1
-            wd = b - a
+            wd, nk = b - a, k1 - k0 + 1
+            tol[0] = TLAST if p == NP - 1 else TFEET
+            rank_[0] = UPF if p < NUP else 0.0
             raw = T.SC[:, 256 * k0 + 15:256 * (k1 + 1):16]
-            sk = ["SC%d" % k for k in range(k0, k1 + 1)] + ["SD%d" % k for k in range(k0 - 1, k1 + 1)]
-            k = k1 + 1
-            qa, tq = TS[:, 128:128 + wd], TS[:, 192:192 + wd]
-            job(k1, 60, lambda: ts(qa, T.Q[:, a + 16:b + 16], nadj, None, A.add,
-                                   r=[x % (j + 1) for j in range(k0, k1 + 1) for x in ("Q%d", "QB%d")] + ["nadj"], w=["QA"], b=["pm1"]))
-            job(k1, 60, lambda: ts(tq, raw, float(V - TB), None, A.add, r=sk, w=["TT"], b=["pm1"]))
-            job(k1, 60, lambda: tt(T.DE[:, a:b], raw, qa, A.subtract, r=sk + ["QA"], w=["DE%d" % p], b=["pm1"]))
-            job(k1, 60, lambda: tt(T.DF[:, a:b], T.SC[:, 256 * (k0 - 1) + 15:256 * k1:16], tq, A.max,
-                                   r=sk + ["SC%d" % (k0 - 1), "TT"], w=["DF%d" % p], b=["pm1"]))
-            job(k1, 60, lambda: ts(T.DI[:, a:b], T.DF[:, a:b], adj, None, A.add, r=["DF%d" % p, "adj"], w=["DI%d" % p]))
-            job(k, 60, lambda: tt(T.VC[:, a:b], T.DE[:, a:b], T.pc[:, a:b], A.mult, r=["DE%d" % p, "pc%d" % p], w=["VC%d" % p], b=["pc"]))
-            for j in range(k0, k1 + 1):
-                job(k, 60, lambda j=j: tt(TS[:, 256 + 16 * j:272 + 16 * j], TS[:, 240 + 16 * j:256 + 16 * j], T.VC[:, 16 * j - 16:16 * j],
-                                           A.add, r=["T%d" % (j - 1), "VC%d" % p], w=["T%d" % j], b=["pm1"]))
+            sk = [x % k for k in range(k0, k1 + 1) for x in ("SC%d", "SD%d")]
+            qa, qk = pc[:, 128 * (p % 2):128 * (p % 2) + wd], ["s%d" % (p % 2)]
+            mm([(pa[:, a:b], T.Bp[:, 15 - i:143 - i], G[:, 256 * (k0 + 1) + i:256 * (k1 + 2):16], i == 0, i == 15)
+                for i in range(16)], r=["Bp"] + ["Gp%d" % j for j in range(k0, k1 + 1)], w=["pc%d" % p, "m0", "m2"], b=["pm0"])
+            if SQA:
+                op("s", lambda raw=raw, a=a, b=b: s.activation(T.RI[:, a:b], raw, F.Identity, bias=MAGIC), r=sk, w=["RI%d" % p], ns=cyc(qa))
+                op("s", lambda qa=qa, a=a, b=b: s.activation(qa, T.RI[:, a:b], F.Identity, bias=-MAGIC), r=["RI%d" % p], w=qk, b=["pc"],
+                   ns=cyc(qa))
+            else:
+                ts(qa, T.Q[:, a + 16:b + 16], nadj, None, A.add,
+                   r=[x % (j + 1) for j in range(k0, k1 + 1) for x in ("Q%d", "QB%d")] + ["nadj"], w=qk, b=["pc"])
+            tt(T.DE[:, a:b], raw, qa, A.subtract, r=sk + qk, w=["DE%d" % p], b=["pc"])
+            tt(T.VC[:, a:b], T.DE[:, a:b], pa[:, a:b], A.mult, r=["DE%d" % p, "pc%d" % p], w=["VC%d" % p], b=["pm0"])
+            if TPE[p]:
+                k2 = max(k0, nk + 1)
+                base = [(ps[:, 16 * k2:16 + b], T.IDf[:, :], T.U[:, 16 * (k2 - nk - 1):b - 16 * nk], k2 == k0, False),
+                        (ps[:, 16 * k2:16 + b], T.IDf[:, :], T.LK[:, 0:16 * (k1 + 1 - k2)], False, k2 > k0)] if k2 <= k1 else []
+                rb = ["IDf", "LK"] + ["U%d" % q for q in range(p)]
+                if k2 == k0:
+                    mm(base, 4, r=rb, w=["T%d" % j for j in range(k0, k1 + 1)], b=["ps"])
+                    base = []
+                lst = []
+                for d in range(nk):
+                    k3 = max(k0, d + 1)
+                    lst.append((ps[:, 16 * k3:16 + b], T.IDf[:, :], T.VC[:, 16 * (k3 - d - 1):b - 16 * d], d == 0 and k2 > k0,
+                                d == nk - 1 and not base))
+                mm(lst + base, 4, r=rb + ["VC%d" % q for q in range(p + 1)], w=["T%d" % j for j in range(k0, k1 + 1)], b=["ps"])
+            else:
+                for j in range(k0, k1 + 1):
+                    tt(ps[:, 16 * j:16 + 16 * j], ps[:, 16 * j - 16:16 * j], T.VC[:, 16 * j - 16:16 * j], A.add,
+                       r=["T%d" % (j - 1), "VC%d" % p], w=["T%d" % j], b=["ps"])
             tk = ["T%d" % j for j in range(k1 + 1)]
-            job(k, 60, lambda: tt(T.U[:, a:b], TS[:, 272 + a:272 + b], T.LK[:, 0:wd], A.subtract, r=tk + ["LK", "LK0"],
-                                   w=["U%d" % p], b=["pm1"]))
+            tt(T.U[:, a:b], ps[:, 16 + a:16 + b], T.LK[:, 0:wd], A.subtract, r=tk + ["LK"], w=["U%d" % p], b=["ps"])
             ds = list(range(1, k1 + 1))
             for x in range(0, k1, CG):
                 grp = []
                 for d in ds[x:x + CG]:
-                    lo = max(k0, d)
-                    grp.append((d, lo, 16 * (k1 + 1 - lo), coff[0]))
-                    coff[0] += 16 * (k1 + 1 - lo)
+                    k2 = max(k0, d)
+                    grp.append((d, k2, 16 * (k1 + 1 - k2), coff))
+                    coff += 16 * (k1 + 1 - k2)
+                key = "CM%d_%d" % (p, x)
+                op("v", [(lambda d=d, k2=k2, w_=w_, o=o, b=b: v.tensor_tensor(
+                    T.CM[:, o:o + w_], T.U[:, 16 * (k2 - 1):b], ps[:, 16 * (k2 - d):16 * (k2 - d) + w_], A.is_ge))
+                    for d, k2, w_, o in grp], r=tk + ["U%d" % p], w=[key], b=["ps"], ns=sum(max(64, y[2]) * CY for y in grp))
+                mm([(pn[:, a:b], T.ID[:, :], T.OKK[:, 0:wd], True, False)][:x == 0]
+                   + [(pn[:, 16 * (k2 - 1):b], T.ID[:, :], T.CM[:, o:o + w_], False, d == k1) for d, k2, w_, o in grp],
+                   r=[key, "ID", "OKK"], w=["pn%d" % p, "m1", "m3"], b=["pm1"])
+            cp(T.FI[:, a:b], pn[:, a:b], r=["pn%d" % p], w=["FI%d" % p], b=["pm1"])
+            rank_[0] = UPF if p < NUPF else 0.0
+            stream("s", "fetch%d_%d" % (t, p),
+                   lambda a, b, k1=k1: move("s", T.NEW[:, 16 * a:16 * b], G[:, 0:256 * (k1 + 1)].indirect(T.FI[:, a:b])),
+                   a, b, 4, GA, lambda c: ["G0", "G1", "FI%d" % p] + ["Gp%d" % k for k in range(1, k1)], lambda c: ["NEW%d" % c])
+        tol[0], rank_[0] = TOL, 0.0
+        stream("v", "store%d" % t, lambda a, b: v.tensor_copy(X[:, :].indirect(T.Q[:, a:b]), T.NEW[:, 16 * a:16 * b]),
+               0, 240, 4, SCA, lambda c: ["NEW%d" % c, "Q%d" % (c // 16 + 1), "QB%d" % (c // 16 + 1)], lambda c: XK)
 
-                def cmpj(grp=grp, x=x):
-                    key = "CM%d_%d" % (p, x)
-                    op("v", [(lambda d=d, lo=lo, w_=w_, o=o: v.tensor_tensor(
-                        T.CM[:, o:o + w_], T.U[:, 16 * (lo - 1):b], TS[:, 256 + 16 * (lo - d):256 + 16 * (lo - d) + w_], A.is_ge))
-                        for d, lo, w_, o in grp], r=tk + ["U%d" % p], w=[key], b=["pm1"])
-                    lst = [(T.pn[:, a:b], T.ID[:, :], T.OKK[:, 0:wd], True, False)] if x == 0 else []
-                    lst += [(T.pn[:, 16 * (lo - 1):b], T.ID[:, :], T.CM[:, o:o + w_], False, d == k1) for d, lo, w_, o in grp]
-                    mm(lst, r=[key, "ID", "OKK"], w=["pn%d" % p], b=["pn"])
-                job(k, 55 * len(grp), cmpj)
-            job(k, 60, lambda: cp(T.FI[:, a:b], T.pn[:, a:b], r=["pn%d" % p], w=["FI%d" % p], b=["pn"]))
+    for j, e in enumerate(YQ):
+        a, b = 256 + V // len(YQ) * j, 256 + V // len(YQ) * (j + 1)
+        dma(T.y[:, a:b], X[:, a:b], r=XK, e=e)
 
-        def fetch(j, e):
-            a, b, p = MOVES[j]
-            k1 = PARTS[p][1]
-            gk = ["G%ds0" % t, "G%ds1" % t] + ["G%dp%d" % (t, k) for k in range(1, k1)]
-            e(T.NEW[:, 16 * a:16 * b], G[t][:, 0:256 * (k1 + 1)].indirect(T.FI[:, a:b]), r=gk + ["FI%d" % p], w=["NEW%d" % j],
-              ns=60 + 21 * (b - a))
-            if probe[0] is None:
-                todo.discard("NEW%d" % j)
+    cnt = {e: 0 for e in "vstg"}
+    waited = {e: {} for e in Q}
+    tok, total, nd = {}, {}, 0
 
-        def store(j, a, b):
-            cp(T.X[:, :].indirect(T.DI[:, a:b]), T.NEW[:, 16 * a:16 * b], r=["NEW%d" % j, "DI%d" % MOVES[j][2]], w=XK,
-               ns=50 + SCAT * (b - a))
+    def wait(e, k):
+        if waited[e].get(k[0], 0) < k[1]:
+            Q[e].wait_ge(T.sem[k[0]], k[1])
+            waited[e][k[0]] = k[1]
 
-        for p in range(len(PARTS)):
-            feet(p)
-            if p == 0 and t >= 2:
-                job(PARTS[0][1] + 3, 110, lambda: labels(T.Ly[:, 120 * (t - 2):120 * (t - 1)], 256, 120, "Ly%d" % (t - 2)))
-            for j in range(NV):
-                if FETCH[j][0] == p:
-                    job(FETCH[j][1], 220, lambda j=j: fetch(j, cp))
-        for x in late:
-            job(*x)
-
-        def ready(k):
-            out, rs, ws = [], set(), set()
-            for x in side:
-                if x[0] <= k and not (x[4] & todo) and not (x[4] & ws) and not (x[5] & (rs | ws)):
-                    out.append((deps(x[3][0], x[3][1], x[3][2], x[3][3], True), x))
-                rs |= x[4]
-                ws |= x[5]
-            return out
-
-        def run(x):
-            side.remove(x)
-            cost[0] = x[1]
-            x[2]()
-            cost[0] = 60.0
-
-        def drain(k, until):
-            while True:
-                fit = [c for c in ready(k) if c[0] + c[1][1] <= until + SLACK]
-                if not fit:
-                    return
-                now = [c for c in fit if c[0] <= clk["v"] + 1]
-                run(now[0][1] if now else min(fit, key=lambda c: c[0])[1])
-
-        t00 = max(clk.values())
-        for e in clk:
-            clk[e] = t00
-        clk["t"] = t00 + (0 if t == 0 else 500)
-        for k in range(1, 16):
-            for u in range(2):
-                act(T.GW[:, 128 * u:128 * u + 128], T.NL[:, 0:XW].indirect(T.Q[:, 16 * k - 16 + 8 * u:16 * k - 8 + 8 * u]),
-                    r=NK + ["tail0", ("Q%d", "QB%d")[u] % k], w=["GW%d" % u], ns=230)
-            act(G[t][:, 256 * (k + 1):256 * (k + 2)], T.X[:, :].indirect(T.Q[:, 16 * (k - 1):16 * k]),
-                r=XK + ["Q%d" % k, "QB%d" % k], w=["G%dp%d" % (t, k)], ns=400)
-            todo.discard("G%dp%d" % (t, k))
-            for u in range(2):
-                sc, qk, o = ("SC%d", "SD%d")[u] % k, ("Q%d", "QB%d")[u] % (k + 1), 256 * k + 128 * u
-                drain(k - 1, deps("v", ["GW%d" % u], [sc], (), True))
-                op("v", lambda o=o, u=u: v.tensor_tensor_scan(T.SC[:, o:o + 128], T.M[:, 0:128], T.GW[:, 128 * u:128 * u + 128],
-                                                               0.0, A.add, A.min), r=["M", "GW%d" % u], w=[sc], ns=110)
-                drain(k - 1, clk["v"] + LAT - SLACK + SL2[u])
-                ts(T.Q[:, 16 * k + 8 * u:16 * k + 8 * u + 8], T.SC[:, o + 15:o + 128:16], adj, None, A.add, r=[sc, "adj"], w=[qk])
-                todo.discard(sc)
-                todo.discard(qk)
-            for p, (k0, k1) in enumerate(PARTS):
-                if k == k1:
-                    mm([(T.pc[:, 16 * (k0 - 1):16 * k1], T.Bp[:, 15 - i:143 - i], G[t][:, 256 * (k0 + 1) + i:256 * (k1 + 2):16],
-                         i == 0, i == 15) for i in range(16)],
-                       r=["Bp"] + ["G%dp%d" % (t, j) for j in range(k0, k1 + 1)], w=["pc%d" % p], b=["pc"])
-                    todo.discard("pc%d" % p)
-        nf, ns_, at = [NV], [0], [0]
-
-        def fetches():
-            left = set(y for x in side for y in x[5])
-            while nf[0] < len(MOVES) and "FI%d" % MOVES[nf[0]][2] not in left:
-                fetch(nf[0], act)
-                nf[0] += 1
-                if t == 0 and nf[0] == len(MOVES) - 1:
-                    silu(1)
-
-        def piece(wd):
-            j = ns_[0]
-            b = min(MOVES[j][1], at[0] + wd)
-            store(j, at[0], b)
-            at[0] = b
-            if b == MOVES[j][1]:
-                ns_[0] += 1
-
-        while side:
-            fetches()
-            rdy = ready(99)
-            best = min(rdy, key=lambda c: c[0])
-            now = [c for c in rdy if c[0] <= clk["v"] + 1]
-            j = ns_[0]
-            left = set(y for x in side for y in x[5])
-            if now:
-                run(now[0][1])
-            elif (j < nf[0] and "NEW%d" % j not in todo and "DI%d" % MOVES[j][2] not in left
-                  and deps("v", ["NEW%d" % j, "DI%d" % MOVES[j][2]], XK, (), True) <= best[0]):
-                piece(PIECE)
+    if not ORDER:
+        ORDER.extend(order(ops))
+    for grp, pre in ORDER:
+        o = ops[grp[0]]
+        e = o["e"]
+        if o["kind"] == "a":
+            k = o["sem"]
+        else:
+            need = {}
+            for p, hard in pre.items():
+                if hard:
+                    need[tok[p][0]] = max(need.get(tok[p][0], 0), tok[p][1])
+            for x in need:
+                wait(e, (x, need[x]))
+            if o["kind"] == "r":
+                o["fn"]()
+                k = o["sem"]
+            elif o["kind"] == "d":
+                k = ("d%d" % nd, 16)
+                nd += 1
+                o["fn"]().then_inc(T.sem[k[0]], 16)
             else:
-                run(best[1])
-        fetches()
-        if not last:
-            z = (t + 1) % 2
-            zs = ["ZG%d" % z, "ZG%dv" % z, "Bz"] + ["ZGv%d" % a for a in range(192, 256, 8)]
-            content(ZG[z], T.Bz, 0, True, False, zs)
-            content(ZG[z], T.Bz, 1, True, False, zs)
-        if t == 0:
-            silu(2)
-        while ns_[0] < len(MOVES):
-            piece(256)
-
-    dma("y", T.y[:, V:W], T.X[:, V:W], r=["Xo"])
-    for j in range(len(FINV) - 1):
-        for e in range(2):
-            a, b = 120 * e + FINV[j], 120 * e + FINV[j + 1]
-            (cp, act)[e](T.XR[:, 16 * a:16 * b], T.X[:, 0:V].indirect(T.Ly[:, a:b]), r=["Xh", "Ly%d" % e], w=["Y%d%d" % (e, j)])
-            dma("y", T.y[:, 256 + 16 * a:256 + 16 * b], T.XR[:, 16 * a:16 * b], r=["Y%d%d" % (e, j)])
+                if o["range"]:
+                    ins = o["fn"](o["range"][0], ops[grp[-1]]["range"][1])
+                else:
+                    for f in o["fn"]:
+                        ins = f()
+                cnt[e] += 1
+                k = ("c" + e, cnt[e])
+                ins.then_inc(T.sem[k[0]], 1)
+        total[k[0]] = k[1]
+        for j in grp:
+            tok[j] = k
     for k in total:
         wait("g", (k, total[k]))

@@ -8,23 +8,29 @@ XW = V + 15 * ST
 ZW = 280
 PARTS = [(1, 2), (3, 5), (6, 8), (9, 12), (13, 15)]
 TPE = (1, 1, 1, 1, 1, 1)
-HALVES = 9
-VCOL = 1
-CG = 4
-PRE0 = 2
+HALVES = 7
+VCOL = 3
+CG = 5
+PRE0 = 1
+TINY = 2.0 ** -60
+WR = 0.0
+PASSES, MIX, TBACK, TMIN, TMAX, SLK, BSL, FAR = 4, 1.0, 60, 150, 900, 1.4, True, 3000.0
 SQA, SY, MAGIC = True, True, 1.5 * 2.0 ** 23
-NX0 = (64, 64, 64, 32)
+NX0 = (64, 64, 32, 32)
 NXV = (32, 32, 32, 32)
-YQ = ("y", "s", "y", "s")
+SUMV = (1, 1, 0, 0)
+UPX, VFIRST = (0.0, 0.0, 0.0, 0.0), (0, 3)
+YQ = ("y",)
 LAT, CY, PE, GA, SCA, MINP = 140, 0.92, 0.66, 1.37, 2.9, 170
-DFIX, DBW, RFIX, RFIRST = 1000.0, 230.0, 1300.0, 2500.0
+DFIX, DROW, DBW, RFIX, RFIRST = 800.0, 400.0, 260.0, 1300.0, 2500.0
 TOL = {"v": 60, "s": 60, "t": 60, "g": 600, "y": 60, "a": 0}
+TX = {"v": 700, "s": 200, "t": 400}
 TWALK = {"v": 150, "s": 250}
 TFEET = {"v": 250, "s": 300, "t": 100}
 TLAST = {"v": 250, "s": 100, "t": 60}
-CAP = {"fetc": 900}
-UPF, NUP, NUPF, LEUP = 3e4, 3, 0, 4e5
-BOOST, AHEAD, DEPTH, MANY, EXTRA = 3000.0, 0, 6, 12, 300.0
+CAP = {"fetc": 500}
+UPF, NUP, NUPF, LD = 3e4, 3, 0, (8, 7, 9, 6, 5, 4)
+BOOST, AHEAD, DEPTH, MANY, EXTRA = 3000.0, 0, 6, 99, 300.0
 
 SCRATCH = {
     "X": ("sbuf", [128, XW], "bfloat16"), "XO": ("sbuf", [128, W + V], "bfloat16"), "G": ("sbuf", [128, W], "bfloat16"),
@@ -32,7 +38,7 @@ SCRATCH = {
     "SC": ("sbuf", [128, 4096], "float32"), "GW": ("sbuf", [128, 256], "float32"),
     "NEW": ("sbuf", [128, 3840], "bfloat16"), "SUM": ("sbuf", [128, 2048], "float32"),
     "SB": ("sbuf", [128, ZW], "bfloat16"), "ZB": ("sbuf", [128, ZW], "bfloat16"),
-    "KN": ("sbuf", [128, 512], "bfloat16"), "KO": ("sbuf", [128, 512], "bfloat16"), "ZK": ("sbuf", [128, 512], "float32"),
+    "KO": ("sbuf", [128, 512], "bfloat16"), "ZK": ("sbuf", [128, 512], "float32"),
     "nxi": ("sbuf", [128, 256], "int32"), "lei": ("sbuf", [128, 512], "int32"), "voi": ("sbuf", [128, 256], "int32"),
     "lai": ("sbuf", [128, 96], "int32"), "nui": ("sbuf", [128, 4], "int32"),
     "IP": ("sbuf", [128, 4], "int32"), "IQ": ("sbuf", [128, 4], "int32"), "col": ("sbuf", [128, 16], "float32"),
@@ -45,12 +51,14 @@ SCRATCH = {
     "Bz": ("sbuf", [128, 144], "bfloat16"), "Bp": ("sbuf", [128, 144], "bfloat16"), "M": ("sbuf", [128, 256], "float32"),
     "LK": ("sbuf", [128, 96], "float32"), "t0": ("sbuf", [128, 256], "float32"), "t1": ("sbuf", [128, 256], "float32"),
     "t4": ("sbuf", [128, 64], "float32"), "i0": ("sbuf", [128, 256], "int32"), "i1": ("sbuf", [128, 256], "int32"),
+    "i2": ("sbuf", [128, 256], "int32"), "By": ("sbuf", [128, 144], "bfloat16"), "C1": ("sbuf", [128, 256], "bfloat16"),
     "LP": ("sbuf", [128, 1280], "bfloat16"), "PC": ("sbuf", [128, 1024], "bfloat16"),
     "Lx": ("sbuf", [128, 256], "uint16"), "Lz": ("sbuf", [128, 256], "uint16"),
     "Q": ("sbuf", [128, 256], "uint16"), "FI": ("sbuf", [128, 240], "uint16"),
     "H": ("sbuf", [128, 256], "float32"), "E": ("sbuf", [128, 256], "float32"), "F0": ("sbuf", [128, 256], "float32"),
     "F1": ("sbuf", [128, 256], "float32"), "D": ("sbuf", [128, 256], "bfloat16"), "XD": ("sbuf", [128, 1024], "bfloat16"),
     "TM": ("sbuf", [128, 256], "float32"), "RI": ("sbuf", [128, 240], "float32"),
+    "IDn": ("sbuf", [128, 128], "float32"), "MC": ("sbuf", [128, 96], "float32"),
     "DE": ("sbuf", [128, 240], "float32"), "VC": ("sbuf", [128, 240], "float32"), "U": ("sbuf", [128, 240], "float32"),
     "CM": ("sbuf", [128, 1920], "bfloat16"), "YN": ("sbuf", [128, 256], "float32"),
     "pp0": ("psum", [128, 512], "float32"), "pp1": ("psum", [128, 512], "float32"), "pp2": ("psum", [128, 512], "float32"),
@@ -77,6 +85,21 @@ def order(ops):
         pri[i] = ((1.0 if o["range"] else o["lat"]) + o["up"]
                   + max([pri[j] + (LAT if ops[j]["pre"][i] and ops[j]["stream"] != o["stream"] else 0) for j in succ[i]] + [0.0]))
     pri = [x + o["rank"] for x, o in zip(pri, ops)]
+    best = None
+    for _ in range(PASSES):
+        out, fin = one_pass(ops, succ, list(pri), best is not None and TMAX > 0)
+        if best is None or max(fin) < best[1]:
+            best = (out, max(fin))
+        if PASSES > 1:
+            back = [dict(ops[n - 1 - i], pre={n - 1 - j: ops[j]["pre"][n - 1 - i] for j in succ[n - 1 - i]}, tol=TBACK) for i in range(n)]
+            bs = [[n - 1 - p for p in ops[n - 1 - i]["pre"]] for i in range(n)]
+            late = one_pass(back, bs, [fin[n - 1 - i] for i in range(n)], BSL)[1]
+            pri = [MIX * (late[n - 1 - i] + WR * ops[i]["rank"]) + (1 - MIX) * pri[i] for i in range(n)]
+    return best[0]
+
+
+def one_pass(ops, succ, pri, slack=False):
+    n = len(ops)
     pri0, ahead = list(pri), [0]
     kind = [str(o["stream"])[:4] for o in ops]
     left = [len(o["pre"]) for o in ops]
@@ -87,13 +110,13 @@ def order(ops):
     out = []
     dfree = 0.0
 
-    def start(i, est=None):
+    base = [0.0] * n
+    gap = [[(j, {True: LAT, False: 0.0, None: -1e18}[ops[j]["pre"][i]]) for j in succ[i]] for i in range(n)]
+    whole = [o["lat"] + o["fix"] for o in ops]
+
+    def start(i, t):
         o = ops[i]
-        t = free[o["e"]]
-        for p, hard in o["pre"].items():
-            f = fin[p] if fin[p] is not None else est[p]
-            if hard is not None:
-                t = max(t, f + (LAT if hard else 0))
+        t = max(t, free[o["e"]])
         for k in o["b"]:
             for e2, j in bank.get(k, {}).items():
                 if e2 != o["e"]:
@@ -103,34 +126,38 @@ def order(ops):
     def done(i, t):
         fin[i] = t
         ready.discard(i)
-        for j in succ[i]:
+        for j, d in gap[i]:
             left[j] -= 1
+            base[j] = max(base[j], t + d)
             if left[j] == 0:
                 ready.add(j)
 
     while ready:
-        st = {i: start(i) for i in ready}
+        st = {i: start(i, base[i]) for i in ready}
         i0 = min(st, key=lambda i: (st[i], -pri[i]))
         e, now = ops[i0]["e"], st[i0]
-        est = {i: st[i] + ops[i]["lat"] + ops[i]["fix"] for i in ready}
-        front = list(ready)
+        front, seen, at = list(ready), {}, {}
         for i in ready:
             if kind[i] == "fetc":
                 pri[i] = pri0[i] + (BOOST if ahead[0] < AHEAD else 0.0)
         for _ in range(DEPTH):
             nxt = []
             for i in front:
-                for j in succ[i]:
-                    if j not in est and all(fin[p] is not None or p in est for p in ops[j]["pre"]):
-                        st[j] = start(j, est)
-                        est[j] = st[j] + ops[j]["lat"] + ops[j]["fix"]
-                        nxt.append(j)
+                t = st[i] + whole[i]
+                if t < now + FAR:
+                    for j, d in gap[i]:
+                        seen[j] = seen.get(j, 0) + 1
+                        at[j] = max(at.get(j, base[j]), t + d)
+                        if seen[j] == left[j]:
+                            st[j] = start(j, at[j])
+                            nxt.append(j)
             front = nxt
         mine = [i for i in st if ops[i]["e"] == e]
         can = sorted([i for i in mine if i in ready and st[i] <= now + 1], key=lambda i: (-pri[i], i))
         pick = None
+        top = max(pri[j] + st[j] for j in st)
         for i in can:
-            lim = min([st[j] + ops[j]["tol"] for j in mine
+            lim = min([st[j] + (ops[j]["tol"] if not slack else min(TMAX, max(TMIN, SLK * (top - pri[j] - st[j])))) for j in mine
                        if pri[j] > pri[i] and st[j] > now + 1 and ops[j]["stream"] != ops[i]["stream"]] + [1e18])
             o = ops[i]
             if kind[i] == "stor" and ahead[0] >= MANY:
@@ -171,7 +198,7 @@ def order(ops):
         for j in grp:
             done(j, end)
         out.append((grp, pre))
-    return out
+    return out, fin
 
 
 def rank_program(g, core, T, topo):
@@ -220,7 +247,7 @@ def rank_program(g, core, T, topo):
             put(e, "c", fn, r(c), w(c), (), 16 * unit * el, None, 60.0, name, (c, c + unit))
 
     def dma(out, in_, r=(), w=(), up=0.0, size=2, e="y"):
-        put(e, "d", lambda: Q[e].dma_start(out, in_), r, w, (), 60.0, DFIX + 128 * out.shape[1] * size / DBW, up=up)
+        put(e, "d", lambda: Q[e].dma_start(out, in_), r, w, (), 60.0, DFIX + DROW + 128 * out.shape[1] * size / DBW, up=up)
 
     def lanes(src, dst):
         es = topo.engines(src, dst)[::2]
@@ -280,8 +307,8 @@ def rank_program(g, core, T, topo):
     AR = [T["AR%d" % t] for t in range(R)]
     pp = [T.pp0, T.pp1, T.pp2, T.pp3]
     pa, pn, ps, pc = T.pm0, T.pm1, T.ps, T.pc
-    BK, BN = [pa[:, 0:128], pn[:, 0:128], pa[:, 128:256], pn[:, 128:256]], ["pm0", "pm1", "pm0", "pm1"]
-    XK = ["Xa", "Xb", "Xi"]
+    BK, BN = [pa[:, 0:128], pn[:, 0:128], ps[:, 0:128], pc[:, 0:128]], ["pm0", "pm1", "ps", "pc"]
+    XK = ["Xb", "Xt"]
     XN = ["XN%d" % c for c in range(0, 256, 8)]
     PK = ["P0%d" % b for b in range(4)] + ["P1%d" % b for b in range(4)] + ["tail"]
     pf, pi, pi1, pg, adj, wf, lo, hi, p8, k8, k88, r8, pm8 = [T.col[:, k:k + 1] for k in range(13)]
@@ -289,8 +316,8 @@ def rank_program(g, core, T, topo):
     NP = len(PARTS)
     NMAX = max(k1 - k0 + 1 for k0, k1 in PARTS)
     AK, NK = ["pc%d" % p for p in range(NP)], ["pn%d" % p for p in range(NP)]
-    MK = [["m0"] + AK, ["m1"] + NK, ["m2"] + AK, ["m3"] + NK]
     TK = ["T%d" % j for j in range(16)]
+    MK = [["m0"] + AK, ["m1"] + NK, ["m2"] + TK, ["m3", "s0"]]
 
     def repeat(buf, width, key, size):
         a = 16
@@ -299,16 +326,13 @@ def rank_program(g, core, T, topo):
             dma(buf[:, a:b], buf[:, 0:b - a], r=[key], w=[key], size=size)
             a = b
 
-    dma(T.nui[:, 0:1], T.nu[:, :], w=["nui"], up=9e5)
-    dma(T.SB[:, 16:272], T.x[:, 0:256], w=["SBa"], up=8e5)
-    dma(T.nxi[:, :], T.nx[:, :], w=["nxi"], up=7e5, size=4)
-    dma(T.voi[:, :], T.vol[:, :], w=["voi"], size=4, up=6e5)
-    dma(X[:, 256:2304], T.x[:, 256:2304], w=["Xa"], up=5e5)
-    dma(X[:, 2304:W], T.x[:, 2304:W], w=["Xb"], up=5e5)
-    dma(T.lei[:, :], T.le[:, :], w=["lei"], size=4, up=LEUP)
-    dma(X[:, 0:256], T.x[:, 0:256], w=["Xi"], up=5e5)
-    for j in range(NMAX):
-        dma(T.lai[:, 16 * j:16 * j + 16], T.lag[:, :], w=["lai%d" % j], size=4)
+    dma(T.nui[:, 0:1], T.nu[:, :], w=["nui"], up=LD[0] * 1e5)
+    dma(T.SB[:, 16:272], T.x[:, 0:256], w=["SBa"], up=LD[1] * 1e5)
+    dma(T.nxi[:, :], T.nx[:, :], w=["nxi"], up=LD[2] * 1e5, size=4)
+    dma(T.voi[:, :], T.vol[:, :], w=["voi"], size=4, up=LD[3] * 1e5)
+    dma(X[:, 256:W], T.x[:, 256:W], w=["Xb"], up=LD[4] * 1e5)
+    dma(T.lei[:, :], T.le[:, :], w=["lei"], size=4, up=LD[5] * 1e5)
+    dma(T.lai[:, 0:16], T.lag[:, :], w=["lai"], size=4)
     dma(G[:, 256:512], T.x[:, 0:256], w=["G1"])
     dma(XO[:, 0:W], T.x[:, :], w=["XO"])
     iota(T.IP[:, 0:1], [[1, 1]], 0, 1, "IP", False)
@@ -345,6 +369,9 @@ def rank_program(g, core, T, topo):
     tt(T.B2[:, :], T.Bf[:, 8:152], T.Bf[:, 0:144], A.add, 2, r=["Bf", "Bf0"], w=["B2"])
     ts(T.ID[:, :], T.IX[:, 0:128], pf, 256.0, A.is_equal, A.mult, r=["IX", "pf"], w=["ID"])
     ts(T.IDf[:, :], T.IX[:, 0:128], pf, None, A.is_equal, r=["IX", "pf"], w=["IDf"])
+    if SQA == 2:
+        ts(T.IDn[:, :], T.IX[:, 0:128], pf, -1.0, A.is_equal, A.mult, r=["IX", "pf"], w=["IDn"])
+        ms(T.MC[:, :], MAGIC, w=["MC"])
     ts(T.UN[:, 0:128], T.IX[:, 0:128], k8, 0.5, A.is_equal, A.mult, r=["IX", "k8"], w=["UN0"])
     ts(T.UN[:, 128:256], T.IX[:, 0:128], k88, 0.5, A.is_equal, A.mult, r=["IX", "k88"], w=["UN1"])
     ts(T.t4[:, 0:16], T.IX[:, 0:16], pi, 32768.0, A.is_equal, A.mult, r=["IX", "pi"], w=["t4"])
@@ -366,9 +393,14 @@ def rank_program(g, core, T, topo):
     cp(wf, T.nui[:, 0:1], r=["nui"], w=["wf"])
     ts(T.Bw[:, :], T.B2[:, :], wf, None, A.mult, r=["B2", "wf"], w=["Bw"])
     ts(T.Bz[:, :], T.B2[:, :], T.ZB[:, 272:273], None, A.mult, r=["B2", "ZB"], w=["Bz"])
+    ts(T.By[:, :], T.Bz[:, :], 1 / TINY, None, A.mult, two=0.5, r=["Bz"], w=["By"])
+    ms(T.C1[:, 0:128], 1.0 / 256, w=["C1"])
+    ms(T.C1[:, 128:256], -1.0 / 256, w=["C2"])
     ts(T.Bp[:, :], T.Bf[:, 8:152], wf, 512.0, A.mult, A.mult, r=["Bf", "wf"], w=["Bp"])
-    cp(T.LK[:, 0:16 * NMAX], T.lai[:, 0:16 * NMAX], r=["lai%d" % j for j in range(NMAX)], w=["LK"])
-    cp(T.Lx[:, :], T.nxi[:, :], r=["nxi"], w=["Lx"])
+    cp(T.LK[:, 0:16], T.lai[:, 0:16], r=["lai"], w=["LK"])
+    repeat(T.LK, 16 * NMAX, "LK", 4)
+    ts(T.i2[:, :], T.nxi[:, :], V - 1, None, A.bitwise_and, r=["nxi"], w=["i2"])
+    cp(T.Lx[:, :], T.i2[:, :], r=["i2"], w=["Lx"])
     ts(T.Lz[:, :], T.nxi[:, :], 16.0 - V, 0.0, A.add, A.max, r=["nxi"], w=["Lz"])
     LP, PC = T.LP, T.PC
     rank_[0] = 2e4
@@ -378,8 +410,6 @@ def rank_program(g, core, T, topo):
     cp(LP[:, 256:512], T.i1[:, :], r=["i1"], w=["Llo"])
     ts(LP[:, 768:1024], T.voi[:, :], 1.0 / 512, None, A.mult, r=["voi"], w=["Lv"])
     rank_[0] = 0.0
-    ts(LP[:, 512:640], LP[:, 0:128], -1.0, None, A.mult, two=0.5, r=["Lhi"], w=["Lnh"])
-    ts(LP[:, 640:768], LP[:, 256:384], -1.0, None, A.mult, two=0.5, r=["Llo"], w=["Lnl"])
     ts(LP[:, 1024:1280], LP[:, 0:256], float(V), None, A.is_ge, two=0.5, r=["Lhi"], w=["Lk"])
     up_ = [T.WL[:, 8:136], T.WH[:, 16:144]]
     dn_ = [T.WL[:, 0:128], T.WH[:, 8:136]]
@@ -389,22 +419,19 @@ def rank_program(g, core, T, topo):
             for u in range(2) for j, (m, c) in enumerate(terms)], r=keys + ["WL", "WH"], w=key, b=[name])
 
     hl = ["Lhi", "Llo"]
-    c0, c1, a0, n0 = ["s0", "s1"], ["x%d" % b for b in range(4)], ["m0", "m2"] + AK, ["m1", "m3"] + NK
+    c0, c1, a0, a1, n0 = ["m3", "s0", "s1"], ["z0", "z1"], ["m0", "sa", "sb"] + AK, ["x%d" % b for b in range(4)], ["m1"] + NK
     EK = ["EP%d" % b for b in range(4)]
     rank_[0] = 2e4
     double(pc, 0, [(up_, 0), (up_, 128), (dn_, 256), (dn_, 384)], hl, c0, "pc")
     double(pc, 256, [(up_, 768), (up_, 896)], ["Lv"], c1, "pc")
-    double(pa, 0, [(up_, 128), (dn_, 384)], hl, a0, "pm0")
-    double(pa, 256, [(up_, 896)], ["Lv"], ["a1"], "pm0")
     op("s", lambda: s.activation(PC[:, 0:512], pc[:, :], F.Identity, scale=-1.0), r=c0 + c1, w=["PC0"], b=["pc"], ns=512 * CY)
-    op("s", lambda: s.activation(PC[:, 512:1024], pa[:, :], F.Identity, scale=-1.0), r=a0 + ["a1"], w=["PC1"], b=["pm0"], ns=512 * CY)
+    rank_[0] = 1.5e4
+    double(pa, 0, [(up_, 128), (dn_, 384)], hl, a0, "pm0")
+    double(pa, 256, [(up_, 896)], ["Lv"], a1, "pm0")
+    op("s", lambda: s.activation(PC[:, 512:1024], pa[:, :], F.Identity, scale=-1.0), r=a0 + a1, w=["PC1"], b=["pm0"], ns=512 * CY)
     rank_[0] = 0.0
-    double(pn, 0, [(up_, 128), (dn_, 384), (up_, 512), (dn_, 640)], hl + ["Lnh", "Lnl"], n0, "pm1")
-    double(ps, 0, [(up_, 1024), (dn_, 1024)], ["Lk"], TK, "ps")
-    double(ps, 256, [(up_, 1152), (dn_, 1152)], ["Lk"], EK, "ps")
-    act(T.D[:, :], pn[:, 0:256], r=n0, w=["D%d" % b for b in range(4)], b=["pm1"])
-    op("s", lambda: s.activation(T.KN[:, :], ps[:, :], F.Identity, scale=-1.0, bias=1.0), r=TK + EK, w=["KN"], b=["ps"], ns=512 * CY)
-    op("s", lambda: s.activation(T.KO[:, :], T.KN[:, :], F.Identity, scale=-1.0, bias=1.0), r=["KN"], w=["KO"], ns=512 * CY)
+    ts(LP[:, 512:768], PC[:, 512:768], -2.0, None, A.mult, two=0.5, r=["PC1"], w=["L2"])
+    tt(T.D[:, :], PC[:, 0:256], LP[:, 512:768], A.add, 2, r=["PC0", "L2"], w=["D%d" % b for b in range(4)])
 
     def spread(b, srcs, keys, how):
         lst = []
@@ -420,13 +447,13 @@ def rank_program(g, core, T, topo):
         mm(lst, r=keys + FK + ["ZR"], w=["pp%d" % b], b=["pp%d" % b])
 
     def before(b, t):
-        spread(b, [PC[:, 512:768], PC[:, 768:1024]] + [T.XD[:, 256 * j:256 * j + 256] for j in range(t)],
-               ["PC1"] + ["XD%d_%d" % (j, b) for j in range(t)], "open")
+        spread(b, [PC[:, 512:768], PC[:, 768:1024]], ["PC1"], "open")
 
-    rank_[0] = 1e4
     for b in range(4):
+        rank_[0] = 1e4 - 1e3 * b
         spread(b, [PC[:, 0:256], PC[:, 256:512]], ["PC0"], "whole")
-        act(T.SUM[:, 512 * b:512 * b + 512], pp[b][:, :], r=["pp%d" % b], w=["SUM%d" % b], b=["pp%d" % b], up=2e4)
+        rank_[0] = 1e4 if b < PRE0 else 0.0
+        (act, cp)[SUMV[b]](T.SUM[:, 512 * b:512 * b + 512], pp[b][:, :], r=["pp%d" % b], w=["SUM%d" % b], b=["pp%d" % b])
         if b < PRE0:
             before(b, 0)
     rank_[0] = 0.0
@@ -436,7 +463,9 @@ def rank_program(g, core, T, topo):
     tt(T.t1[:, 128:256], T.t0[:, 0:128], T.t0[:, 128:256], A.subtract, 2, r=["al", "be"], w=["t1b"])
     mm([(ps[:, 256 * a + u:256 * a + 256:2], T.DU[:, 128 * u:128 * u + 128], T.t1[:, 128 * a:128 * a + 128], True, True)
         for a in range(2) for u in range(2)], 4, r=["t1a", "t1b", "DU0", "DU1"], w=TK + EK, b=["ps"])
+    rank_[0] = 2e4
     act(T.H[:, :], ps[:, 0:256], r=["T0"], w=["H"], b=["ps"])
+    rank_[0] = 0.0
 
     def factors(b):
         c = 64 * b
@@ -448,10 +477,17 @@ def rank_program(g, core, T, topo):
     for b in range(4):
         factors(b)
 
-    def content(src, o, lhs, b, key, keys, out, w, bank):
+    def content(src, o, lhs, b, key, keys, out, w, bank, whole=False, more=()):
         mm([(out[:, 64 * a:64 * a + 64], lhs[:, 15 - r:143 - r], src[:, o + 2048 * a + 512 * b + r:o + 2048 * a + 512 * b + 512:8],
-             r == 0, r == 7) for a in range(2) for r in range(8)],
+             whole and r == 0, whole and r == 7) for a in range(2) for r in range(8)] + list(more),
            r=keys + [key % (c + x) for c in (32 * b, 128 + 32 * b) for x in range(0, 32, 8)], w=w, b=[bank])
+
+    def begin(b, t):
+        mm([(BK[b], T.ID[:, :], T.C1[:, 0:128], True, False)], r=["ID", "C1"], w=MK[b], b=[BN[b]])
+        if t == 0:
+            content(ZG, 0, T.Bz, b, "Z%d", ["Bz"], BK[b], MK[b][:1], BN[b])
+        else:
+            mm([(BK[b], T.IDf[:, :], T.ZK[:, 128 * b:128 * b + 128], False, False)], 4, r=["IDf", "ZK%d" % b], w=MK[b][:1], b=[BN[b]])
 
     def sides(out, in0, in1, o, q, **k):
         op("v", [(lambda a=a: v.tensor_tensor(out[:, 64 * a:64 * a + 64], in0[:, 256 * a + 64 * q:256 * a + 64 * q + 64],
@@ -461,15 +497,16 @@ def rank_program(g, core, T, topo):
         for c in (32 * b, 128 + 32 * b):
             gather("s", ZG[:, 16 * c:16 * c + 512], T.ZB[:, 0:272].indirect(T.Lz[:, c:c + 32]), r=["ZB", "Lz"],
                    w=["Z%d" % x for x in range(c, c + 32, 8)])
-        content(ZG, 0, T.Bz, b, "Z%d", ["Bz"], pa[:, 256 + 128 * (b % 2):384 + 128 * (b % 2)], ["a1", "z%d" % (b % 2)], "pm0")
-        act(T.ZK[:, 128 * b:128 * b + 128], pa[:, 256 + 128 * (b % 2):384 + 128 * (b % 2)], r=["z%d" % (b % 2)], w=["ZK%d" % b], b=["pm0"])
+        begin(b, 0)
 
     for t in range(R):
         last = t == R - 1
+        if not last:
+            ts(X[:, 0:256], X[:, V:W], TINY, None, A.mult, two=0.5, r=["Xb"], w=["Xt"])
         if t > 0:
             send(nxt, AR[t][:, :], X[:, V:W], "arr%d" % t, "sent%d" % t, ["Xb"])
             arrive(prv, "arr%d" % t, "sent%d" % t, "AR%d" % t)
-            dma(XO[:, 256:V], X[:, 256:V], r=XK, w=["XO"])
+            dma(XO[:, 256:V], X[:, 256:V], r=["Xb"], w=["XO"])
             dma(G[:, 256:512], AR[t - 1][:, :], r=["AR%d" % (t - 1)], w=["G1"])
         dma(G[:, 0:256], AR[t][:, :], r=["AR%d" % t], w=["G0"])
         if last:
@@ -481,29 +518,41 @@ def rank_program(g, core, T, topo):
             for e, cs in (("v", cols[:nv]), ("s", cols[nv:])):
                 for run in ([x for x in cs if x < 128], [x for x in cs if x >= 128]):
                     if run:
-                        gather(e, XO[:, W + 16 * run[0]:W + 16 * run[-1] + 128], X[:, 0:W].indirect(T.Lx[:, run[0]:run[-1] + 8]),
+                        gather(e, XO[:, W + 16 * run[0]:W + 16 * run[-1] + 128], X[:, 0:V].indirect(T.Lx[:, run[0]:run[-1] + 8]),
                                r=XK + ["Lx"], w=["XN%d" % x for x in run])
-            content(XO, W, T.Bw, b, "XN%d", ["Bw"], BK[b], MK[b], BN[b])
-            m, sk, x1 = pc[:, 128 * u:128 * u + 128], "s%d" % u, pc[:, 256 + c:320 + c]
-            sides(m, T.KN, BK[b], A.mult, b, r=["m%d" % b, "KN"], w=[sk], b=[BN[b], "pc"])
-            tt(m, T.ZK[:, 128 * b:128 * b + 128], m, A.add, r=[sk, "ZK%d" % b], w=[sk], b=["pc"])
+            m, x1 = BK[b], pa[:, 256 + c:320 + c]
+            content(XO, W, T.Bw, b, "XN%d", ["Bw", "C2"], m, MK[b][:1], BN[b], more=[(m, T.ID[:, :], T.C1[:, 128:256], False, True)])
+            rank_[0], tol[0] = UPX[0], TX
             op("v", [lambda c=c, m=m: v.tensor_tensor(T.TM[:, c:c + 64], T.F0[:, c:c + 64], m[:, 0:64], A.mult),
                      lambda c=c, m=m: v.tensor_tensor(m[:, 64:128], T.F1[:, c:c + 64], m[:, 64:128], A.mult)],
-               r=[sk, "F%d" % b], w=["TM%d" % b, sk], b=["pc"], ns=120)
-            tt(x1, T.TM[:, c:c + 64], m[:, 64:128], A.is_lt, r=["TM%d" % b, sk], w=["x%d" % b], b=["pc"])
-            tt(T.XD[:, 256 * t + c:256 * t + c + 64], T.D[:, c:c + 64], x1, A.mult, r=["x%d" % b, "D%d" % b], w=["XD%d_%d" % (t, b)], b=["pc"])
+               r=["m%d" % b, "F%d" % b], w=["TM%d" % b, "m%d" % b], b=[BN[b]], ns=120)
+            tt(x1, T.TM[:, c:c + 64], m[:, 64:128], A.is_lt, r=["TM%d" % b, "m%d" % b], w=["x%d" % b], b=["pm0", BN[b]])
+            tt(T.XD[:, 256 * t + c:256 * t + c + 64], T.D[:, c:c + 64], x1, A.mult, r=["x%d" % b, "D%d" % b], w=["XD%d_%d" % (t, b)], b=["pm0"])
+            rank_[0] = UPX[1]
             if t == 0 and b >= PRE0:
                 spread(b, [PC[:, 512:768], PC[:, 768:1024], T.XD[:, 0:256]], ["PC1", "XD0_%d" % b], "whole")
             else:
                 spread(b, [T.XD[:, 256 * t:256 * t + 256]], ["XD%d_%d" % (t, b)], "close")
             o = 512 * b
-            act(NL[:, o + 2048:o + 2560], pp[b][:, :], r=["pp%d" % b], w=["P1%d" % b], b=["pp%d" % b])
+            rank_[0] = UPX[2]
             tt(NL[:, o:o + 512], T.SUM[:, o:o + 512], pp[b][:, :], A.subtract, r=["pp%d" % b, "SUM%d" % b], w=["P0%d" % b], b=["pp%d" % b])
+            rank_[0] = 0.0
+            act(NL[:, o + 2048:o + 2560], pp[b][:, :], r=["pp%d" % b] + ["P0%d" % b][:b in VFIRST], w=["P1%d" % b], b=["pp%d" % b])
+            tol[0] = TOL
+        if t == 0:
+            for a in range(2):
+                double(pc, 256, [(up_, 1024 + 128 * a), (dn_, 1024 + 128 * a)], ["Lk"], ["z0", "z1"], "pc")
+                act(T.KO[:, 256 * a:256 * a + 256], pc[:, 256:512], r=["z0", "z1"], w=["KO%d" % a], b=["pc"])
+        if not last:
+            mm([(pn[:, 256:512], T.ID[:, :], PC[:, 512:768], True, False), (pn[:, 256:512], T.ID[:, :], T.XD[:, 256 * t:256 * t + 256], False, True)],
+               r=["ID", "PC1"] + ["XD%d_%d" % (t, b) for b in range(4)], w=["n1"], b=["pm1"])
+            op("s", lambda: s.activation(PC[:, 512:768], pn[:, 256:512], F.Identity, scale=1.0 / 256), r=["n1"], w=["PC1"], b=["pm1"],
+               ns=256 * CY)
         for b in range(4):
             c = 64 * b
-            x1, ep, bn = pc[:, 256 + c:320 + c], ps[:, 256 + c:320 + c], "pc"
+            x1, ep, bn = pa[:, 256 + c:320 + c], ps[:, 256 + c:320 + c], "pm0"
             if t == 0:
-                act(T.E[:, c:c + 64], ep, r=["EP%d" % b], w=["E%d" % b], b=["ps"], up=5e4)
+                act(T.E[:, c:c + 64], ep, r=["EP%d" % b], w=["E%d" % b], b=["ps"])
             if SY:
                 op("s", lambda x1=x1: s.activation(x1, x1, F.Identity, bias=1.0, scale=-2.0), r=["x%d" % b], w=["x%d" % b], b=[bn])
             else:
@@ -515,19 +564,18 @@ def rank_program(g, core, T, topo):
                 if t < R - 2:
                     act(T.E[:, c:c + 64], ep, r=["EP%d" % b], w=["E%d" % b], b=["ps"], up=5e4)
                 before(b, t + 1)
-                z = pn[:, 256 + 128 * (b % 2):384 + 128 * (b % 2)]
-                content(XO, W, T.Bz, b, "XN%d", ["Bz"], z, ["z%d" % (b % 2)], "pm1")
-                sides(T.ZK[:, 128 * b:128 * b + 128], T.KO, z, A.mult, b, r=["z%d" % (b % 2), "KO"], w=["ZK%d" % b], b=["pm1"])
+                z = pc[:, 256 + 128 * (b % 2):384 + 128 * (b % 2)]
+                content(XO, W, T.By, b, "XN%d", ["By"], z, ["z%d" % (b % 2)], "pc", True)
+                sides(T.ZK[:, 128 * b:128 * b + 128], T.KO, z, A.mult, b, r=["z%d" % (b % 2), "KO0", "KO1"], w=["ZK%d" % b], b=["pc"])
         if last:
-            mm([(pn[:, 256:384], T.UN[:, 128 * u:128 * u + 128], T.D[:, u:256:2], u == 0, u == 1) for u in range(2)],
-               r=["UN0", "UN1"] + ["D%d" % b for b in range(4)], w=["z0"], b=["pm1"])
+            mm([(pc[:, 256:384], T.UN[:, 128 * u:128 * u + 128], T.D[:, u:256:2], u == 0, u == 1) for u in range(2)],
+               r=["UN0", "UN1"] + ["D%d" % b for b in range(4)], w=["z0"], b=["pc"])
             tt(T.t0[:, 0:128], T.nxi[:, 128:256], T.nxi[:, 0:128], A.add, 2, r=["nxi"], w=["al"])
             ts(T.t0[:, 128:256], T.t0[:, 0:128], 0.5, None, A.mult, r=["al"], w=["be"])
-            tt(T.YN[:, 0:128], T.t0[:, 128:256], pn[:, 256:384], A.subtract, r=["be", "z0"], w=["YNa"], b=["pm1"])
-            tt(T.YN[:, 128:256], T.t0[:, 128:256], pn[:, 256:384], A.add, r=["be", "z0"], w=["YNb"], b=["pm1"])
+            tt(T.YN[:, 0:128], T.t0[:, 128:256], pc[:, 256:384], A.subtract, r=["be", "z0"], w=["YNa"], b=["pc"])
+            tt(T.YN[:, 128:256], T.t0[:, 128:256], pc[:, 256:384], A.add, r=["be", "z0"], w=["YNb"], b=["pc"])
             dma(T.yn[:, :], T.YN[:, :], r=["YNa", "YNb"], size=4)
-        if t == 0:
-            mm([(ps[:, 0:16], T.ZR[:, :], T.FM[:, 0:16], True, True)], r=["ZR"] + FK, w=["T0"], b=["ps"])
+        mm([(ps[:, 0:16], T.ZR[:, :], T.FM[:, 0:16], True, True)], r=["ZR"] + FK, w=MK[2], b=["ps"])
 
         tol[0] = TWALK
         for k in range(16):
@@ -541,6 +589,7 @@ def rank_program(g, core, T, topo):
                 else:
                     gather("s", src, NL[:, :].indirect(T.Q[:, 16 * k - 16 + a:16 * k - 16 + b]), r=PK + [x[1] % k for x in nm], w=gk)
                 o = 256 * k
+                rank_[0] = UPX[3] if k == 0 else 0.0
                 op("v", lambda o=o, a=a, b=b, src=src: v.tensor_tensor_scan(T.SC[:, o + 16 * a:o + 16 * b], T.M[:, 16 * a:16 * b],
                                                                              src, 0.0, A.add, A.min),
                    r=["M"] + gk, w=[x[0] % k for x in nm], ns=16 * (b - a) * CY)
@@ -560,18 +609,26 @@ def rank_program(g, core, T, topo):
             rank_[0] = UPF if p < NUP else 0.0
             raw = T.SC[:, 256 * k0 + 15:256 * (k1 + 1):16]
             sk = [x % k for k in range(k0, k1 + 1) for x in ("SC%d", "SD%d")]
-            qa, qk = pc[:, 128 * (p % 2):128 * (p % 2) + wd], ["s%d" % (p % 2)]
+            qa, qk = pc[:, 128:128 + wd], ["s1"]
             mm([(pa[:, a:b], T.Bp[:, 15 - i:143 - i], G[:, 256 * (k0 + 1) + i:256 * (k1 + 2):16], i == 0, i == 15)
-                for i in range(16)], r=["Bp"] + ["Gp%d" % j for j in range(k0, k1 + 1)], w=["pc%d" % p, "m0", "m2"], b=["pm0"])
-            if SQA:
+                for i in range(16)], r=["Bp"] + ["Gp%d" % j for j in range(k0, k1 + 1)], w=["pc%d" % p, "m0"], b=["pm0"])
+            if SQA == 2:
+                op("s", lambda raw=raw, a=a, b=b: s.activation(T.RI[:, a:b], raw, F.Identity, bias=MAGIC), r=sk, w=["RI%d" % p], ns=cyc(qa))
+                act(T.DE[:, a:b], pa[:, a:b], r=["pc%d" % p], w=["DE%d" % p], b=["pm0"])
+                mm([(qa, T.IDf[:, :], T.MC[:, 0:wd], True, False)], 4, r=["IDf", "MC"], w=qk, b=["pc"])
+                mm([(qa, T.IDn[:, :], T.RI[:, a:b], False, False), (qa, T.IDf[:, :], raw, False, True)], 4,
+                   r=["IDn", "RI%d" % p] + sk, w=qk, b=["pc"])
+                tt(T.VC[:, a:b], T.DE[:, a:b], qa, A.mult, r=["DE%d" % p] + qk, w=["VC%d" % p], b=["pc"])
+            elif SQA:
                 op("s", lambda raw=raw, a=a, b=b: s.activation(T.RI[:, a:b], raw, F.Identity, bias=MAGIC), r=sk, w=["RI%d" % p], ns=cyc(qa))
                 op("s", lambda qa=qa, a=a, b=b: s.activation(qa, T.RI[:, a:b], F.Identity, bias=-MAGIC), r=["RI%d" % p], w=qk, b=["pc"],
                    ns=cyc(qa))
             else:
                 ts(qa, T.Q[:, a + 16:b + 16], nadj, None, A.add,
                    r=[x % (j + 1) for j in range(k0, k1 + 1) for x in ("Q%d", "QB%d")] + ["nadj"], w=qk, b=["pc"])
-            tt(T.DE[:, a:b], raw, qa, A.subtract, r=sk + qk, w=["DE%d" % p], b=["pc"])
-            tt(T.VC[:, a:b], T.DE[:, a:b], pa[:, a:b], A.mult, r=["DE%d" % p, "pc%d" % p], w=["VC%d" % p], b=["pm0"])
+            if SQA != 2:
+                tt(T.DE[:, a:b], raw, qa, A.subtract, r=sk + qk, w=["DE%d" % p], b=["pc"])
+                tt(T.VC[:, a:b], T.DE[:, a:b], pa[:, a:b], A.mult, r=["DE%d" % p, "pc%d" % p], w=["VC%d" % p], b=["pm0"])
             if TPE[p]:
                 k2 = max(k0, nk + 1)
                 base = [(ps[:, 16 * k2:16 + b], T.IDf[:, :], T.U[:, 16 * (k2 - nk - 1):b - 16 * nk], k2 == k0, False),
@@ -605,13 +662,16 @@ def rank_program(g, core, T, topo):
                     for d, k2, w_, o in grp], r=tk + ["U%d" % p], w=[key], b=["ps"], ns=sum(max(64, y[2]) * CY for y in grp))
                 mm([(pn[:, a:b], T.ID[:, :], T.OKK[:, 0:wd], True, False)][:x == 0]
                    + [(pn[:, 16 * (k2 - 1):b], T.ID[:, :], T.CM[:, o:o + w_], False, d == k1) for d, k2, w_, o in grp],
-                   r=[key, "ID", "OKK"], w=["pn%d" % p, "m1", "m3"], b=["pm1"])
+                   r=[key, "ID", "OKK"], w=["pn%d" % p, "m1"], b=["pm1"])
             cp(T.FI[:, a:b], pn[:, a:b], r=["pn%d" % p], w=["FI%d" % p], b=["pm1"])
             rank_[0] = UPF if p < NUPF else 0.0
             stream("s", "fetch%d_%d" % (t, p),
                    lambda a, b, k1=k1: move("s", T.NEW[:, 16 * a:16 * b], G[:, 0:256 * (k1 + 1)].indirect(T.FI[:, a:b])),
                    a, b, 4, GA, lambda c: ["G0", "G1", "FI%d" % p] + ["Gp%d" % k for k in range(1, k1)], lambda c: ["NEW%d" % c])
         tol[0], rank_[0] = TOL, 0.0
+        if not last:
+            for b in range(4):
+                begin(b, t + 1)
         stream("v", "store%d" % t, lambda a, b: v.tensor_copy(X[:, :].indirect(T.Q[:, a:b]), T.NEW[:, 16 * a:16 * b]),
                0, 240, 4, SCA, lambda c: ["NEW%d" % c, "Q%d" % (c // 16 + 1), "QB%d" % (c // 16 + 1)], lambda c: XK)
 

from concourse.mybir import AluOpType as A, ActivationFunctionType as F

R = 4
V = 4096
W = 4352
ST = 256
XW = V + 15 * ST
ZW = 280
PARTS = [(1, 2), (3, 5), (6, 8), (9, 12), (13, 15)]
TPE = (1, 1, 1, 1, 1, 1)
HALVES = 7
VCOL = 3
CG = 5
PRE0 = 1
TINY = 2.0 ** -60
WR = 0.0
PASSES, MIX, TBACK, TMIN, TMAX, SLK, BSL, FAR = 4, 1.0, 60, 150, 900, 1.4, True, 3000.0
SQA, SY, MAGIC = True, True, 1.5 * 2.0 ** 23
NX0 = (64, 64, 32, 32)
NXV = (32, 32, 32, 32)
SUMV = (1, 1, 0, 0)
UPX, VFIRST = (0.0, 0.0, 0.0, 0.0), (0, 3)
YQ = ("y",)
LAT, CY, PE, GA, SCA, MINP = 140, 0.92, 0.66, 1.37, 2.9, 170
DFIX, DROW, DBW, RFIX, RFIRST = 800.0, 400.0, 260.0, 1300.0, 2500.0
TOL = {"v": 60, "s": 60, "t": 60, "g": 600, "y": 60, "a": 0}
TX = {"v": 700, "s": 200, "t": 400}
TWALK = {"v": 150, "s": 250}
TFEET = {"v": 250, "s": 300, "t": 100}
TLAST = {"v": 250, "s": 100, "t": 60}
CAP = {"fetc": 500}
UPF, NUP, NUPF, LD = 3e4, 3, 0, (8, 7, 9, 6, 5, 4)
BOOST, AHEAD, DEPTH, MANY, EXTRA = 3000.0, 0, 6, 99, 300.0

SCRATCH = {
    "X": ("sbuf", [128, XW], "bfloat16"), "XO": ("sbuf", [128, W + V], "bfloat16"), "G": ("sbuf", [128, W], "bfloat16"),
    "NL": ("sbuf", [128, XW], "float32"), "ZG": ("sbuf", [128, V], "bfloat16"),
    "SC": ("sbuf", [128, 4096], "float32"), "GW": ("sbuf", [128, 256], "float32"),
    "NEW": ("sbuf", [128, 3840], "bfloat16"), "SUM": ("sbuf", [128, 2048], "float32"),
    "SB": ("sbuf", [128, ZW], "bfloat16"), "ZB": ("sbuf", [128, ZW], "bfloat16"),
    "KO": ("sbuf", [128, 512], "bfloat16"), "ZK": ("sbuf", [128, 512], "float32"),
    "nxi": ("sbuf", [128, 256], "int32"), "lei": ("sbuf", [128, 512], "int32"), "voi": ("sbuf", [128, 256], "int32"),
    "lai": ("sbuf", [128, 96], "int32"), "nui": ("sbuf", [128, 4], "int32"),
    "IP": ("sbuf", [128, 4], "int32"), "IQ": ("sbuf", [128, 4], "int32"), "col": ("sbuf", [128, 16], "float32"),
    "IX": ("sbuf", [128, 144], "float32"), "J": ("sbuf", [128, 128], "float32"), "K8": ("sbuf", [128, 128], "float32"),
    "RM": ("sbuf", [128, 16], "float32"), "IDf": ("sbuf", [128, 128], "float32"), "ID": ("sbuf", [128, 128], "bfloat16"),
    "ZR": ("sbuf", [128, 128], "bfloat16"), "BO": ("sbuf", [128, 128], "bfloat16"), "FM": ("sbuf", [128, 1024], "bfloat16"),
    "OKK": ("sbuf", [128, 512], "bfloat16"), "WL": ("sbuf", [128, 144], "bfloat16"), "WH": ("sbuf", [128, 144], "bfloat16"),
    "DU": ("sbuf", [128, 256], "float32"), "UN": ("sbuf", [128, 256], "bfloat16"),
    "Bf": ("sbuf", [128, 152], "float32"), "B2": ("sbuf", [128, 144], "float32"), "Bw": ("sbuf", [128, 144], "bfloat16"),
    "Bz": ("sbuf", [128, 144], "bfloat16"), "Bp": ("sbuf", [128, 144], "bfloat16"), "M": ("sbuf", [128, 256], "float32"),
    "LK": ("sbuf", [128, 96], "float32"), "t0": ("sbuf", [128, 256], "float32"), "t1": ("sbuf", [128, 256], "float32"),
    "t4": ("sbuf", [128, 64], "float32"), "i0": ("sbuf", [128, 256], "int32"), "i1": ("sbuf", [128, 256], "int32"),
    "i2": ("sbuf", [128, 256], "int32"), "By": ("sbuf", [128, 144], "bfloat16"), "C1": ("sbuf", [128, 256], "bfloat16"),
    "LP": ("sbuf", [128, 1280], "bfloat16"), "PC": ("sbuf", [128, 1024], "bfloat16"),
    "Lx": ("sbuf", [128, 256], "uint16"), "Lz": ("sbuf", [128, 256], "uint16"),
    "Q": ("sbuf", [128, 256], "uint16"), "FI": ("sbuf", [128, 240], "uint16"),
    "H": ("sbuf", [128, 256], "float32"), "E": ("sbuf", [128, 256], "float32"), "F0": ("sbuf", [128, 256], "float32"),
    "F1": ("sbuf", [128, 256], "float32"), "D": ("sbuf", [128, 256], "bfloat16"), "XD": ("sbuf", [128, 1024], "bfloat16"),
    "TM": ("sbuf", [128, 256], "float32"), "RI": ("sbuf", [128, 240], "float32"),
    "IDn": ("sbuf", [128, 128], "float32"), "MC": ("sbuf", [128, 96], "float32"),
    "DE": ("sbuf", [128, 240], "float32"), "VC": ("sbuf", [128, 240], "float32"), "U": ("sbuf", [128, 240], "float32"),
    "CM": ("sbuf", [128, 1920], "bfloat16"), "YN": ("sbuf", [128, 256], "float32"),
    "pp0": ("psum", [128, 512], "float32"), "pp1": ("psum", [128, 512], "float32"), "pp2": ("psum", [128, 512], "float32"),
    "pp3": ("psum", [128, 512], "float32"), "pm0": ("psum", [128, 512], "float32"), "pm1": ("psum", [128, 512], "float32"),
    "pc": ("psum", [128, 512], "float32"), "ps": ("psum", [128, 512], "float32"),
}
for _t in range(R):
    SCRATCH["AR%d" % _t] = ("sbuf", [128, 256], "bfloat16")
NDMA = 56
SEMAPHORES = (["cv", "cs", "ct", "cg", "zarr"] + ["arr%d" % t for t in range(R)] + ["sent%d" % t for t in range(R + 1)]
              + ["d%d" % k for k in range(NDMA)])
ORDER = []


def order(ops):
    n = len(ops)
    succ = [[] for _ in ops]
    for i, o in enumerate(ops):
        for p in o["pre"]:
            succ[p].append(i)
    pri = [0.0] * n
    for i in range(n - 1, -1, -1):
        o = ops[i]
        pri[i] = ((1.0 if o["range"] else o["lat"]) + o["up"]
                  + max([pri[j] + (LAT if ops[j]["pre"][i] and ops[j]["stream"] != o["stream"] else 0) for j in succ[i]] + [0.0]))
    pri = [x + o["rank"] for x, o in zip(pri, ops)]
    best = None
    for _ in range(PASSES):
        out, fin = one_pass(ops, succ, list(pri), best is not None and TMAX > 0)
        if best is None or max(fin) < best[1]:
            best = (out, max(fin))
        if PASSES > 1:
            back = [dict(ops[n - 1 - i], pre={n - 1 - j: ops[j]["pre"][n - 1 - i] for j in succ[n - 1 - i]}, tol=TBACK) for i in range(n)]
            bs = [[n - 1 - p for p in ops[n - 1 - i]["pre"]] for i in range(n)]
            late = one_pass(back, bs, [fin[n - 1 - i] for i in range(n)], BSL)[1]
            pri = [MIX * (late[n - 1 - i] + WR * ops[i]["rank"]) + (1 - MIX) * pri[i] for i in range(n)]
    return best[0]


def one_pass(ops, succ, pri, slack=False):
    n = len(ops)
    pri0, ahead = list(pri), [0]
    kind = [str(o["stream"])[:4] for o in ops]
    left = [len(o["pre"]) for o in ops]
    fin = [None] * n
    free = {e: 0.0 for e in "vstgya"}
    bank = {}
    ready = set(i for i in range(n) if left[i] == 0)
    out = []
    dfree = 0.0

    base = [0.0] * n
    gap = [[(j, {True: LAT, False: 0.0, None: -1e18}[ops[j]["pre"][i]]) for j in succ[i]] for i in range(n)]
    whole = [o["lat"] + o["fix"] for o in ops]

    def start(i, t):
        o = ops[i]
        t = max(t, free[o["e"]])
        for k in o["b"]:
            for e2, j in bank.get(k, {}).items():
                if e2 != o["e"]:
                    t = max(t, fin[j] + LAT)
        return t

    def done(i, t):
        fin[i] = t
        ready.discard(i)
        for j, d in gap[i]:
            left[j] -= 1
            base[j] = max(base[j], t + d)
            if left[j] == 0:
                ready.add(j)

    while ready:
        st = {i: start(i, base[i]) for i in ready}
        i0 = min(st, key=lambda i: (st[i], -pri[i]))
        e, now = ops[i0]["e"], st[i0]
        front, seen, at = list(ready), {}, {}
        for i in ready:
            if kind[i] == "fetc":
                pri[i] = pri0[i] + (BOOST if ahead[0] < AHEAD else 0.0)
        for _ in range(DEPTH):
            nxt = []
            for i in front:
                t = st[i] + whole[i]
                if t < now + FAR:
                    for j, d in gap[i]:
                        seen[j] = seen.get(j, 0) + 1
                        at[j] = max(at.get(j, base[j]), t + d)
                        if seen[j] == left[j]:
                            st[j] = start(j, at[j])
                            nxt.append(j)
            front = nxt
        mine = [i for i in st if ops[i]["e"] == e]
        can = sorted([i for i in mine if i in ready and st[i] <= now + 1], key=lambda i: (-pri[i], i))
        pick = None
        top = max(pri[j] + st[j] for j in st)
        for i in can:
            lim = min([st[j] + (ops[j]["tol"] if not slack else min(TMAX, max(TMIN, SLK * (top - pri[j] - st[j])))) for j in mine
                       if pri[j] > pri[i] and st[j] > now + 1 and ops[j]["stream"] != ops[i]["stream"]] + [1e18])
            o = ops[i]
            if kind[i] == "stor" and ahead[0] >= MANY:
                lim += EXTRA
            need = o["fix"] + max(o["ns"], MINP if o["range"] else 0)
            if now + need <= lim:
                pick = (i, lim)
                break
        if pick is None:
            free[e] = min(st[j] for j in mine if st[j] > now + 1)
            continue
        i, lim = pick
        o = ops[i]
        grp, t = [i], now + o["fix"] + o["ns"]
        pre = dict(o["pre"])
        while o["range"]:
            j = grp[-1] + 1
            if j >= n or ops[j]["stream"] != o["stream"] or fin[j] is not None or t + ops[j]["ns"] > min(lim, now + o["cap"]):
                break
            if any(p not in grp and (fin[p] is None or fin[p] + (LAT if h else 0) > now + 1) for p, h in ops[j]["pre"].items()):
                break
            grp.append(j)
            t += ops[j]["ns"]
            for p, h in ops[j]["pre"].items():
                if p not in grp:
                    pre[p] = pre.get(p, False) or h
        for k in o["b"]:
            for e2, j in bank.get(k, {}).items():
                if e2 != e:
                    pre[j] = True
            bank.setdefault(k, {})[e] = grp[-1]
        free[e] = t
        ahead[0] += len(grp) * {"fetc": 1, "stor": -1}.get(kind[i], 0)
        end = t + o["lat"] - o["ns"]
        if o["kind"] == "d":
            dfree = max(dfree, now + 0.6 * DFIX) + o["lat"] - DFIX
            end = dfree + 0.4 * DFIX
        for j in grp:
            done(j, end)
        out.append((grp, pre))
    return out, fin


def rank_program(g, core, T, topo):
    rank = T.rank_of(core)
    if rank is None:
        return
    n = len(T.cores)
    nxt, prv = T.cores[(rank + 1) % n], T.cores[(rank - 1) % n]
    v, s, pe = g.vector, g.scalar, g.tensor
    Q = {"v": v, "s": s, "t": pe, "g": g, "y": g.sync}
    ops, wr, rd = [], {}, {}
    tol, lastg, rank_ = [TOL], [None], [0.0]

    def put(e, kind, fn, r, w, b, ns, lat=None, fix=0.0, stream=None, rng=None, sem=None, up=0.0):
        i = len(ops)
        pre = {}

        def add(p):
            pre[p] = not (e == "t" and ops[p]["e"] == "t")
        for k in r:
            assert k in wr, k
            add(wr[k])
        for k in w:
            if k in wr:
                add(wr[k])
            for p in rd.get(k, []):
                add(p)
        for k in r:
            rd.setdefault(k, []).append(i)
        for k in w:
            wr[k] = i
            rd[k] = []
        ops.append({"e": e, "kind": kind, "fn": fn, "pre": pre, "b": list(b), "ns": ns, "lat": ns if lat is None else lat,
                    "fix": fix, "stream": stream or i, "range": rng, "sem": sem, "up": up, "rank": rank_[0],
                    "tol": tol[0][e], "cap": CAP.get((stream or "")[:4], 1e9)})
        if e == "g":
            if lastg[0] is not None:
                pre.setdefault(lastg[0], None)
            lastg[0] = i

    def op(e, fns, r=(), w=(), b=(), ns=60.0, up=0.0):
        put(e, "c", fns if isinstance(fns, list) else [fns], r, w, b, ns, up=up)

    def stream(e, name, fn, a, b, unit, el, r, w):
        for c in range(a, b, unit):
            put(e, "c", fn, r(c), w(c), (), 16 * unit * el, None, 60.0, name, (c, c + unit))

    def dma(out, in_, r=(), w=(), up=0.0, size=2, e="y"):
        put(e, "d", lambda: Q[e].dma_start(out, in_), r, w, (), 60.0, DFIX + DROW + 128 * out.shape[1] * size / DBW, up=up)

    def lanes(src, dst):
        es = topo.engines(src, dst)[::2]
        m = 0
        for x in es:
            m |= 1 << x
        return m, len(es)

    def send(dst, out, in_, sem, sent, r, first=0.0):
        m, k = lanes(core, dst)
        rid, pid, _ = topo.addr(dst)
        put("g", "r", lambda: g.remote_dma(out, in_, T.sem[sem], T.sem[sent], pid, rid, m), r, [sent], (), 300.0 + first,
            RFIX + first, sem=(sent, k))

    def arrive(src, sem, sent, key):
        put("a", "a", None, [sent], [key], (), 0.0, sem=(sem, lanes(src, core)[1]))

    def cyc(a, two=1):
        return max(64, a.shape[1] * two) * CY

    def ts(out, in0, s1, s2, o0, o1=None, two=1, **k):
        if o1 is None:
            op("v", lambda: v.tensor_scalar(out, in0, s1, None, o0), ns=cyc(out, two), **k)
        else:
            op("v", lambda: v.tensor_scalar(out, in0, s1, s2, o0, o1), ns=cyc(out, two), **k)

    def tt(out, a, b_, o, two=1, **k):
        op("v", lambda: v.tensor_tensor(out, a, b_, o), ns=cyc(out, two), **k)

    def cp(out, a, **k):
        op("v", lambda: v.tensor_copy(out, a), ns=cyc(out), **k)

    def ms(out, c, **k):
        op("v", lambda: v.memset(out, c), ns=cyc(out, 0.5), **k)

    def act(out, a, **k):
        op("s", lambda: s.activation(out, a, F.Copy), ns=cyc(out), **k)

    def move(e, out, a):
        return v.tensor_copy(out, a) if e == "v" else s.activation(out, a, F.Copy)

    def gather(e, out, a, **k):
        op(e, lambda: move(e, out, a), ns=60 + GA * out.shape[1], **k)

    def mm(lst, f32=1, **k):
        k["w"] = list(k["w"]) + ["group " + k["b"][0]]
        op("t", [(lambda a=a: pe.matmul(*a)) for a in lst], ns=sum(PE * f32 * max(64, a[0].shape[1]) for a in lst), **k)

    def iota(out, pat, base, cm, key, flt=True):
        ns = 130 + 2 * CY * out.shape[1]
        if flt:
            op("g", lambda: g.iota(out, pat, base, cm, allow_small_or_imprecise_dtypes=True), w=[key], ns=ns)
        else:
            op("g", lambda: g.iota(out, pat, base, cm), w=[key], ns=ns)

    X, G, XO, NL, ZG = T.X, T.G, T.XO, T.NL, T.ZG
    AR = [T["AR%d" % t] for t in range(R)]
    pp = [T.pp0, T.pp1, T.pp2, T.pp3]
    pa, pn, ps, pc = T.pm0, T.pm1, T.ps, T.pc
    BK, BN = [pa[:, 0:128], pn[:, 0:128], ps[:, 0:128], pc[:, 0:128]], ["pm0", "pm1", "ps", "pc"]
    XK = ["Xb", "Xt"]
    XN = ["XN%d" % c for c in range(0, 256, 8)]
    PK = ["P0%d" % b for b in range(4)] + ["P1%d" % b for b in range(4)] + ["tail"]
    pf, pi, pi1, pg, adj, wf, lo, hi, p8, k8, k88, r8, pm8 = [T.col[:, k:k + 1] for k in range(13)]
    nadj = T.col[:, 13:14]
    NP = len(PARTS)
    NMAX = max(k1 - k0 + 1 for k0, k1 in PARTS)
    AK, NK = ["pc%d" % p for p in range(NP)], ["pn%d" % p for p in range(NP)]
    TK = ["T%d" % j for j in range(16)]
    MK = [["m0"] + AK, ["m1"] + NK, ["m2"] + TK, ["m3", "s0"]]

    def repeat(buf, width, key, size):
        a = 16
        while a < width:
            b = min(2 * a, width)
            dma(buf[:, a:b], buf[:, 0:b - a], r=[key], w=[key], size=size)
            a = b

    dma(T.nui[:, 0:1], T.nu[:, :], w=["nui"], up=LD[0] * 1e5)
    dma(T.SB[:, 16:272], T.x[:, 0:256], w=["SBa"], up=LD[1] * 1e5)
    dma(T.nxi[:, :], T.nx[:, :], w=["nxi"], up=LD[2] * 1e5, size=4)
    dma(T.voi[:, :], T.vol[:, :], w=["voi"], size=4, up=LD[3] * 1e5)
    dma(X[:, 256:W], T.x[:, 256:W], w=["Xb"], up=LD[4] * 1e5)
    dma(T.lei[:, :], T.le[:, :], w=["lei"], size=4, up=LD[5] * 1e5)
    dma(T.lai[:, 0:16], T.lag[:, :], w=["lai"], size=4)
    dma(G[:, 256:512], T.x[:, 0:256], w=["G1"])
    dma(XO[:, 0:W], T.x[:, :], w=["XO"])
    iota(T.IP[:, 0:1], [[1, 1]], 0, 1, "IP", False)
    iota(T.IX[:, :], [[1, 144]], 0, 0, "IX")
    iota(T.J[:, :], [[16, 8], [0, 16]], 0, 0, "J")
    ms(T.SB[:, 0:16], 0.0, w=["SBb"])
    ms(T.SB[:, 272:ZW], 0.0, w=["SBd"])
    ms(T.ZR[:, :], 0.0, w=["ZR"])
    ms(T.Bf[:, 0:8], 0.0, w=["Bf0"])
    ts(T.IQ[:, 0:1], T.IP[:, 0:1], 15, None, A.bitwise_and, r=["IP"], w=["IQ"])
    ts(T.IQ[:, 1:2], T.IP[:, 0:1], 7, None, A.bitwise_and, r=["IP"], w=["IQ8"])
    cp(pf, T.IP[:, 0:1], r=["IP"], w=["pf"])
    cp(pi, T.IQ[:, 0:1], r=["IQ"], w=["pi"])
    cp(r8, T.IQ[:, 1:2], r=["IQ8"], w=["r8"])
    tt(pg, pf, pi, A.subtract, r=["pf", "pi"], w=["pg"])
    ts(pi1, pi, 1.0, None, A.add, r=["pi"], w=["pi1"])
    ts(adj, pi, 15.0, 16384.0, A.is_lt, A.mult, r=["pi"], w=["adj"])
    ts(nadj, pi, 15.0, -16384.0, A.is_lt, A.mult, r=["pi"], w=["nadj"])
    ts(lo, pi, 8.0, None, A.is_lt, r=["pi"], w=["lo"])
    ts(hi, pi, 8.0, None, A.is_ge, r=["pi"], w=["hi"])
    ts(p8, pf, 8.0, None, A.add, r=["pf"], w=["p8"])
    ts(pm8, pf, -8.0, None, A.add, r=["pf"], w=["pm8"])
    tt(k8, pg, r8, A.add, r=["pg", "r8"], w=["k8"])
    ts(k88, k8, 8.0, None, A.add, r=["k8"], w=["k88"])
    ts(T.RM[:, 0:8], T.IX[:, 0:8], r8, -1.0, A.is_equal, A.mult, r=["IX", "r8"], w=["RM"])
    ts(T.BO[:, :], T.J[:, :], pg, None, A.is_equal, r=["J", "pg"], w=["BO"])
    for q in range(2):
        op("s", [(lambda i=i: s.activation(T.FM[:, 128 * i:128 * i + 128], T.BO[:, :], F.Identity, scale=T.RM[:, i:i + 1]))
                 for i in range(4 * q, 4 * q + 4)], r=["BO", "RM"], w=["FM%d" % q], ns=4 * 128 * CY)
    FK = ["FM0", "FM1"]
    ts(T.WL[:, :], T.IX[:, :], p8, lo, A.is_equal, A.mult, r=["IX", "p8", "lo"], w=["WL"])
    ts(T.WH[:, :], T.IX[:, :], p8, hi, A.is_equal, A.mult, r=["IX", "p8", "hi"], w=["WH"])
    ts(T.Bf[:, 8:152], T.IX[:, :], -15.0, pg, A.add, A.is_equal, r=["IX", "pg"], w=["Bf"])
    tt(T.B2[:, :], T.Bf[:, 8:152], T.Bf[:, 0:144], A.add, 2, r=["Bf", "Bf0"], w=["B2"])
    ts(T.ID[:, :], T.IX[:, 0:128], pf, 256.0, A.is_equal, A.mult, r=["IX", "pf"], w=["ID"])
    ts(T.IDf[:, :], T.IX[:, 0:128], pf, None, A.is_equal, r=["IX", "pf"], w=["IDf"])
    if SQA == 2:
        ts(T.IDn[:, :], T.IX[:, 0:128], pf, -1.0, A.is_equal, A.mult, r=["IX", "pf"], w=["IDn"])
        ms(T.MC[:, :], MAGIC, w=["MC"])
    ts(T.UN[:, 0:128], T.IX[:, 0:128], k8, 0.5, A.is_equal, A.mult, r=["IX", "k8"], w=["UN0"])
    ts(T.UN[:, 128:256], T.IX[:, 0:128], k88, 0.5, A.is_equal, A.mult, r=["IX", "k88"], w=["UN1"])
    ts(T.t4[:, 0:16], T.IX[:, 0:16], pi, 32768.0, A.is_equal, A.mult, r=["IX", "pi"], w=["t4"])
    ts(T.t4[:, 16:32], T.IX[:, 0:16], pi1, -16384.0, A.is_equal, A.mult, r=["IX", "pi1"], w=["t5"])
    tt(T.M[:, 0:16], T.t4[:, 0:16], T.t4[:, 16:32], A.add, r=["t4", "t5"], w=["M"])
    repeat(T.M, 256, "M", 4)
    ts(T.t4[:, 32:48], T.IX[:, 0:16], 16.0, pi, A.mult, A.add, r=["IX", "pi"], w=["OL"])
    ts(T.OKK[:, 0:16], T.t4[:, 32:48], 1.0 / 256, None, A.mult, r=["OL"], w=["OKK"])
    repeat(T.OKK, 16 * NMAX, "OKK", 2)
    cp(T.SB[:, 272:273], T.nui[:, 0:1], r=["nui", "SBd"], w=["SBc"])
    send(prv, T.ZB[:, :], T.SB[:, :], "zarr", "sent%d" % R, ["SBa", "SBb", "SBc"], RFIRST)
    arrive(nxt, "zarr", "sent%d" % R, "ZB")
    iota(T.K8[:, :], [[16, 8], [0, 2], [1, 8]], 0, 0, "K8")
    send(nxt, AR[0][:, :], X[:, V:W], "arr0", "sent0", ["Xb"])
    arrive(prv, "arr0", "sent0", "AR0")
    iota(NL[:, V:XW], [[1, XW - V]], V + ST, 0, "tail")
    ts(T.DU[:, 0:128], T.K8[:, :], pf, 0.5, A.is_equal, A.mult, r=["K8", "pf"], w=["DU0"])
    ts(T.DU[:, 128:256], T.K8[:, :], pm8, 0.5, A.is_equal, A.mult, r=["K8", "pm8"], w=["DU1"])
    cp(wf, T.nui[:, 0:1], r=["nui"], w=["wf"])
    ts(T.Bw[:, :], T.B2[:, :], wf, None, A.mult, r=["B2", "wf"], w=["Bw"])
    ts(T.Bz[:, :], T.B2[:, :], T.ZB[:, 272:273], None, A.mult, r=["B2", "ZB"], w=["Bz"])
    ts(T.By[:, :], T.Bz[:, :], 1 / TINY, None, A.mult, two=0.5, r=["Bz"], w=["By"])
    ms(T.C1[:, 0:128], 1.0 / 256, w=["C1"])
    ms(T.C1[:, 128:256], -1.0 / 256, w=["C2"])
    ts(T.Bp[:, :], T.Bf[:, 8:152], wf, 512.0, A.mult, A.mult, r=["Bf", "wf"], w=["Bp"])
    cp(T.LK[:, 0:16], T.lai[:, 0:16], r=["lai"], w=["LK"])
    repeat(T.LK, 16 * NMAX, "LK", 4)
    ts(T.i2[:, :], T.nxi[:, :], V - 1, None, A.bitwise_and, r=["nxi"], w=["i2"])
    cp(T.Lx[:, :], T.i2[:, :], r=["i2"], w=["Lx"])
    ts(T.Lz[:, :], T.nxi[:, :], 16.0 - V, 0.0, A.add, A.max, r=["nxi"], w=["Lz"])
    LP, PC = T.LP, T.PC
    rank_[0] = 2e4
    ts(T.i0[:, :], T.nxi[:, :], 0x1FC0, None, A.bitwise_and, r=["nxi"], w=["i0"])
    ts(T.i1[:, :], T.nxi[:, :], 63, None, A.bitwise_and, r=["nxi"], w=["i1"])
    cp(LP[:, 0:256], T.i0[:, :], r=["i0"], w=["Lhi"])
    cp(LP[:, 256:512], T.i1[:, :], r=["i1"], w=["Llo"])
    ts(LP[:, 768:1024], T.voi[:, :], 1.0 / 512, None, A.mult, r=["voi"], w=["Lv"])
    rank_[0] = 0.0
    ts(LP[:, 1024:1280], LP[:, 0:256], float(V), None, A.is_ge, two=0.5, r=["Lhi"], w=["Lk"])
    up_ = [T.WL[:, 8:136], T.WH[:, 16:144]]
    dn_ = [T.WL[:, 0:128], T.WH[:, 8:136]]

    def double(bank, o, terms, keys, key, name):
        mm([(bank[:, o + u:o + 256:2], m[u], LP[:, c:c + 128], j == 0, j == len(terms) - 1)
            for u in range(2) for j, (m, c) in enumerate(terms)], r=keys + ["WL", "WH"], w=key, b=[name])

    hl = ["Lhi", "Llo"]
    c0, c1, a0, a1, n0 = ["m3", "s0", "s1"], ["z0", "z1"], ["m0", "sa", "sb"] + AK, ["x%d" % b for b in range(4)], ["m1"] + NK
    EK = ["EP%d" % b for b in range(4)]
    rank_[0] = 2e4
    double(pc, 0, [(up_, 0), (up_, 128), (dn_, 256), (dn_, 384)], hl, c0, "pc")
    double(pc, 256, [(up_, 768), (up_, 896)], ["Lv"], c1, "pc")
    op("s", lambda: s.activation(PC[:, 0:512], pc[:, :], F.Identity, scale=-1.0), r=c0 + c1, w=["PC0"], b=["pc"], ns=512 * CY)
    rank_[0] = 1.5e4
    double(pa, 0, [(up_, 128), (dn_, 384)], hl, a0, "pm0")
    double(pa, 256, [(up_, 896)], ["Lv"], a1, "pm0")
    op("s", lambda: s.activation(PC[:, 512:1024], pa[:, :], F.Identity, scale=-1.0), r=a0 + a1, w=["PC1"], b=["pm0"], ns=512 * CY)
    rank_[0] = 0.0
    ts(LP[:, 512:768], PC[:, 512:768], -2.0, None, A.mult, two=0.5, r=["PC1"], w=["L2"])
    tt(T.D[:, :], PC[:, 0:256], LP[:, 512:768], A.add, 2, r=["PC0", "L2"], w=["D%d" % b for b in range(4)])

    def spread(b, srcs, keys, how):
        lst = []
        if how == "open":
            mm([(pp[b][:, :], T.ZR[:, :], T.FM[:, 0:512], True, False)], r=FK + ["ZR"], w=["pp%d" % b], b=["pp%d" % b])
            for src in srcs:
                spread(b, [src], keys, "more")
            return
        for r in range(8):
            for j, src in enumerate(srcs):
                lst.append((pp[b][:, r:512:8], T.FM[:, 128 * r:128 * r + 128], src[:, 64 * b:64 * b + 64], how == "whole" and j == 0,
                            j == len(srcs) - 1 and (how == "whole" or how == "close" and r == 7)))
        mm(lst, r=keys + FK + ["ZR"], w=["pp%d" % b], b=["pp%d" % b])

    def before(b, t):
        spread(b, [PC[:, 512:768], PC[:, 768:1024]], ["PC1"], "open")

    for b in range(4):
        rank_[0] = 1e4 - 1e3 * b
        spread(b, [PC[:, 0:256], PC[:, 256:512]], ["PC0"], "whole")
        rank_[0] = 1e4 if b < PRE0 else 0.0
        (act, cp)[SUMV[b]](T.SUM[:, 512 * b:512 * b + 512], pp[b][:, :], r=["pp%d" % b], w=["SUM%d" % b], b=["pp%d" % b])
        if b < PRE0:
            before(b, 0)
    rank_[0] = 0.0
    tt(T.t0[:, 0:128], T.lei[:, 256:384], T.lei[:, 0:128], A.subtract, 2, r=["lei"], w=["al"])
    tt(T.t0[:, 128:256], T.lei[:, 128:256], T.lei[:, 384:512], A.subtract, 2, r=["lei"], w=["be"])
    tt(T.t1[:, 0:128], T.t0[:, 0:128], T.t0[:, 128:256], A.add, 2, r=["al", "be"], w=["t1a"])
    tt(T.t1[:, 128:256], T.t0[:, 0:128], T.t0[:, 128:256], A.subtract, 2, r=["al", "be"], w=["t1b"])
    mm([(ps[:, 256 * a + u:256 * a + 256:2], T.DU[:, 128 * u:128 * u + 128], T.t1[:, 128 * a:128 * a + 128], True, True)
        for a in range(2) for u in range(2)], 4, r=["t1a", "t1b", "DU0", "DU1"], w=TK + EK, b=["ps"])
    rank_[0] = 2e4
    act(T.H[:, :], ps[:, 0:256], r=["T0"], w=["H"], b=["ps"])
    rank_[0] = 0.0

    def factors(b):
        c = 64 * b
        ep = ps[:, 256 + c:320 + c]
        op("v", [lambda: v.tensor_tensor(T.F0[:, c:c + 64], T.H[:, c:c + 64], ep, A.add),
                 lambda: v.tensor_tensor(T.F1[:, c:c + 64], ep, T.H[:, c:c + 64], A.subtract)],
           r=["H", "EP%d" % b], w=["F%d" % b], b=["ps"], ns=120)

    for b in range(4):
        factors(b)

    def content(src, o, lhs, b, key, keys, out, w, bank, whole=False, more=()):
        mm([(out[:, 64 * a:64 * a + 64], lhs[:, 15 - r:143 - r], src[:, o + 2048 * a + 512 * b + r:o + 2048 * a + 512 * b + 512:8],
             whole and r == 0, whole and r == 7) for a in range(2) for r in range(8)] + list(more),
           r=keys + [key % (c + x) for c in (32 * b, 128 + 32 * b) for x in range(0, 32, 8)], w=w, b=[bank])

    def begin(b, t):
        mm([(BK[b], T.ID[:, :], T.C1[:, 0:128], True, False)], r=["ID", "C1"], w=MK[b], b=[BN[b]])
        if t == 0:
            content(ZG, 0, T.Bz, b, "Z%d", ["Bz"], BK[b], MK[b][:1], BN[b])
        else:
            mm([(BK[b], T.IDf[:, :], T.ZK[:, 128 * b:128 * b + 128], False, False)], 4, r=["IDf", "ZK%d" % b], w=MK[b][:1], b=[BN[b]])

    def sides(out, in0, in1, o, q, **k):
        op("v", [(lambda a=a: v.tensor_tensor(out[:, 64 * a:64 * a + 64], in0[:, 256 * a + 64 * q:256 * a + 64 * q + 64],
                                              in1[:, 64 * a:64 * a + 64], o)) for a in range(2)], ns=120, **k)

    for b in range(4):
        for c in (32 * b, 128 + 32 * b):
            gather("s", ZG[:, 16 * c:16 * c + 512], T.ZB[:, 0:272].indirect(T.Lz[:, c:c + 32]), r=["ZB", "Lz"],
                   w=["Z%d" % x for x in range(c, c + 32, 8)])
        begin(b, 0)

    for t in range(R):
        last = t == R - 1
        if not last:
            ts(X[:, 0:256], X[:, V:W], TINY, None, A.mult, two=0.5, r=["Xb"], w=["Xt"])
        if t > 0:
            send(nxt, AR[t][:, :], X[:, V:W], "arr%d" % t, "sent%d" % t, ["Xb"])
            arrive(prv, "arr%d" % t, "sent%d" % t, "AR%d" % t)
            dma(XO[:, 256:V], X[:, 256:V], r=["Xb"], w=["XO"])
            dma(G[:, 256:512], AR[t - 1][:, :], r=["AR%d" % (t - 1)], w=["G1"])
        dma(G[:, 0:256], AR[t][:, :], r=["AR%d" % t], w=["G0"])
        if last:
            dma(T.y[:, 0:256], AR[t][:, :], r=["AR%d" % t])
        for b in range(4):
            h, u, c = b // 2, b % 2, 64 * b
            cols = list(range(32 * b, 32 * b + 32, 8)) + list(range(128 + 32 * b, 160 + 32 * b, 8))
            nv = (NX0[b] if t == 0 else NXV[b]) // 8
            for e, cs in (("v", cols[:nv]), ("s", cols[nv:])):
                for run in ([x for x in cs if x < 128], [x for x in cs if x >= 128]):
                    if run:
                        gather(e, XO[:, W + 16 * run[0]:W + 16 * run[-1] + 128], X[:, 0:V].indirect(T.Lx[:, run[0]:run[-1] + 8]),
                               r=XK + ["Lx"], w=["XN%d" % x for x in run])
            m, x1 = BK[b], pa[:, 256 + c:320 + c]
            content(XO, W, T.Bw, b, "XN%d", ["Bw", "C2"], m, MK[b][:1], BN[b], more=[(m, T.ID[:, :], T.C1[:, 128:256], False, True)])
            rank_[0], tol[0] = UPX[0], TX
            op("v", [lambda c=c, m=m: v.tensor_tensor(T.TM[:, c:c + 64], T.F0[:, c:c + 64], m[:, 0:64], A.mult),
                     lambda c=c, m=m: v.tensor_tensor(m[:, 64:128], T.F1[:, c:c + 64], m[:, 64:128], A.mult)],
               r=["m%d" % b, "F%d" % b], w=["TM%d" % b, "m%d" % b], b=[BN[b]], ns=120)
            tt(x1, T.TM[:, c:c + 64], m[:, 64:128], A.is_lt, r=["TM%d" % b, "m%d" % b], w=["x%d" % b], b=["pm0", BN[b]])
            tt(T.XD[:, 256 * t + c:256 * t + c + 64], T.D[:, c:c + 64], x1, A.mult, r=["x%d" % b, "D%d" % b], w=["XD%d_%d" % (t, b)], b=["pm0"])
            rank_[0] = UPX[1]
            if t == 0 and b >= PRE0:
                spread(b, [PC[:, 512:768], PC[:, 768:1024], T.XD[:, 0:256]], ["PC1", "XD0_%d" % b], "whole")
            else:
                spread(b, [T.XD[:, 256 * t:256 * t + 256]], ["XD%d_%d" % (t, b)], "close")
            o = 512 * b
            rank_[0] = UPX[2]
            tt(NL[:, o:o + 512], T.SUM[:, o:o + 512], pp[b][:, :], A.subtract, r=["pp%d" % b, "SUM%d" % b], w=["P0%d" % b], b=["pp%d" % b])
            rank_[0] = 0.0
            act(NL[:, o + 2048:o + 2560], pp[b][:, :], r=["pp%d" % b] + ["P0%d" % b][:b in VFIRST], w=["P1%d" % b], b=["pp%d" % b])
            tol[0] = TOL
        if t == 0:
            for a in range(2):
                double(pc, 256, [(up_, 1024 + 128 * a), (dn_, 1024 + 128 * a)], ["Lk"], ["z0", "z1"], "pc")
                act(T.KO[:, 256 * a:256 * a + 256], pc[:, 256:512], r=["z0", "z1"], w=["KO%d" % a], b=["pc"])
        if not last:
            mm([(pn[:, 256:512], T.ID[:, :], PC[:, 512:768], True, False), (pn[:, 256:512], T.ID[:, :], T.XD[:, 256 * t:256 * t + 256], False, True)],
               r=["ID", "PC1"] + ["XD%d_%d" % (t, b) for b in range(4)], w=["n1"], b=["pm1"])
            op("s", lambda: s.activation(PC[:, 512:768], pn[:, 256:512], F.Identity, scale=1.0 / 256), r=["n1"], w=["PC1"], b=["pm1"],
               ns=256 * CY)
        for b in range(4):
            c = 64 * b
            x1, ep, bn = pa[:, 256 + c:320 + c], ps[:, 256 + c:320 + c], "pm0"
            if t == 0:
                act(T.E[:, c:c + 64], ep, r=["EP%d" % b], w=["E%d" % b], b=["ps"])
            if SY:
                op("s", lambda x1=x1: s.activation(x1, x1, F.Identity, bias=1.0, scale=-2.0), r=["x%d" % b], w=["x%d" % b], b=[bn])
            else:
                ts(x1, x1, -2.0, 1.0, A.mult, A.add, r=["x%d" % b], w=["x%d" % b], b=[bn])
            tt(T.D[:, c:c + 64], T.D[:, c:c + 64], x1, A.mult, r=["x%d" % b, "D%d" % b], w=["D%d" % b], b=[bn])
            if not last:
                tt(ep, T.E[:, c:c + 64], x1, A.mult, r=["x%d" % b, "E%d" % b], w=["EP%d" % b], b=[bn, "ps"])
                factors(b)
                if t < R - 2:
                    act(T.E[:, c:c + 64], ep, r=["EP%d" % b], w=["E%d" % b], b=["ps"], up=5e4)
                before(b, t + 1)
                z = pc[:, 256 + 128 * (b % 2):384 + 128 * (b % 2)]
                content(XO, W, T.By, b, "XN%d", ["By"], z, ["z%d" % (b % 2)], "pc", True)
                sides(T.ZK[:, 128 * b:128 * b + 128], T.KO, z, A.mult, b, r=["z%d" % (b % 2), "KO0", "KO1"], w=["ZK%d" % b], b=["pc"])
        if last:
            mm([(pc[:, 256:384], T.UN[:, 128 * u:128 * u + 128], T.D[:, u:256:2], u == 0, u == 1) for u in range(2)],
               r=["UN0", "UN1"] + ["D%d" % b for b in range(4)], w=["z0"], b=["pc"])
            tt(T.t0[:, 0:128], T.nxi[:, 128:256], T.nxi[:, 0:128], A.add, 2, r=["nxi"], w=["al"])
            ts(T.t0[:, 128:256], T.t0[:, 0:128], 0.5, None, A.mult, r=["al"], w=["be"])
            tt(T.YN[:, 0:128], T.t0[:, 128:256], pc[:, 256:384], A.subtract, r=["be", "z0"], w=["YNa"], b=["pc"])
            tt(T.YN[:, 128:256], T.t0[:, 128:256], pc[:, 256:384], A.add, r=["be", "z0"], w=["YNb"], b=["pc"])
            dma(T.yn[:, :], T.YN[:, :], r=["YNa", "YNb"], size=4)
        mm([(ps[:, 0:16], T.ZR[:, :], T.FM[:, 0:16], True, True)], r=["ZR"] + FK, w=MK[2], b=["ps"])

        tol[0] = TWALK
        for k in range(16):
            for u, (a, b) in enumerate(((0, 8), (8, 16)) if 0 < k <= HALVES else ((0, 16),)):
                nm = [("SC%d", "Q%d"), ("SD%d", "QB%d")]
                nm = nm[u:u + 1] if 0 < k <= HALVES else nm
                gk = ["GW%d" % x for x in range(a // 8, b // 8)]
                src = T.GW[:, 16 * a:16 * b]
                if k == 0:
                    src, gk = NL[:, 0:256], ["P00"]
                else:
                    gather("s", src, NL[:, :].indirect(T.Q[:, 16 * k - 16 + a:16 * k - 16 + b]), r=PK + [x[1] % k for x in nm], w=gk)
                o = 256 * k
                rank_[0] = UPX[3] if k == 0 else 0.0
                op("v", lambda o=o, a=a, b=b, src=src: v.tensor_tensor_scan(T.SC[:, o + 16 * a:o + 16 * b], T.M[:, 16 * a:16 * b],
                                                                             src, 0.0, A.add, A.min),
                   r=["M"] + gk, w=[x[0] % k for x in nm], ns=16 * (b - a) * CY)
                ts(T.Q[:, 16 * k + a:16 * k + b], T.SC[:, o + 16 * a + 15:o + 16 * b:16], adj, None, A.add,
                   r=[x[0] % k for x in nm] + ["adj"], w=[x[1] % (k + 1) for x in nm])
        tol[0] = TFEET
        gather("s", G[:, 512:768], X[:, 0:W].indirect(T.Q[:, 0:16]), r=XK + ["Q1"], w=["Gp1"])
        for e, a, b in (("v", 1, VCOL), ("s", VCOL, 15)):
            stream(e, "col%s%d" % (e, t), lambda a, b, e=e: move(e, G[:, 512 + 16 * a:512 + 16 * b], XO[:, 0:XW].indirect(T.Q[:, a:b])),
                   16 * a, 16 * b, 16, GA, lambda c: ["XO"] + XN + ["Q%d" % (c // 16 + 1), "QB%d" % (c // 16 + 1)],
                   lambda c: ["Gp%d" % (c // 16 + 1)])
        coff = 0
        for p, (k0, k1) in enumerate(PARTS):
            a, b = 16 * (k0 - 1), 16 * k1
            wd, nk = b - a, k1 - k0 + 1
            tol[0] = TLAST if p == NP - 1 else TFEET
            rank_[0] = UPF if p < NUP else 0.0
            raw = T.SC[:, 256 * k0 + 15:256 * (k1 + 1):16]
            sk = [x % k for k in range(k0, k1 + 1) for x in ("SC%d", "SD%d")]
            qa, qk = pc[:, 128:128 + wd], ["s1"]
            mm([(pa[:, a:b], T.Bp[:, 15 - i:143 - i], G[:, 256 * (k0 + 1) + i:256 * (k1 + 2):16], i == 0, i == 15)
                for i in range(16)], r=["Bp"] + ["Gp%d" % j for j in range(k0, k1 + 1)], w=["pc%d" % p, "m0"], b=["pm0"])
            if SQA == 2:
                op("s", lambda raw=raw, a=a, b=b: s.activation(T.RI[:, a:b], raw, F.Identity, bias=MAGIC), r=sk, w=["RI%d" % p], ns=cyc(qa))
                act(T.DE[:, a:b], pa[:, a:b], r=["pc%d" % p], w=["DE%d" % p], b=["pm0"])
                mm([(qa, T.IDf[:, :], T.MC[:, 0:wd], True, False)], 4, r=["IDf", "MC"], w=qk, b=["pc"])
                mm([(qa, T.IDn[:, :], T.RI[:, a:b], False, False), (qa, T.IDf[:, :], raw, False, True)], 4,
                   r=["IDn", "RI%d" % p] + sk, w=qk, b=["pc"])
                tt(T.VC[:, a:b], T.DE[:, a:b], qa, A.mult, r=["DE%d" % p] + qk, w=["VC%d" % p], b=["pc"])
            elif SQA:
                op("s", lambda raw=raw, a=a, b=b: s.activation(T.RI[:, a:b], raw, F.Identity, bias=MAGIC), r=sk, w=["RI%d" % p], ns=cyc(qa))
                op("s", lambda qa=qa, a=a, b=b: s.activation(qa, T.RI[:, a:b], F.Identity, bias=-MAGIC), r=["RI%d" % p], w=qk, b=["pc"],
                   ns=cyc(qa))
            else:
                ts(qa, T.Q[:, a + 16:b + 16], nadj, None, A.add,
                   r=[x % (j + 1) for j in range(k0, k1 + 1) for x in ("Q%d", "QB%d")] + ["nadj"], w=qk, b=["pc"])
            if SQA != 2:
                tt(T.DE[:, a:b], raw, qa, A.subtract, r=sk + qk, w=["DE%d" % p], b=["pc"])
                tt(T.VC[:, a:b], T.DE[:, a:b], pa[:, a:b], A.mult, r=["DE%d" % p, "pc%d" % p], w=["VC%d" % p], b=["pm0"])
            if TPE[p]:
                k2 = max(k0, nk + 1)
                base = [(ps[:, 16 * k2:16 + b], T.IDf[:, :], T.U[:, 16 * (k2 - nk - 1):b - 16 * nk], k2 == k0, False),
                        (ps[:, 16 * k2:16 + b], T.IDf[:, :], T.LK[:, 0:16 * (k1 + 1 - k2)], False, k2 > k0)] if k2 <= k1 else []
                rb = ["IDf", "LK"] + ["U%d" % q for q in range(p)]
                if k2 == k0:
                    mm(base, 4, r=rb, w=["T%d" % j for j in range(k0, k1 + 1)], b=["ps"])
                    base = []
                lst = []
                for d in range(nk):
                    k3 = max(k0, d + 1)
                    lst.append((ps[:, 16 * k3:16 + b], T.IDf[:, :], T.VC[:, 16 * (k3 - d - 1):b - 16 * d], d == 0 and k2 > k0,
                                d == nk - 1 and not base))
                mm(lst + base, 4, r=rb + ["VC%d" % q for q in range(p + 1)], w=["T%d" % j for j in range(k0, k1 + 1)], b=["ps"])
            else:
                for j in range(k0, k1 + 1):
                    tt(ps[:, 16 * j:16 + 16 * j], ps[:, 16 * j - 16:16 * j], T.VC[:, 16 * j - 16:16 * j], A.add,
                       r=["T%d" % (j - 1), "VC%d" % p], w=["T%d" % j], b=["ps"])
            tk = ["T%d" % j for j in range(k1 + 1)]
            tt(T.U[:, a:b], ps[:, 16 + a:16 + b], T.LK[:, 0:wd], A.subtract, r=tk + ["LK"], w=["U%d" % p], b=["ps"])
            ds = list(range(1, k1 + 1))
            for x in range(0, k1, CG):
                grp = []
                for d in ds[x:x + CG]:
                    k2 = max(k0, d)
                    grp.append((d, k2, 16 * (k1 + 1 - k2), coff))
                    coff += 16 * (k1 + 1 - k2)
                key = "CM%d_%d" % (p, x)
                op("v", [(lambda d=d, k2=k2, w_=w_, o=o, b=b: v.tensor_tensor(
                    T.CM[:, o:o + w_], T.U[:, 16 * (k2 - 1):b], ps[:, 16 * (k2 - d):16 * (k2 - d) + w_], A.is_ge))
                    for d, k2, w_, o in grp], r=tk + ["U%d" % p], w=[key], b=["ps"], ns=sum(max(64, y[2]) * CY for y in grp))
                mm([(pn[:, a:b], T.ID[:, :], T.OKK[:, 0:wd], True, False)][:x == 0]
                   + [(pn[:, 16 * (k2 - 1):b], T.ID[:, :], T.CM[:, o:o + w_], False, d == k1) for d, k2, w_, o in grp],
                   r=[key, "ID", "OKK"], w=["pn%d" % p, "m1"], b=["pm1"])
            cp(T.FI[:, a:b], pn[:, a:b], r=["pn%d" % p], w=["FI%d" % p], b=["pm1"])
            rank_[0] = UPF if p < NUPF else 0.0
            stream("s", "fetch%d_%d" % (t, p),
                   lambda a, b, k1=k1: move("s", T.NEW[:, 16 * a:16 * b], G[:, 0:256 * (k1 + 1)].indirect(T.FI[:, a:b])),
                   a, b, 4, GA, lambda c: ["G0", "G1", "FI%d" % p] + ["Gp%d" % k for k in range(1, k1)], lambda c: ["NEW%d" % c])
        tol[0], rank_[0] = TOL, 0.0
        if not last:
            for b in range(4):
                begin(b, t + 1)
        stream("v", "store%d" % t, lambda a, b: v.tensor_copy(X[:, :].indirect(T.Q[:, a:b]), T.NEW[:, 16 * a:16 * b]),
               0, 240, 4, SCA, lambda c: ["NEW%d" % c, "Q%d" % (c // 16 + 1), "QB%d" % (c // 16 + 1)], lambda c: XK)

    for j, e in enumerate(YQ):
        a, b = 256 + V // len(YQ) * j, 256 + V // len(YQ) * (j + 1)
        dma(T.y[:, a:b], X[:, a:b], r=XK, e=e)

    cnt = {e: 0 for e in "vstg"}
    waited = {e: {} for e in Q}
    tok, total, nd = {}, {}, 0

    def wait(e, k):
        if waited[e].get(k[0], 0) < k[1]:
            Q[e].wait_ge(T.sem[k[0]], k[1])
            waited[e][k[0]] = k[1]

    if not ORDER:
        ORDER.extend(order(ops))
    for grp, pre in ORDER:
        o = ops[grp[0]]
        e = o["e"]
        if o["kind"] == "a":
            k = o["sem"]
        else:
            need = {}
            for p, hard in pre.items():
                if hard:
                    need[tok[p][0]] = max(need.get(tok[p][0], 0), tok[p][1])
            for x in need:
                wait(e, (x, need[x]))
            if o["kind"] == "r":
                o["fn"]()
                k = o["sem"]
            elif o["kind"] == "d":
                k = ("d%d" % nd, 16)
                nd += 1
                o["fn"]().then_inc(T.sem[k[0]], 16)
            else:
                if o["range"]:
                    ins = o["fn"](o["range"][0], ops[grp[-1]]["range"][1])
                else:
                    for f in o["fn"]:
                        ins = f()
                cnt[e] += 1
                k = ("c" + e, cnt[e])
                ins.then_inc(T.sem[k[0]], 1)
        total[k[0]] = k[1]
        for j in grp:
            tok[j] = k
    for k in total:
        wait("g", (k, total[k]))
